import numpy as np
import ml_dtypes


def mxq(x, axis, fmt="e4m3"):
    dtype, down = {"e4m3": (ml_dtypes.float8_e4m3fn, 7), "e5m2": (ml_dtypes.float8_e5m2, 14)}[fmt]
    v = np.moveaxis(np.asarray(x, np.float32).astype(ml_dtypes.bfloat16).astype(np.float64), axis, -1)
    blocks = v.reshape(v.shape[:-1] + (-1, 32))
    amax = np.abs(blocks).max(-1, keepdims=True)
    byte = np.maximum(np.where(amax > 0, np.frexp(amax)[1] - 1 + 127, 0) - down, 1)
    scale = np.exp2(byte - 127.0)
    codes = (blocks / scale).astype(np.float32).astype(dtype).astype(np.float64)
    return np.moveaxis((codes * scale).reshape(v.shape), -1, axis)


WIDE = False


def mx_kscale(k):
    if not WIDE:
        return np.ones(k)
    levels = np.array([10, -10, 5, -5, 0])
    if k % 512:
        return np.exp2(np.random.permutation(np.resize(levels, k // 32))).repeat(32)
    a = np.empty((k // 512, 16))
    for p in range(k // 512):
        a[p, :8] = np.random.permutation(np.resize(levels, 8))
        for g in range(8):
            far = levels[np.abs(levels - a[p, g]) >= 10]
            a[p, g + 8] = far[np.random.randint(len(far))]
    return np.exp2(a.ravel()).repeat(32)


def f64(x):
    return np.asarray(x).astype(np.float64)


def striped(idx):
    return np.tile(idx.reshape(-1, 16).T, (8, 1)).astype(np.uint16)


def unstriped(offs):
    return offs[:16].T.reshape(-1).astype(np.int64)


def pack_weight(w):
    k, n = w.shape
    w = f64(np.asarray(w, np.float32).astype(ml_dtypes.bfloat16)).reshape(k // 32, 32, n)
    amax = np.abs(w).max(1)
    byte = np.clip(np.where(amax > 0, np.frexp(amax)[1] - 1 + 127 - 7, 1), 1, 254)
    scaled = (w * np.exp2(127.0 - byte)[:, None, :]).reshape(k, n).astype(np.float32)
    words = np.ascontiguousarray(scaled.reshape(k // 512, 128, 4, n).transpose(0, 1, 3, 2)).astype(ml_dtypes.float8_e4m3fn).view(np.uint8)
    return words, np.ascontiguousarray(byte.astype(np.uint8).reshape(k // 512, 16, n))


def unpack_weight(words, scales):
    g, p, n, _ = words.shape
    vals = np.ascontiguousarray(words).view(ml_dtypes.float8_e4m3fn).astype(np.float64) * np.repeat(np.exp2(scales.astype(np.float64) - 127.0), 8, axis=1)[..., None]
    return vals.transpose(0, 1, 3, 2).reshape(g * 512, n)


E2M1 = np.array([0.0, 0.5, 1.0, 1.5, 2.0, 3.0, 4.0, 6.0, -0.0, -0.5, -1.0, -1.5, -2.0, -3.0, -4.0, -6.0])


def pack_fp4(w):
    k, n = w.shape
    w = f64(np.asarray(w, np.float32).astype(ml_dtypes.bfloat16)).reshape(k // 32, 32, n)
    amax = np.abs(w).max(1)
    mant, ex = np.frexp(amax / 6.0)
    byte = np.clip(np.where(amax > 0, np.where(mant > 0.5, ex, ex - 1) + 127, 1), 1, 254)
    scaled = (w * np.exp2(127.0 - byte)[:, None, :]).reshape(k, n).astype(np.float32)
    c = np.ascontiguousarray(scaled.reshape(k // 512, 128, 4, n).transpose(0, 1, 3, 2)).astype(ml_dtypes.float4_e2m1fn).view(np.uint8) & 0xF
    words = (c[..., 0::2] | (c[..., 1::2] << 4)).reshape(k // 512, 128, 2 * n)
    return np.ascontiguousarray(words), np.ascontiguousarray(byte.astype(np.uint8).reshape(k // 512, 16, n))


def unpack_fp4(words, scales):
    g, _, n = scales.shape
    words = np.ascontiguousarray(words).reshape(g, 128, n, 2)
    nib = np.empty((g, 128, n, 4), np.uint8)
    nib[..., 0::2] = words & 0xF
    nib[..., 1::2] = words >> 4
    vals = E2M1[nib] * np.repeat(np.exp2(scales.astype(np.float64) - 127.0), 8, axis=1)[..., None]
    return vals.transpose(0, 1, 3, 2).reshape(g * 512, n)


def silu(v):
    return v / (1.0 + np.exp(-np.maximum(v, -700.0)))


K, T, S, V, H, N, J, U = 1024, 2048, 1024, 512, 512, 128, 512, 1024


def setup_inputs():
    n = np.random.standard_normal
    s = mx_kscale(K)[:, None]
    u = mx_kscale(H)
    r = mx_kscale(J)[:, None]
    packed_xT = pack_weight(n((K, T)) * s)
    packed_w2 = pack_fp4(n((H, N)) / np.sqrt(2 * H) / u[:, None])
    return {
        "x_words": packed_xT[0],
        "x_scales": packed_xT[1],
        "aT": (n((J, U)) * r).astype(np.float32),
        "w1": (n((K, H)) / np.sqrt(K) / s * u).astype(np.float32),
        "w3": (n((J, H)) / np.sqrt(J) / r).astype(np.float32),
        "w2_words": packed_w2[0],
        "w2_scales": packed_w2[1],
        "offs": striped(np.random.permutation(T)[:S]),
        "pos1": striped(np.random.permutation(S)[:V]),
        "pos2": striped(np.random.permutation(S)[:V]),
    }


def reference(x_words, x_scales, aT, w1, w3, w2_words, w2_scales, offs, pos1, pos2):
    xq = unpack_weight(x_words, x_scales)[:, unstriped(offs)]
    h = silu(mxq(f64(w1), 0, "e4m3").T @ xq)
    f = mxq(f64(w3), 0, "e4m3").T @ mxq(f64(aT), 0, "e4m3")
    z = h[:, unstriped(pos1)] * f[:, :V] + h[:, unstriped(pos2)] * f[:, V:2 * V]
    return unpack_fp4(w2_words, w2_scales).T @ mxq(z, 0, "e4m3")

@@ -1,0 +1,203 @@
+from contextlib import ExitStack
+
+import concourse.mybir as mybir
+
+K, T, S, V, H, N, J, U = 1024, 2048, 1024, 512, 512, 128, 512, 1024
+FLOPS = 2 * (K * H * S + J * H * U + H * N * V)
+
+F32 = mybir.dt.float32
+BF16 = mybir.dt.bfloat16
+I32 = mybir.dt.int32
+U32 = mybir.dt.uint32
+U16 = mybir.dt.uint16
+U8 = mybir.dt.uint8
+FP8X4 = mybir.dt.float8_e4m3fn_x4
+FP4X4 = mybir.dt.float4_e2m1fn_x4
+SILU = mybir.ActivationFunctionType.Silu
+MULT = mybir.AluOpType.mult
+ADD = mybir.AluOpType.add
+
+P = 128
+PACK = 4
+BANK = 512
+PER_COL = 16
+V_BLOCKS = ((0, 256), (256, 384), (384, 512))
+
+
+def tile_picked_dime_none_p_kernel(
+    tc, x_words, x_scales, aT, w1, w3, w2_words, w2_scales, offs, pos1, pos2, out
+):
+    nc = tc.nc
+    with ExitStack() as ctx:
+        keep = ctx.enter_context(tc.tile_pool(name="keep", bufs=1))
+        psum = ctx.enter_context(tc.psum_pool(name="psum", bufs=8))
+
+        def sb(name, shape, dtype):
+            return keep.tile(shape, dtype, name=name, align_bytes=64)
+
+        def bank(name):
+            return psum.tile([P, BANK], F32, name=name, tag="bank")
+
+        offs_t = keep.tile([P, S // PER_COL], U16, name="offs_t")
+        pos_t = [keep.tile([P, V // PER_COL], U16, name="pos%d_t" % d) for d in range(2)]
+        xw = [sb("xw%d" % g, [P, T], U32) for g in range(2)]
+        xs = sb("xs", [P, T], U8)
+        w1_raw = [sb("w1_raw%d" % g, [P, PACK, H], F32) for g in range(2)]
+        w3_raw = sb("w3_raw", [P, PACK, H], F32)
+        a_raw = [sb("a_raw%d" % d, [P, PACK, V], F32) for d in range(2)]
+        w2w = sb("w2w", [P, 2 * N], U8)
+        w2s = sb("w2s", [P, N], U8)
+        warm = sb("warm", [P, 8], F32)
+        warm_out = sb("warm_out", [P, 8], F32)
+
+        nc.vector.memset(warm[:], 0.0)
+        nc.scalar.activation(warm_out[:], warm[:], SILU)
+
+        def load_words(g):
+            nc.sync.dma_start(out=xw[g][:].bitcast(I32), in_=x_words[g].rearrange("p n t -> p (n t)").bitcast(I32))
+
+        def load_rows(raw, rows):
+            nc.sync.dma_start(out=raw[:], in_=rows.rearrange("(p j) c -> p j c", j=PACK))
+
+        nc.sync.dma_start(offs_t[:], offs)
+        load_words(0)
+        load_rows(w1_raw[0], w1[0:512, :])
+        load_rows(w1_raw[1], w1[512:1024, :])
+        load_words(1)
+        nc.sync.dma_start(pos_t[0][:], pos1)
+        nc.sync.dma_start(pos_t[1][:], pos2)
+        load_rows(w3_raw, w3)
+        load_rows(a_raw[0], aT[:, 0:V])
+        load_rows(a_raw[1], aT[:, V : 2 * V])
+
+        nc.gpsimd.memset(xs[:].bitcast(I32), 0)
+        nc.gpsimd.memset(w2s[:].bitcast(I32), 0)
+        for q in range(4):
+            nc.gpsimd.dma_start(out=xs[32 * q : 32 * q + 8, :].bitcast(I32), in_=x_scales[:, 4 * q : 4 * q + 4, :].bitcast(I32))
+        nc.gpsimd.dma_start(out=w2w[:].bitcast(I32), in_=w2_words[0].bitcast(I32))
+        for q in range(4):
+            nc.gpsimd.dma_start(out=w2s[32 * q : 32 * q + 4, :].bitcast(I32), in_=w2_scales[0, 4 * q : 4 * q + 4, :].bitcast(I32))
+
+        gw = [[sb("gw%d_%d" % (g, s), [P, BANK], U32) for s in range(2)] for g in range(2)]
+        gs = sb("gs", [P, S], U8)
+
+        def gather_words(g, s):
+            nc.vector.tensor_copy(gw[g][s][:], xw[g][:].indirect(offs_t[:, 32 * s : 32 * s + 32]))
+
+        def cast_weight(copy, dst, raw, m0, m1):
+            copy(
+                dst[:].rearrange("p (t m j) -> p m j t", t=PACK, j=PACK)[:, m0:m1],
+                raw[:].rearrange("p j (m t) -> p m j t", t=PACK)[:, m0:m1],
+            )
+
+        def cast_angles(copy, dst, raw, c0, c1):
+            copy(
+                dst[:].rearrange("p (c i j) -> p c j i", i=4, j=PACK)[:, c0:c1],
+                raw[:].rearrange("p j (c i) -> p c j i", i=4)[:, c0:c1],
+            )
+
+        def quantize(name, src, cols):
+            codes = sb(name + "_codes", [P, cols], U32)
+            scales = sb(name + "_scales", [P, cols], U8)
+            nc.vector.quantize_mx(out=codes[:].bitcast(FP8X4), scales=scales[:], in_=src)
+            return codes, scales
+
+        w1_bf = [sb("w1_bf%d" % g, [P, PACK * H], BF16) for g in range(2)]
+        w3_bf = sb("w3_bf", [P, PACK * H], BF16)
+        a_bf = [sb("a_bf%d" % d, [P, PACK * V], BF16) for d in range(2)]
+        h = [sb("h%d" % t, [P, S], F32) for t in range(PACK)]
+        h_ps = [[bank("h_ps%d_%d" % (s, t)) for t in range(PACK)] for s in range(2)]
+
+        def h_pass(wq, g, s, t):
+            nc.tensor.matmul_mx(
+                out=h_ps[s][t][:],
+                lhsT=wq[0][:, P * t : P * (t + 1)].bitcast(FP8X4),
+                lhsT_scale=wq[1][:, P * t : P * (t + 1)],
+                rhs=gw[g][s][:].bitcast(FP8X4),
+                rhs_scale=gs[4 * g : P, BANK * s : BANK * (s + 1)],
+                start=(g == 0),
+                stop=(g == 1),
+            )
+
+        gather_words(0, 0)
+        gather_words(0, 1)
+        nc.vector.tensor_copy(gs[:], xs[:].indirect(offs_t[:]))
+        cast_weight(nc.scalar.copy, w1_bf[0], w1_raw[0], 0, P)
+        w1q0 = quantize("w1q0", w1_bf[0][:], H)
+        for s in range(2):
+            for t in range(PACK):
+                h_pass(w1q0, 0, s, t)
+        cast_weight(nc.scalar.copy, w1_bf[1], w1_raw[1], 0, 64)
+        cast_weight(nc.vector.tensor_copy, w1_bf[1], w1_raw[1], 64, P)
+        w1q1 = quantize("w1q1", w1_bf[1][:], H)
+        for s in range(2):
+            gather_words(1, s)
+            for t in range(PACK):
+                h_pass(w1q1, 1, s, t)
+                nc.scalar.activation(h[t][:, BANK * s : BANK * (s + 1)], h_ps[s][t][:], SILU)
+
+        cast_weight(nc.vector.tensor_copy, w3_bf, w3_raw, 0, P)
+        w3q = quantize("w3q", w3_bf[:], H)
+
+        prod = [sb("prod%d" % d, [P, PACK, V], F32) for d in range(2)]
+
+        def filters(d, aq):
+            f_sb = []
+            for t in range(PACK):
+                f_ps = bank("f_ps%d_%d" % (d, t))
+                nc.tensor.matmul_mx(
+                    out=f_ps[:],
+                    lhsT=w3q[0][:, P * t : P * (t + 1)].bitcast(FP8X4),
+                    lhsT_scale=w3q[1][:, P * t : P * (t + 1)],
+                    rhs=aq[0][:].bitcast(FP8X4),
+                    rhs_scale=aq[1][:],
+                    start=True,
+                    stop=True,
+                )
+                f_t = sb("f%d_%d" % (d, t), [P, V], F32)
+                nc.scalar.copy(f_t[:], f_ps[:])
+                f_sb.append(f_t)
+            return f_sb
+
+        def gather_product(d, f_sb, t, v0, v1):
+            nc.vector.tensor_tensor(
+                prod[d][:, t, v0:v1],
+                h[t][:].indirect(pos_t[d][:, v0 // PER_COL : v1 // PER_COL]),
+                f_sb[t][:, v0:v1],
+                MULT,
+            )
+
+        cast_angles(nc.vector.tensor_copy, a_bf[0], a_raw[0], 0, V // 4)
+        aq0 = quantize("aq0", a_bf[0][:], V)
+        f0 = filters(0, aq0)
+        cast_angles(nc.scalar.copy, a_bf[1], a_raw[1], 0, V // 4)
+        for t in range(3):
+            gather_product(0, f0, t, 0, V)
+        aq1 = quantize("aq1", a_bf[1][:], V)
+        gather_product(0, f0, 3, 0, V)
+        f1 = filters(1, aq1)
+
+        for b, (v0, v1) in enumerate(V_BLOCKS):
+            for t in range(PACK):
+                gather_product(1, f1, t, v0, v1)
+            z_bf = sb("z_bf%d" % b, [P, PACK * (v1 - v0)], BF16)
+            nc.vector.tensor_tensor(
+                z_bf[:].rearrange("p (c i t) -> p c t i", i=4, t=PACK),
+                prod[0][:, :, v0:v1].rearrange("p t (c i) -> p c t i", i=4),
+                prod[1][:, :, v0:v1].rearrange("p t (c i) -> p c t i", i=4),
+                ADD,
+            )
+            zq = quantize("zq%d" % b, z_bf[:], v1 - v0)
+            o_ps = bank("o_ps%d" % b)
+            nc.tensor.matmul_mx(
+                out=o_ps[:, 0 : v1 - v0],
+                lhsT=w2w[:].bitcast(FP4X4),
+                lhsT_scale=w2s[:],
+                rhs=zq[0][:].bitcast(FP8X4),
+                rhs_scale=zq[1][:],
+                start=True,
+                stop=True,
+            )
+            o_sb = sb("o_sb%d" % b, [P, v1 - v0], F32)
+            nc.scalar.copy(o_sb[:], o_ps[:, 0 : v1 - v0])
+            nc.sync.dma_start(out=out[:, v0:v1], in_=o_sb[:])

@@ -32,8 +32,8 @@ def tile_picked_dime_none_p_kernel(
         keep = ctx.enter_context(tc.tile_pool(name="keep", bufs=1))
         psum = ctx.enter_context(tc.psum_pool(name="psum", bufs=8))
 
-        def sb(name, shape, dtype):
-            return keep.tile(shape, dtype, name=name, align_bytes=64)
+        def sb(name, shape, dtype, tag=""):
+            return keep.tile(shape, dtype, name=name, tag=tag or name, align_bytes=64)
 
         def bank(name):
             return psum.tile([P, BANK], F32, name=name, tag="bank")
@@ -50,7 +50,9 @@ def tile_picked_dime_none_p_kernel(
         warm = sb("warm", [P, 8], F32)
         warm_out = sb("warm_out", [P, 8], F32)
 
-        nc.vector.memset(warm[:], 0.0)
+        nc.vector.memset(xs[:].bitcast(I32), 0)
+        nc.gpsimd.memset(warm[:], 0.0)
+        nc.gpsimd.memset(w2s[:].bitcast(I32), 0)
         nc.scalar.activation(warm_out[:], warm[:], SILU)
 
         def load_words(g):
@@ -61,6 +63,8 @@ def tile_picked_dime_none_p_kernel(
 
         nc.sync.dma_start(offs_t[:], offs)
         load_words(0)
+        for q in range(4):
+            nc.sync.dma_start(out=xs[32 * q : 32 * q + 8, :].bitcast(I32), in_=x_scales[:, 4 * q : 4 * q + 4, :].bitcast(I32))
         load_rows(w1_raw[0], w1[0:512, :])
         load_rows(w1_raw[1], w1[512:1024, :])
         load_words(1)
@@ -70,41 +74,45 @@ def tile_picked_dime_none_p_kernel(
         load_rows(a_raw[0], aT[:, 0:V])
         load_rows(a_raw[1], aT[:, V : 2 * V])
 
-        nc.gpsimd.memset(xs[:].bitcast(I32), 0)
-        nc.gpsimd.memset(w2s[:].bitcast(I32), 0)
+        nc.sync.dma_start(out=w2w[:].bitcast(I32), in_=w2_words[0].bitcast(I32))
         for q in range(4):
-            nc.gpsimd.dma_start(out=xs[32 * q : 32 * q + 8, :].bitcast(I32), in_=x_scales[:, 4 * q : 4 * q + 4, :].bitcast(I32))
-        nc.gpsimd.dma_start(out=w2w[:].bitcast(I32), in_=w2_words[0].bitcast(I32))
-        for q in range(4):
-            nc.gpsimd.dma_start(out=w2s[32 * q : 32 * q + 4, :].bitcast(I32), in_=w2_scales[0, 4 * q : 4 * q + 4, :].bitcast(I32))
+            nc.sync.dma_start(out=w2s[32 * q : 32 * q + 4, :].bitcast(I32), in_=w2_scales[0, 4 * q : 4 * q + 4, :].bitcast(I32))
 
-        gw = [[sb("gw%d_%d" % (g, s), [P, BANK], U32) for s in range(2)] for g in range(2)]
-        gs = sb("gs", [P, S], U8)
+        gw = [[None, None], [None, None]]
+        gs = [None, None]
 
-        def gather_words(g, s):
+        def gather_scales(s, tag=""):
+            gs[s] = sb("gs%d" % s, [P, BANK], U8, tag)
+            nc.vector.tensor_copy(gs[s][:], xs[:].indirect(offs_t[:, 32 * s : 32 * s + 32]))
+
+        def gather_words(g, s, tag=""):
+            gw[g][s] = sb("gw%d_%d" % (g, s), [P, BANK], U32, tag)
             nc.vector.tensor_copy(gw[g][s][:], xw[g][:].indirect(offs_t[:, 32 * s : 32 * s + 32]))
 
-        def cast_weight(copy, dst, raw, m0, m1):
+        def cast_weight(copy, dst, raw, u):
             copy(
-                dst[:].rearrange("p (t m j) -> p m j t", t=PACK, j=PACK)[:, m0:m1],
-                raw[:].rearrange("p j (m t) -> p m j t", t=PACK)[:, m0:m1],
+                dst.rearrange("p (t m j) -> p m j t", t=2, j=PACK),
+                raw[:].rearrange("p j (m t) -> p m j t", t=PACK)[:, :, :, 2 * u : 2 * u + 2],
             )
 
-        def cast_angles(copy, dst, raw, c0, c1):
+        def cast_angles(copy, dst, raw):
             copy(
-                dst[:].rearrange("p (c i j) -> p c j i", i=4, j=PACK)[:, c0:c1],
-                raw[:].rearrange("p j (c i) -> p c j i", i=4)[:, c0:c1],
+                dst.rearrange("p (c i j) -> p c j i", i=2, j=PACK),
+                raw.rearrange("p j (c i) -> p c j i", i=2),
             )
+
+        def planes(name, cols, tag=""):
+            return sb(name + "_codes", [P, cols], U32, tag), sb(name + "_scales", [P, cols], U8)
+
+        def quantize_into(q, c0, c1, src):
+            nc.vector.quantize_mx(out=q[0][:, c0:c1].bitcast(FP8X4), scales=q[1][:, c0:c1], in_=src)
 
         def quantize(name, src, cols):
-            codes = sb(name + "_codes", [P, cols], U32)
-            scales = sb(name + "_scales", [P, cols], U8)
-            nc.vector.quantize_mx(out=codes[:].bitcast(FP8X4), scales=scales[:], in_=src)
-            return codes, scales
+            q = planes(name, cols)
+            quantize_into(q, 0, cols, src)
+            return q
 
-        w1_bf = [sb("w1_bf%d" % g, [P, PACK * H], BF16) for g in range(2)]
-        w3_bf = sb("w3_bf", [P, PACK * H], BF16)
-        a_bf = [sb("a_bf%d" % d, [P, PACK * V], BF16) for d in range(2)]
+        HALF = 2 * H
         h = [sb("h%d" % t, [P, S], F32) for t in range(PACK)]
         h_ps = [[bank("h_ps%d_%d" % (s, t)) for t in range(PACK)] for s in range(2)]
 
@@ -114,35 +122,45 @@ def tile_picked_dime_none_p_kernel(
                 lhsT=wq[0][:, P * t : P * (t + 1)].bitcast(FP8X4),
                 lhsT_scale=wq[1][:, P * t : P * (t + 1)],
                 rhs=gw[g][s][:].bitcast(FP8X4),
-                rhs_scale=gs[4 * g : P, BANK * s : BANK * (s + 1)],
+                rhs_scale=gs[s][4 * g : P, :],
                 start=(g == 0),
                 stop=(g == 1),
             )
 
         gather_words(0, 0)
         gather_words(0, 1)
-        nc.vector.tensor_copy(gs[:], xs[:].indirect(offs_t[:]))
-        cast_weight(nc.scalar.copy, w1_bf[0], w1_raw[0], 0, P)
-        w1q0 = quantize("w1q0", w1_bf[0][:], H)
+        gather_scales(0)
+        w1a_bf = [sb("w1a_bf%d" % u, [P, HALF], BF16) for u in range(2)]
+        for u in range(2):
+            cast_weight(nc.scalar.copy, w1a_bf[u][:], w1_raw[0], u)
+        w1q0 = planes("w1q0", H)
+        quantize_into(w1q0, 0, H // 2, w1a_bf[0][:])
+        gather_scales(1, "w1a_bf0")
+        quantize_into(w1q0, H // 2, H, w1a_bf[1][:])
         for s in range(2):
             for t in range(PACK):
                 h_pass(w1q0, 0, s, t)
-        cast_weight(nc.scalar.copy, w1_bf[1], w1_raw[1], 0, 64)
-        cast_weight(nc.vector.tensor_copy, w1_bf[1], w1_raw[1], 64, P)
-        w1q1 = quantize("w1q1", w1_bf[1][:], H)
+        w1b_bf = [sb("w1b_bf0", [P, HALF], BF16), sb("w1b_bf1", [P, HALF], BF16, "w1a_bf1")]
+        cast_weight(nc.scalar.copy, w1b_bf[0][:], w1_raw[1], 0)
+        cast_weight(nc.vector.tensor_copy, w1b_bf[1][:], w1_raw[1], 1)
+        w1q1 = planes("w1q1", H, "w1_raw1")
+        quantize_into(w1q1, 0, H // 2, w1b_bf[0][:])
+        quantize_into(w1q1, H // 2, H, w1b_bf[1][:])
         for s in range(2):
-            gather_words(1, s)
+            gather_words(1, s, "w1a_bf1" if s else "w1b_bf0")
             for t in range(PACK):
                 h_pass(w1q1, 1, s, t)
                 nc.scalar.activation(h[t][:, BANK * s : BANK * (s + 1)], h_ps[s][t][:], SILU)
 
-        cast_weight(nc.vector.tensor_copy, w3_bf, w3_raw, 0, P)
+        w3_bf = sb("w3_bf", [P, 2 * HALF], BF16, "xw1")
+        for u in range(2):
+            cast_weight(nc.vector.tensor_copy, w3_bf[:, HALF * u : HALF * (u + 1)], w3_raw, u)
         w3q = quantize("w3q", w3_bf[:], H)
 
         prod = [sb("prod%d" % d, [P, PACK, V], F32) for d in range(2)]
 
-        def filters(d, aq):
-            f_sb = []
+        def filter_products(d, aq):
+            banks = []
             for t in range(PACK):
                 f_ps = bank("f_ps%d_%d" % (d, t))
                 nc.tensor.matmul_mx(
@@ -154,37 +172,54 @@ def tile_picked_dime_none_p_kernel(
                     start=True,
                     stop=True,
                 )
-                f_t = sb("f%d_%d" % (d, t), [P, V], F32)
-                nc.scalar.copy(f_t[:], f_ps[:])
-                f_sb.append(f_t)
-            return f_sb
+                banks.append(f_ps)
+            return banks
+
+        def filter_copy(name, f_ps, tag=""):
+            f_t = sb(name, [P, V], F32, tag)
+            nc.scalar.copy(f_t[:], f_ps[:])
+            return f_t
 
         def gather_product(d, f_sb, t, v0, v1):
             nc.vector.tensor_tensor(
                 prod[d][:, t, v0:v1],
                 h[t][:].indirect(pos_t[d][:, v0 // PER_COL : v1 // PER_COL]),
-                f_sb[t][:, v0:v1],
+                f_sb[:, v0:v1],
                 MULT,
             )
 
-        cast_angles(nc.vector.tensor_copy, a_bf[0], a_raw[0], 0, V // 4)
-        aq0 = quantize("aq0", a_bf[0][:], V)
-        f0 = filters(0, aq0)
-        cast_angles(nc.scalar.copy, a_bf[1], a_raw[1], 0, V // 4)
-        for t in range(3):
-            gather_product(0, f0, t, 0, V)
-        aq1 = quantize("aq1", a_bf[1][:], V)
-        gather_product(0, f0, 3, 0, V)
-        f1 = filters(1, aq1)
+        def gather_plain(t, tag=""):
+            g_t = sb("g%d" % t, [P, V], F32, tag)
+            nc.vector.tensor_copy(g_t[:], h[t][:].indirect(pos_t[0][:]))
+            return g_t
+
+        a0_bf = [sb("a0_bf0", [P, HALF], BF16, "w3_raw"), sb("a0_bf1", [P, HALF], BF16, "xw1")]
+        aq0 = planes("aq0", V)
+        for c in range(2):
+            cast_angles(nc.vector.tensor_copy, a0_bf[c][:], a_raw[0][:, :, V // 2 * c : V // 2 * (c + 1)])
+        for c in range(2):
+            quantize_into(aq0, V // 2 * c, V // 2 * (c + 1), a0_bf[c][:])
+        picked = [gather_plain(0, "w3_raw"), gather_plain(1, "xw1")]
+        f0_ps = filter_products(0, aq0)
+        for t in range(2):
+            nc.vector.tensor_tensor(prod[0][:, t, :], picked[t][:], f0_ps[t][:], MULT)
+        a_bf1 = sb("a_bf1", [P, PACK * V], BF16)
+        cast_angles(nc.scalar.copy, a_bf1[:], a_raw[1][:])
+        aq1 = quantize("aq1", a_bf1[:], V)
+        for t in range(2, PACK):
+            gather_product(0, filter_copy("f0_%d" % t, f0_ps[t]), t, 0, V)
+        f1_ps = filter_products(1, aq1)
+        f1 = []
+        for t in range(PACK):
+            f1.append(filter_copy("f1_%d" % t, f1_ps[t]))
+            gather_product(1, f1[t], t, 0, V)
 
         for b, (v0, v1) in enumerate(V_BLOCKS):
-            for t in range(PACK):
-                gather_product(1, f1, t, v0, v1)
             z_bf = sb("z_bf%d" % b, [P, PACK * (v1 - v0)], BF16)
             nc.vector.tensor_tensor(
-                z_bf[:].rearrange("p (c i t) -> p c t i", i=4, t=PACK),
-                prod[0][:, :, v0:v1].rearrange("p t (c i) -> p c t i", i=4),
-                prod[1][:, :, v0:v1].rearrange("p t (c i) -> p c t i", i=4),
+                z_bf[:].rearrange("p (c i t) -> p c t i", i=2, t=PACK),
+                prod[0][:, :, v0:v1].rearrange("p t (c i) -> p c t i", i=2),
+                prod[1][:, :, v0:v1].rearrange("p t (c i) -> p c t i", i=2),
                 ADD,
             )
             zq = quantize("zq%d" % b, z_bf[:], v1 - v0)

@@ -21,7 +21,7 @@ P = 128
 PACK = 4
 BANK = 512
 PER_COL = 16
-V_BLOCKS = ((0, 256), (256, 384), (384, 512))
+HALF_V = V // 2
 
 
 def tile_picked_dime_none_p_kernel(
@@ -30,10 +30,14 @@ def tile_picked_dime_none_p_kernel(
     nc = tc.nc
     with ExitStack() as ctx:
         keep = ctx.enter_context(tc.tile_pool(name="keep", bufs=1))
+        lap = ctx.enter_context(tc.tile_pool(name="lap", bufs=1))
         psum = ctx.enter_context(tc.psum_pool(name="psum", bufs=8))
 
         def sb(name, shape, dtype, tag=""):
             return keep.tile(shape, dtype, name=name, tag=tag or name, align_bytes=64)
+
+        def sb_at(name, shape, dtype, offset):
+            return lap.tile(shape, dtype, name=name, offset=offset, align_bytes=64)
 
         def bank(name):
             return psum.tile([P, BANK], F32, name=name, tag="bank")
@@ -44,7 +48,10 @@ def tile_picked_dime_none_p_kernel(
         xs = sb("xs", [P, T], U8)
         w1_raw = [sb("w1_raw%d" % g, [P, PACK, H], F32) for g in range(2)]
         w3_raw = sb("w3_raw", [P, PACK, H], F32)
-        a_raw = [sb("a_raw%d" % d, [P, PACK, V], F32) for d in range(2)]
+        a_raw = [
+            [sb("a_raw0_0", [P, PACK, HALF_V], F32), sb_at("a_raw0_1", [P, PACK, HALF_V], F32, 1024)],
+            [sb("a_raw1_%d" % d, [P, PACK, HALF_V], F32) for d in range(2)],
+        ]
         w2w = sb("w2w", [P, 2 * N], U8)
         w2s = sb("w2s", [P, N], U8)
         warm = sb("warm", [P, 8], F32)
@@ -61,169 +68,133 @@ def tile_picked_dime_none_p_kernel(
         def load_rows(raw, rows):
             nc.sync.dma_start(out=raw[:], in_=rows.rearrange("(p j) c -> p j c", j=PACK))
 
+        def load_angles(c, d):
+            load_rows(a_raw[c][d], aT[:, V * d + HALF_V * c : V * d + HALF_V * (c + 1)])
+
         nc.sync.dma_start(offs_t[:], offs)
         load_words(0)
         for q in range(4):
             nc.sync.dma_start(out=xs[32 * q : 32 * q + 8, :].bitcast(I32), in_=x_scales[:, 4 * q : 4 * q + 4, :].bitcast(I32))
         load_rows(w1_raw[0], w1[0:512, :])
-        load_rows(w1_raw[1], w1[512:1024, :])
         load_words(1)
+        load_rows(w1_raw[1], w1[512:1024, :])
+        load_rows(w3_raw, w3)
+        load_angles(0, 0)
         nc.sync.dma_start(pos_t[0][:], pos1)
         nc.sync.dma_start(pos_t[1][:], pos2)
-        load_rows(w3_raw, w3)
-        load_rows(a_raw[0], aT[:, 0:V])
-        load_rows(a_raw[1], aT[:, V : 2 * V])
+        load_angles(0, 1)
+        load_angles(1, 0)
+        load_angles(1, 1)
 
         nc.sync.dma_start(out=w2w[:].bitcast(I32), in_=w2_words[0].bitcast(I32))
         for q in range(4):
             nc.sync.dma_start(out=w2s[32 * q : 32 * q + 4, :].bitcast(I32), in_=w2_scales[0, 4 * q : 4 * q + 4, :].bitcast(I32))
 
-        gw = [[None, None], [None, None]]
-        gs = [None, None]
-
-        def gather_scales(s, tag=""):
-            gs[s] = sb("gs%d" % s, [P, BANK], U8, tag)
-            nc.vector.tensor_copy(gs[s][:], xs[:].indirect(offs_t[:, 32 * s : 32 * s + 32]))
-
-        def gather_words(g, s, tag=""):
-            gw[g][s] = sb("gw%d_%d" % (g, s), [P, BANK], U32, tag)
-            nc.vector.tensor_copy(gw[g][s][:], xw[g][:].indirect(offs_t[:, 32 * s : 32 * s + 32]))
-
-        def cast_weight(copy, dst, raw, u):
+        def cast_weight(copy, dst, raw, u, m0=0, m1=P):
             copy(
-                dst.rearrange("p (t m j) -> p m j t", t=2, j=PACK),
-                raw[:].rearrange("p j (m t) -> p m j t", t=PACK)[:, :, :, 2 * u : 2 * u + 2],
+                dst[:].rearrange("p (t m j) -> p m j t", t=2, j=PACK)[:, m0:m1],
+                raw[:].rearrange("p j (m t) -> p m j t", t=PACK)[:, m0:m1, :, 2 * u : 2 * u + 2],
             )
 
-        def cast_angles(copy, dst, raw):
+        def cast_angles(copy, dst, c, d):
             copy(
                 dst.rearrange("p (c i j) -> p c j i", i=2, j=PACK),
-                raw.rearrange("p j (c i) -> p c j i", i=2),
+                a_raw[c][d][:].rearrange("p j (c i) -> p c j i", i=2),
             )
 
-        def planes(name, cols, tag=""):
-            return sb(name + "_codes", [P, cols], U32, tag), sb(name + "_scales", [P, cols], U8)
+        def quantize(name, src, tag="", offset=None):
+            cols = src.shape[1] // PACK
+            codes = sb(name + "_codes", [P, cols], U32, tag) if offset is None else sb_at(name + "_codes", [P, cols], U32, offset)
+            scales = sb(name + "_scales", [P, cols], U8)
+            nc.vector.quantize_mx(out=codes[:].bitcast(FP8X4), scales=scales[:], in_=src)
+            return codes, scales
 
-        def quantize_into(q, c0, c1, src):
-            nc.vector.quantize_mx(out=q[0][:, c0:c1].bitcast(FP8X4), scales=q[1][:, c0:c1], in_=src)
+        h = [sb("h%d" % t, [P, S], F32) for t in range(PACK - 1)]
+        h_ps = [[bank("h_ps%d_%d" % (t, s)) for s in range(2)] for t in range(PACK)]
+        gw0 = sb("gw0", [P, S], U32)
+        gs = sb("gs", [P, S], U8)
+        gw1 = [sb("gw1_%d" % s, [P, BANK], U32) for s in range(2)]
 
-        def quantize(name, src, cols):
-            q = planes(name, cols)
-            quantize_into(q, 0, cols, src)
-            return q
+        def h_pass(wq, g, u):
+            for i in range(2):
+                for s in range(2):
+                    cols = slice(BANK * s, BANK * (s + 1))
+                    words = gw0[:, cols] if g == 0 else gw1[s][:]
+                    nc.tensor.matmul_mx(
+                        out=h_ps[2 * u + i][s][:],
+                        lhsT=wq[0][:, P * i : P * (i + 1)].bitcast(FP8X4),
+                        lhsT_scale=wq[1][:, P * i : P * (i + 1)],
+                        rhs=words.bitcast(FP8X4),
+                        rhs_scale=gs[4 * g : P, cols],
+                        start=(g == 0),
+                        stop=(g == 1),
+                    )
 
-        HALF = 2 * H
-        h = [sb("h%d" % t, [P, S], F32) for t in range(PACK)]
-        h_ps = [[bank("h_ps%d_%d" % (s, t)) for t in range(PACK)] for s in range(2)]
+        def silu(t):
+            for s in range(2):
+                nc.scalar.activation(h[t][:, BANK * s : BANK * (s + 1)], h_ps[t][s][:], SILU)
 
-        def h_pass(wq, g, s, t):
-            nc.tensor.matmul_mx(
-                out=h_ps[s][t][:],
-                lhsT=wq[0][:, P * t : P * (t + 1)].bitcast(FP8X4),
-                lhsT_scale=wq[1][:, P * t : P * (t + 1)],
-                rhs=gw[g][s][:].bitcast(FP8X4),
-                rhs_scale=gs[s][4 * g : P, :],
-                start=(g == 0),
-                stop=(g == 1),
-            )
-
-        gather_words(0, 0)
-        gather_words(0, 1)
-        gather_scales(0)
-        w1a_bf = [sb("w1a_bf%d" % u, [P, HALF], BF16) for u in range(2)]
+        nc.vector.tensor_copy(gw0[:], xw[0][:].indirect(offs_t[:]))
+        nc.vector.tensor_copy(gs[:], xs[:].indirect(offs_t[:]))
+        w1_bf = [[sb("w1_bf%d_%d" % (g, u), [P, 2 * H], BF16) for u in range(2)] for g in range(2)]
         for u in range(2):
-            cast_weight(nc.scalar.copy, w1a_bf[u][:], w1_raw[0], u)
-        w1q0 = planes("w1q0", H)
-        quantize_into(w1q0, 0, H // 2, w1a_bf[0][:])
-        gather_scales(1, "w1a_bf0")
-        quantize_into(w1q0, H // 2, H, w1a_bf[1][:])
+            cast_weight(nc.scalar.copy, w1_bf[0][u], w1_raw[0], u)
+        h_pass(quantize("w1q00", w1_bf[0][0][:]), 0, 0)
         for s in range(2):
-            for t in range(PACK):
-                h_pass(w1q0, 0, s, t)
-        w1b_bf = [sb("w1b_bf0", [P, HALF], BF16), sb("w1b_bf1", [P, HALF], BF16, "w1a_bf1")]
-        cast_weight(nc.scalar.copy, w1b_bf[0][:], w1_raw[1], 0)
-        cast_weight(nc.vector.tensor_copy, w1b_bf[1][:], w1_raw[1], 1)
-        w1q1 = planes("w1q1", H, "w1_raw1")
-        quantize_into(w1q1, 0, H // 2, w1b_bf[0][:])
-        quantize_into(w1q1, H // 2, H, w1b_bf[1][:])
-        for s in range(2):
-            gather_words(1, s, "w1a_bf1" if s else "w1b_bf0")
-            for t in range(PACK):
-                h_pass(w1q1, 1, s, t)
-                nc.scalar.activation(h[t][:, BANK * s : BANK * (s + 1)], h_ps[s][t][:], SILU)
-
-        w3_bf = sb("w3_bf", [P, 2 * HALF], BF16, "xw1")
+            nc.vector.tensor_copy(gw1[s][:], xw[1][:].indirect(offs_t[:, 32 * s : 32 * s + 32]))
         for u in range(2):
-            cast_weight(nc.vector.tensor_copy, w3_bf[:, HALF * u : HALF * (u + 1)], w3_raw, u)
-        w3q = quantize("w3q", w3_bf[:], H)
+            cast_weight(nc.scalar.copy, w1_bf[1][u], w1_raw[1], u, 0, P // 2)
+            cast_weight(nc.vector.tensor_copy, w1_bf[1][u], w1_raw[1], u, P // 2, P)
+        h_pass(quantize("w1q10", w1_bf[1][0][:]), 1, 0)
+        h_pass(quantize("w1q01", w1_bf[0][1][:], "w1_raw1"), 0, 1)
+        h_pass(quantize("w1q11", w1_bf[1][1][:]), 1, 1)
+        for t in range(PACK - 1):
+            silu(t)
 
-        prod = [sb("prod%d" % d, [P, PACK, V], F32) for d in range(2)]
+        prod = {}
 
-        def filter_products(d, aq):
-            banks = []
-            for t in range(PACK):
-                f_ps = bank("f_ps%d_%d" % (d, t))
+        def new_product(c, d, tag=""):
+            prod[c, d] = sb("prod%d_%d" % (c, d), [P, PACK * HALF_V], F32, tag)
+            return prod[c, d][:, 2 * HALF_V : 4 * HALF_V].bitcast(BF16)
+
+        def filters(c, d, u, aq, offset=None):
+            f_ps = bank("f_ps%d_%d_%d" % (c, d, u))
+            for i in range(2):
                 nc.tensor.matmul_mx(
-                    out=f_ps[:],
-                    lhsT=w3q[0][:, P * t : P * (t + 1)].bitcast(FP8X4),
-                    lhsT_scale=w3q[1][:, P * t : P * (t + 1)],
+                    out=f_ps[:, HALF_V * i : HALF_V * (i + 1)],
+                    lhsT=w3q[u][0][:, P * i : P * (i + 1)].bitcast(FP8X4),
+                    lhsT_scale=w3q[u][1][:, P * i : P * (i + 1)],
                     rhs=aq[0][:].bitcast(FP8X4),
                     rhs_scale=aq[1][:],
                     start=True,
                     stop=True,
                 )
-                banks.append(f_ps)
-            return banks
+            name = "f%d_%d_%d" % (c, d, u)
+            f_sb = sb(name, [P, BANK], F32) if offset is None else sb_at(name, [P, BANK], F32, offset)
+            nc.scalar.copy(f_sb[:], f_ps[:])
+            return f_sb
 
-        def filter_copy(name, f_ps, tag=""):
-            f_t = sb(name, [P, V], F32, tag)
-            nc.scalar.copy(f_t[:], f_ps[:])
-            return f_t
-
-        def gather_product(d, f_sb, t, v0, v1):
+        def gather_product(c, d, t, f_sb):
             nc.vector.tensor_tensor(
-                prod[d][:, t, v0:v1],
-                h[t][:].indirect(pos_t[d][:, v0 // PER_COL : v1 // PER_COL]),
-                f_sb[:, v0:v1],
+                prod[c, d][:, HALF_V * t : HALF_V * (t + 1)],
+                h[t][:].indirect(pos_t[d][:, HALF_V // PER_COL * c : HALF_V // PER_COL * (c + 1)]),
+                f_sb[t // 2][:, HALF_V * (t % 2) : HALF_V * (t % 2 + 1)],
                 MULT,
             )
 
-        def gather_plain(t, tag=""):
-            g_t = sb("g%d" % t, [P, V], F32, tag)
-            nc.vector.tensor_copy(g_t[:], h[t][:].indirect(pos_t[0][:]))
-            return g_t
-
-        a0_bf = [sb("a0_bf0", [P, HALF], BF16, "w3_raw"), sb("a0_bf1", [P, HALF], BF16, "xw1")]
-        aq0 = planes("aq0", V)
-        for c in range(2):
-            cast_angles(nc.vector.tensor_copy, a0_bf[c][:], a_raw[0][:, :, V // 2 * c : V // 2 * (c + 1)])
-        for c in range(2):
-            quantize_into(aq0, V // 2 * c, V // 2 * (c + 1), a0_bf[c][:])
-        picked = [gather_plain(0, "w3_raw"), gather_plain(1, "xw1")]
-        f0_ps = filter_products(0, aq0)
-        for t in range(2):
-            nc.vector.tensor_tensor(prod[0][:, t, :], picked[t][:], f0_ps[t][:], MULT)
-        a_bf1 = sb("a_bf1", [P, PACK * V], BF16)
-        cast_angles(nc.scalar.copy, a_bf1[:], a_raw[1][:])
-        aq1 = quantize("aq1", a_bf1[:], V)
-        for t in range(2, PACK):
-            gather_product(0, filter_copy("f0_%d" % t, f0_ps[t]), t, 0, V)
-        f1_ps = filter_products(1, aq1)
-        f1 = []
-        for t in range(PACK):
-            f1.append(filter_copy("f1_%d" % t, f1_ps[t]))
-            gather_product(1, f1[t], t, 0, V)
-
-        for b, (v0, v1) in enumerate(V_BLOCKS):
-            z_bf = sb("z_bf%d" % b, [P, PACK * (v1 - v0)], BF16)
+        def add_neighbours(c, v0, v1, tag=""):
+            z_bf = sb("z_bf%d_%d" % (c, v0), [P, PACK * (v1 - v0)], BF16, tag)
             nc.vector.tensor_tensor(
                 z_bf[:].rearrange("p (c i t) -> p c t i", i=2, t=PACK),
-                prod[0][:, :, v0:v1].rearrange("p t (c i) -> p c t i", i=2),
-                prod[1][:, :, v0:v1].rearrange("p t (c i) -> p c t i", i=2),
+                prod[c, 0][:].rearrange("p (t c i) -> p c t i", i=2, t=PACK)[:, v0 // 2 : v1 // 2],
+                prod[c, 1][:].rearrange("p (t c i) -> p c t i", i=2, t=PACK)[:, v0 // 2 : v1 // 2],
                 ADD,
             )
-            zq = quantize("zq%d" % b, z_bf[:], v1 - v0)
-            o_ps = bank("o_ps%d" % b)
+            return z_bf
+
+        def project(c, v0, v1, z_bf, tag=""):
+            zq = quantize("zq%d_%d" % (c, v0), z_bf[:], tag)
+            o_ps = bank("o_ps%d_%d" % (c, v0))
             nc.tensor.matmul_mx(
                 out=o_ps[:, 0 : v1 - v0],
                 lhsT=w2w[:].bitcast(FP4X4),
@@ -233,6 +204,51 @@ def tile_picked_dime_none_p_kernel(
                 start=True,
                 stop=True,
             )
-            o_sb = sb("o_sb%d" % b, [P, v1 - v0], F32)
+            o_sb = sb("o_sb%d_%d" % (c, v0), [P, v1 - v0], F32)
             nc.scalar.copy(o_sb[:], o_ps[:, 0 : v1 - v0])
-            nc.sync.dma_start(out=out[:, v0:v1], in_=o_sb[:])
+            nc.sync.dma_start(out=out[:, HALF_V * c + v0 : HALF_V * c + v1], in_=o_sb[:])
+
+        w3_bf = [sb("w3_bf0", [P, 2 * H], BF16, "w1_bf1_1"), sb("w3_bf1", [P, 2 * H], BF16, "w1_bf0_1")]
+        for u in range(2):
+            cast_weight(nc.vector.tensor_copy, w3_bf[u], w3_raw, u)
+        w3q = [quantize("w3q0", w3_bf[0][:])]
+        a_bf = sb("a_bf0_0", [P, PACK * HALF_V], BF16)
+        cast_angles(nc.vector.tensor_copy, a_bf[:], 0, 0)
+        w3q.append(quantize("w3q1", w3_bf[1][:], "a_raw0_0"))
+        aq = quantize("aq00", a_bf[:], offset=7168)
+        a_bf = new_product(0, 0)
+        cast_angles(nc.vector.tensor_copy, a_bf, 0, 1)
+        f00 = [filters(0, 0, u, aq, 2048 * u) for u in range(2)]
+        h.append(sb_at("h3", [P, S], F32, 4096))
+        silu(PACK - 1)
+        gather_product(0, 0, 0, f00)
+        aq = quantize("aq01", a_bf)
+        f01 = [filters(0, 1, 0, aq)]
+        for t in range(1, PACK):
+            gather_product(0, 0, t, f00)
+        f01.append(filters(0, 1, 1, aq))
+        a_bf = new_product(0, 1, "aq01_codes")
+        cast_angles(nc.scalar.copy, a_bf, 1, 0)
+        for t in range(2):
+            gather_product(0, 1, t, f01)
+        aq = quantize("aq10", a_bf)
+        f10 = [filters(1, 0, u, aq) for u in range(2)]
+        for t in range(2, PACK):
+            gather_product(0, 1, t, f01)
+        a_bf = new_product(1, 0, "aq10_codes")
+        cast_angles(nc.scalar.copy, a_bf, 1, 1)
+        for t in range(2):
+            gather_product(1, 0, t, f10)
+        aq = quantize("aq11", a_bf)
+        f11 = [filters(1, 1, u, aq) for u in range(2)]
+        z0 = add_neighbours(0, 0, HALF_V, "f1_0_0")
+        for t in range(2, PACK):
+            gather_product(1, 0, t, f10)
+        project(0, 0, HALF_V, z0, "f1_0_1")
+        new_product(1, 1)
+        for t in range(PACK):
+            gather_product(1, 1, t, f11)
+        ends = ((0, HALF_V // 2), (HALF_V // 2, HALF_V))
+        z1 = [add_neighbours(1, v0, v1) for v0, v1 in ends]
+        for (v0, v1), z_bf in zip(ends, z1):
+            project(1, v0, v1, z_bf)

@@ -1,6 +1,7 @@
 from contextlib import ExitStack
 
 import concourse.mybir as mybir
+from concourse.masks import make_identity
 
 K, T, S, V, H, N, J, U = 1024, 2048, 1024, 512, 512, 128, 512, 1024
 FLOPS = 2 * (K * H * S + J * H * U + H * N * V)
@@ -31,7 +32,7 @@ def tile_picked_dime_none_p_kernel(
     with ExitStack() as ctx:
         keep = ctx.enter_context(tc.tile_pool(name="keep", bufs=1))
         lap = ctx.enter_context(tc.tile_pool(name="lap", bufs=1))
-        psum = ctx.enter_context(tc.psum_pool(name="psum", bufs=8))
+        psum = ctx.enter_context(tc.psum_pool(name="psum", bufs=1))
 
         def sb(name, shape, dtype, tag=""):
             return keep.tile(shape, dtype, name=name, tag=tag or name, align_bytes=64)
@@ -39,8 +40,8 @@ def tile_picked_dime_none_p_kernel(
         def sb_at(name, shape, dtype, offset):
             return lap.tile(shape, dtype, name=name, offset=offset, align_bytes=64)
 
-        def bank(name):
-            return psum.tile([P, BANK], F32, name=name, tag="bank")
+        def bank(name, n):
+            return psum.tile([P, BANK], F32, name=name, tag="bank%d" % n)
 
         offs_t = keep.tile([P, S // PER_COL], U16, name="offs_t")
         pos_t = [keep.tile([P, V // PER_COL], U16, name="pos%d_t" % d) for d in range(2)]
@@ -61,6 +62,9 @@ def tile_picked_dime_none_p_kernel(
         nc.gpsimd.memset(warm[:], 0.0)
         nc.gpsimd.memset(w2s[:].bitcast(I32), 0)
         nc.scalar.activation(warm_out[:], warm[:], SILU)
+
+        ident = sb("ident", [P, P], F32)
+        make_identity(nc, ident[:])
 
         def load_words(g):
             nc.sync.dma_start(out=xw[g][:].bitcast(I32), in_=x_words[g].rearrange("p n t -> p (n t)").bitcast(I32))
@@ -110,7 +114,7 @@ def tile_picked_dime_none_p_kernel(
             return codes, scales
 
         h = [sb("h%d" % t, [P, S], F32) for t in range(PACK - 1)]
-        h_ps = [[bank("h_ps%d_%d" % (t, s)) for s in range(2)] for t in range(PACK)]
+        h_ps = [[bank("h_ps%d_%d" % (t, s), 2 * t + s) for s in range(2)] for t in range(PACK)]
         gw0 = sb("gw0", [P, S], U32)
         gs = sb("gs", [P, S], U8)
         gw1 = [sb("gw1_%d" % s, [P, BANK], U32) for s in range(2)]
@@ -142,11 +146,11 @@ def tile_picked_dime_none_p_kernel(
         h_pass(quantize("w1q00", w1_bf[0][0][:]), 0, 0)
         for s in range(2):
             nc.vector.tensor_copy(gw1[s][:], xw[1][:].indirect(offs_t[:, 32 * s : 32 * s + 32]))
-        for u in range(2):
-            cast_weight(nc.scalar.copy, w1_bf[1][u], w1_raw[1], u, 0, P // 2)
-            cast_weight(nc.vector.tensor_copy, w1_bf[1][u], w1_raw[1], u, P // 2, P)
+        cast_weight(nc.scalar.copy, w1_bf[1][0], w1_raw[1], 0, 0, P // 2)
+        cast_weight(nc.vector.tensor_copy, w1_bf[1][0], w1_raw[1], 0, P // 2, P)
+        cast_weight(nc.scalar.copy, w1_bf[1][1], w1_raw[1], 1)
         h_pass(quantize("w1q10", w1_bf[1][0][:]), 1, 0)
-        h_pass(quantize("w1q01", w1_bf[0][1][:], "w1_raw1"), 0, 1)
+        h_pass(quantize("w1q01", w1_bf[0][1][:], "w1_bf1_0"), 0, 1)
         h_pass(quantize("w1q11", w1_bf[1][1][:]), 1, 1)
         for t in range(PACK - 1):
             silu(t)
@@ -155,10 +159,10 @@ def tile_picked_dime_none_p_kernel(
 
         def new_product(c, d, tag=""):
             prod[c, d] = sb("prod%d_%d" % (c, d), [P, PACK * HALF_V], F32, tag)
-            return prod[c, d][:, 2 * HALF_V : 4 * HALF_V].bitcast(BF16)
+            return prod[c, d][:, HALF_V : 3 * HALF_V].bitcast(BF16)
 
-        def filters(c, d, u, aq, offset=None):
-            f_ps = bank("f_ps%d_%d_%d" % (c, d, u))
+        def filters(c, d, u, aq):
+            f_ps = bank("f_ps%d_%d_%d" % (c, d, u), 2 * d + u)
             for i in range(2):
                 nc.tensor.matmul_mx(
                     out=f_ps[:, HALF_V * i : HALF_V * (i + 1)],
@@ -169,6 +173,9 @@ def tile_picked_dime_none_p_kernel(
                     start=True,
                     stop=True,
                 )
+            return f_ps
+
+        def unload(c, d, u, f_ps, offset=None):
             name = "f%d_%d_%d" % (c, d, u)
             f_sb = sb(name, [P, BANK], F32) if offset is None else sb_at(name, [P, BANK], F32, offset)
             nc.scalar.copy(f_sb[:], f_ps[:])
@@ -192,9 +199,44 @@ def tile_picked_dime_none_p_kernel(
             )
             return z_bf
 
+        def add_turned(c, b):
+            sums = bank("sums%d_%d" % (c, b), 4 + b)
+            for t in range(PACK):
+                for d in range(2):
+                    nc.tensor.matmul(
+                        sums[:, P * t : P * (t + 1)],
+                        lhsT=prod[c, d][:, HALF_V * t + P * b : HALF_V * t + P * (b + 1)],
+                        rhs=ident[:],
+                        start=(d == 0),
+                        stop=(d == 1),
+                        is_transpose=True,
+                    )
+            return sums
+
+        def turn_back(c, b, sums, back):
+            turned = sb("turned%d_%d" % (c, b), [P, PACK * P], BF16)
+            nc.scalar.copy(
+                turned[:].rearrange("v (u p e) -> v u p e", u=2, e=2),
+                sums[:].rearrange("v (u e p) -> v u p e", u=2, e=2),
+            )
+            for u in range(2):
+                nc.tensor.transpose(
+                    back[:, P * (2 * b + u) : P * (2 * b + u + 1)],
+                    turned[:].bitcast(F32)[:, P * u : P * (u + 1)],
+                    ident[:],
+                )
+
+        def weave_words(c, back):
+            z_bf = sb("z_bf%d" % c, [P, PACK * HALF_V], BF16)
+            nc.scalar.copy(
+                z_bf[:].bitcast(F32).rearrange("p (b v u) -> p b v u", b=2, u=2),
+                back[:].rearrange("p (b u v) -> p b v u", b=2, u=2),
+            )
+            return z_bf
+
         def project(c, v0, v1, z_bf, tag=""):
             zq = quantize("zq%d_%d" % (c, v0), z_bf[:], tag)
-            o_ps = bank("o_ps%d_%d" % (c, v0))
+            o_ps = bank("o_ps%d_%d" % (c, v0), 7 - c - v0 // P)
             nc.tensor.matmul_mx(
                 out=o_ps[:, 0 : v1 - v0],
                 lhsT=w2w[:].bitcast(FP4X4),
@@ -211,44 +253,53 @@ def tile_picked_dime_none_p_kernel(
         w3_bf = [sb("w3_bf0", [P, 2 * H], BF16, "w1_bf1_1"), sb("w3_bf1", [P, 2 * H], BF16, "w1_bf0_1")]
         for u in range(2):
             cast_weight(nc.vector.tensor_copy, w3_bf[u], w3_raw, u)
-        w3q = [quantize("w3q0", w3_bf[0][:])]
         a_bf = sb("a_bf0_0", [P, PACK * HALF_V], BF16)
         cast_angles(nc.vector.tensor_copy, a_bf[:], 0, 0)
-        w3q.append(quantize("w3q1", w3_bf[1][:], "a_raw0_0"))
+        w3q = [quantize("w3q0", w3_bf[0][:], "a_raw0_0")]
         aq = quantize("aq00", a_bf[:], offset=7168)
+        f00 = [unload(0, 0, 0, filters(0, 0, 0, aq), 0)]
         a_bf = new_product(0, 0)
         cast_angles(nc.vector.tensor_copy, a_bf, 0, 1)
-        f00 = [filters(0, 0, u, aq, 2048 * u) for u in range(2)]
+        w3q.append(quantize("w3q1", w3_bf[1][:], offset=2048))
+        f00.append(unload(0, 0, 1, filters(0, 0, 1, aq)))
         h.append(sb_at("h3", [P, S], F32, 4096))
         silu(PACK - 1)
-        gather_product(0, 0, 0, f00)
         aq = quantize("aq01", a_bf)
-        f01 = [filters(0, 1, 0, aq)]
-        for t in range(1, PACK):
+        f_ps = [filters(0, 1, u, aq) for u in range(2)]
+        for t in range(PACK):
             gather_product(0, 0, t, f00)
-        f01.append(filters(0, 1, 1, aq))
+
+        f01 = [unload(0, 1, 0, f_ps[0])]
         a_bf = new_product(0, 1, "aq01_codes")
         cast_angles(nc.scalar.copy, a_bf, 1, 0)
-        for t in range(2):
-            gather_product(0, 1, t, f01)
+        f01.append(unload(0, 1, 1, f_ps[1]))
+        gather_product(0, 1, 0, f01)
         aq = quantize("aq10", a_bf)
-        f10 = [filters(1, 0, u, aq) for u in range(2)]
-        for t in range(2, PACK):
+        f_ps = [filters(1, 0, u, aq) for u in range(2)]
+        for t in range(1, PACK):
             gather_product(0, 1, t, f01)
+
+        sums = [add_turned(0, b) for b in range(2)]
+        f10 = [unload(1, 0, 0, f_ps[0])]
         a_bf = new_product(1, 0, "aq10_codes")
         cast_angles(nc.scalar.copy, a_bf, 1, 1)
-        for t in range(2):
-            gather_product(1, 0, t, f10)
+        f10.append(unload(1, 0, 1, f_ps[1]))
+        gather_product(1, 0, 0, f10)
         aq = quantize("aq11", a_bf)
-        f11 = [filters(1, 1, u, aq) for u in range(2)]
-        z0 = add_neighbours(0, 0, HALF_V, "f1_0_0")
-        for t in range(2, PACK):
+        f_ps = [filters(1, 1, u, aq) for u in range(2)]
+        for t in range(1, PACK):
             gather_product(1, 0, t, f10)
-        project(0, 0, HALF_V, z0, "f1_0_1")
+
+        f11 = [unload(1, 1, u, f_ps[u]) for u in range(2)]
+        back = bank("back0", 6)
+        for b in range(2):
+            turn_back(0, b, sums[b], back)
+        z0 = weave_words(0, back)
         new_product(1, 1)
         for t in range(PACK):
             gather_product(1, 1, t, f11)
+        project(0, 0, HALF_V, z0)
         ends = ((0, HALF_V // 2), (HALF_V // 2, HALF_V))
-        z1 = [add_neighbours(1, v0, v1) for v0, v1 in ends]
+        z1 = [add_neighbours(1, v0, v1, "" if v0 else "z_bf0") for v0, v1 in ends]
         for (v0, v1), z_bf in zip(ends, z1):
             project(1, v0, v1, z_bf)

@@ -31,14 +31,10 @@ def tile_picked_dime_none_p_kernel(
     nc = tc.nc
     with ExitStack() as ctx:
         keep = ctx.enter_context(tc.tile_pool(name="keep", bufs=1))
-        lap = ctx.enter_context(tc.tile_pool(name="lap", bufs=1))
         psum = ctx.enter_context(tc.psum_pool(name="psum", bufs=1))
 
         def sb(name, shape, dtype, tag=""):
             return keep.tile(shape, dtype, name=name, tag=tag or name, align_bytes=64)
-
-        def sb_at(name, shape, dtype, offset):
-            return lap.tile(shape, dtype, name=name, offset=offset, align_bytes=64)
 
         def bank(name, n):
             return psum.tile([P, BANK], F32, name=name, tag="bank%d" % n)
@@ -49,9 +45,13 @@ def tile_picked_dime_none_p_kernel(
         xs = sb("xs", [P, T], U8)
         w1_raw = [sb("w1_raw%d" % g, [P, PACK, H], F32) for g in range(2)]
         w3_raw = sb("w3_raw", [P, PACK, H], F32)
+        last_first = sb("last_first", [P, (PACK + 1) * HALF_V], F32)
         a_raw = [
-            [sb("a_raw0_0", [P, PACK, HALF_V], F32), sb_at("a_raw0_1", [P, PACK, HALF_V], F32, 1024)],
-            [sb("a_raw1_%d" % d, [P, PACK, HALF_V], F32) for d in range(2)],
+            [sb("a_raw0_%d" % d, [P, PACK, HALF_V], F32)[:] for d in range(2)],
+            [
+                sb("a_raw1_0", [P, PACK, HALF_V], F32)[:],
+                last_first[:, HALF_V:].rearrange("p (j c) -> p j c", j=PACK),
+            ],
         ]
         w2w = sb("w2w", [P, 2 * N], U8)
         w2s = sb("w2s", [P, N], U8)
@@ -70,7 +70,7 @@ def tile_picked_dime_none_p_kernel(
             nc.sync.dma_start(out=xw[g][:].bitcast(I32), in_=x_words[g].rearrange("p n t -> p (n t)").bitcast(I32))
 
         def load_rows(raw, rows):
-            nc.sync.dma_start(out=raw[:], in_=rows.rearrange("(p j) c -> p j c", j=PACK))
+            nc.sync.dma_start(out=raw, in_=rows.rearrange("(p j) c -> p j c", j=PACK))
 
         def load_angles(c, d):
             load_rows(a_raw[c][d], aT[:, V * d + HALF_V * c : V * d + HALF_V * (c + 1)])
@@ -79,14 +79,14 @@ def tile_picked_dime_none_p_kernel(
         load_words(0)
         for q in range(4):
             nc.sync.dma_start(out=xs[32 * q : 32 * q + 8, :].bitcast(I32), in_=x_scales[:, 4 * q : 4 * q + 4, :].bitcast(I32))
-        load_rows(w1_raw[0], w1[0:512, :])
+        load_rows(w1_raw[0][:], w1[0:512, :])
         load_words(1)
-        load_rows(w1_raw[1], w1[512:1024, :])
-        load_rows(w3_raw, w3)
+        load_rows(w1_raw[1][:], w1[512:1024, :])
         load_angles(0, 0)
+        load_rows(w3_raw[:], w3)
+        load_angles(0, 1)
         nc.sync.dma_start(pos_t[0][:], pos1)
         nc.sync.dma_start(pos_t[1][:], pos2)
-        load_angles(0, 1)
         load_angles(1, 0)
         load_angles(1, 1)
 
@@ -103,32 +103,30 @@ def tile_picked_dime_none_p_kernel(
         def cast_angles(copy, dst, c, d):
             copy(
                 dst.rearrange("p (c i j) -> p c j i", i=2, j=PACK),
-                a_raw[c][d][:].rearrange("p j (c i) -> p c j i", i=2),
+                a_raw[c][d].rearrange("p j (c i) -> p c j i", i=2),
             )
 
-        def quantize(name, src, tag="", offset=None):
+        def quantize(name, src, tag=""):
             cols = src.shape[1] // PACK
-            codes = sb(name + "_codes", [P, cols], U32, tag) if offset is None else sb_at(name + "_codes", [P, cols], U32, offset)
+            codes = sb(name + "_codes", [P, cols], U32, tag)
             scales = sb(name + "_scales", [P, cols], U8)
             nc.vector.quantize_mx(out=codes[:].bitcast(FP8X4), scales=scales[:], in_=src)
             return codes, scales
 
         h = [sb("h%d" % t, [P, S], F32) for t in range(PACK - 1)]
         h_ps = [[bank("h_ps%d_%d" % (t, s), 2 * t + s) for s in range(2)] for t in range(PACK)]
-        gw0 = sb("gw0", [P, S], U32)
+        gw = [sb("gw%d" % g, [P, S], U32) for g in range(2)]
         gs = sb("gs", [P, S], U8)
-        gw1 = [sb("gw1_%d" % s, [P, BANK], U32) for s in range(2)]
 
         def h_pass(wq, g, u):
             for i in range(2):
                 for s in range(2):
                     cols = slice(BANK * s, BANK * (s + 1))
-                    words = gw0[:, cols] if g == 0 else gw1[s][:]
                     nc.tensor.matmul_mx(
                         out=h_ps[2 * u + i][s][:],
                         lhsT=wq[0][:, P * i : P * (i + 1)].bitcast(FP8X4),
                         lhsT_scale=wq[1][:, P * i : P * (i + 1)],
-                        rhs=words.bitcast(FP8X4),
+                        rhs=gw[g][:, cols].bitcast(FP8X4),
                         rhs_scale=gs[4 * g : P, cols],
                         start=(g == 0),
                         stop=(g == 1),
@@ -138,63 +136,57 @@ def tile_picked_dime_none_p_kernel(
             for s in range(2):
                 nc.scalar.activation(h[t][:, BANK * s : BANK * (s + 1)], h_ps[t][s][:], SILU)
 
-        nc.vector.tensor_copy(gw0[:], xw[0][:].indirect(offs_t[:]))
+        nc.vector.tensor_copy(gw[0][:], xw[0][:].indirect(offs_t[:]))
         nc.vector.tensor_copy(gs[:], xs[:].indirect(offs_t[:]))
         w1_bf = [[sb("w1_bf%d_%d" % (g, u), [P, 2 * H], BF16) for u in range(2)] for g in range(2)]
         for u in range(2):
             cast_weight(nc.scalar.copy, w1_bf[0][u], w1_raw[0], u)
         h_pass(quantize("w1q00", w1_bf[0][0][:]), 0, 0)
-        for s in range(2):
-            nc.vector.tensor_copy(gw1[s][:], xw[1][:].indirect(offs_t[:, 32 * s : 32 * s + 32]))
-        cast_weight(nc.scalar.copy, w1_bf[1][0], w1_raw[1], 0, 0, P // 2)
-        cast_weight(nc.vector.tensor_copy, w1_bf[1][0], w1_raw[1], 0, P // 2, P)
-        cast_weight(nc.scalar.copy, w1_bf[1][1], w1_raw[1], 1)
+        nc.vector.tensor_copy(gw[1][:], xw[1][:].indirect(offs_t[:]))
+        for u in range(2):
+            cast_weight(nc.scalar.copy, w1_bf[1][u], w1_raw[1], u, 0, P // 2)
+            cast_weight(nc.vector.tensor_copy, w1_bf[1][u], w1_raw[1], u, P // 2, P)
         h_pass(quantize("w1q10", w1_bf[1][0][:]), 1, 0)
-        h_pass(quantize("w1q01", w1_bf[0][1][:], "w1_bf1_0"), 0, 1)
+        h_pass(quantize("w1q01", w1_bf[0][1][:], "w1_raw1"), 0, 1)
         h_pass(quantize("w1q11", w1_bf[1][1][:]), 1, 1)
         for t in range(PACK - 1):
             silu(t)
 
-        prod = {}
-
-        def new_product(c, d, tag=""):
-            prod[c, d] = sb("prod%d_%d" % (c, d), [P, PACK * HALF_V], F32, tag)
-            return prod[c, d][:, HALF_V : 3 * HALF_V].bitcast(BF16)
-
-        def filters(c, d, u, aq):
-            f_ps = bank("f_ps%d_%d_%d" % (c, d, u), 2 * d + u)
-            for i in range(2):
+        def filters(name, tiles, aq, n):
+            f_ps = bank(name, n)
+            for i, t in enumerate(tiles):
                 nc.tensor.matmul_mx(
                     out=f_ps[:, HALF_V * i : HALF_V * (i + 1)],
-                    lhsT=w3q[u][0][:, P * i : P * (i + 1)].bitcast(FP8X4),
-                    lhsT_scale=w3q[u][1][:, P * i : P * (i + 1)],
+                    lhsT=w3q[t // 2][0][:, P * (t % 2) : P * (t % 2 + 1)].bitcast(FP8X4),
+                    lhsT_scale=w3q[t // 2][1][:, P * (t % 2) : P * (t % 2 + 1)],
                     rhs=aq[0][:].bitcast(FP8X4),
                     rhs_scale=aq[1][:],
                     start=True,
                     stop=True,
                 )
-            return f_ps
+            return f_ps[:, 0 : HALF_V * len(tiles)]
 
-        def unload(c, d, u, f_ps, offset=None):
-            name = "f%d_%d_%d" % (c, d, u)
-            f_sb = sb(name, [P, BANK], F32) if offset is None else sb_at(name, [P, BANK], F32, offset)
-            nc.scalar.copy(f_sb[:], f_ps[:])
-            return f_sb
+        def unload(name, f_ps):
+            f_sb = sb(name, [P, f_ps.shape[1]], F32)
+            nc.scalar.copy(f_sb[:], f_ps)
+            return [f_sb[:, v : v + HALF_V] for v in range(0, f_ps.shape[1], HALF_V)]
 
-        def gather_product(c, d, t, f_sb):
+        prod = {}
+
+        def gather_product(c, d, t, f_sb, v0=0, v1=HALF_V):
             nc.vector.tensor_tensor(
-                prod[c, d][:, HALF_V * t : HALF_V * (t + 1)],
-                h[t][:].indirect(pos_t[d][:, HALF_V // PER_COL * c : HALF_V // PER_COL * (c + 1)]),
-                f_sb[t // 2][:, HALF_V * (t % 2) : HALF_V * (t % 2 + 1)],
+                prod[c, d][t][:, v0:v1],
+                h[t][:].indirect(pos_t[d][:, (HALF_V * c + v0) // PER_COL : (HALF_V * c + v1) // PER_COL]),
+                f_sb[t][:, v0:v1],
                 MULT,
             )
 
-        def add_neighbours(c, v0, v1, tag=""):
-            z_bf = sb("z_bf%d_%d" % (c, v0), [P, PACK * (v1 - v0)], BF16, tag)
+        def add_neighbours(first, second, v0, v1):
+            z_bf = sb("z_bf1_%d" % v0, [P, PACK * (v1 - v0)], BF16)
             nc.vector.tensor_tensor(
                 z_bf[:].rearrange("p (c i t) -> p c t i", i=2, t=PACK),
-                prod[c, 0][:].rearrange("p (t c i) -> p c t i", i=2, t=PACK)[:, v0 // 2 : v1 // 2],
-                prod[c, 1][:].rearrange("p (t c i) -> p c t i", i=2, t=PACK)[:, v0 // 2 : v1 // 2],
+                first.rearrange("p (t c i) -> p c t i", i=2, t=PACK)[:, v0 // 2 : v1 // 2],
+                second.rearrange("p (t c i) -> p c t i", i=2, t=PACK)[:, v0 // 2 : v1 // 2],
                 ADD,
             )
             return z_bf
@@ -205,7 +197,7 @@ def tile_picked_dime_none_p_kernel(
                 for d in range(2):
                     nc.tensor.matmul(
                         sums[:, P * t : P * (t + 1)],
-                        lhsT=prod[c, d][:, HALF_V * t + P * b : HALF_V * t + P * (b + 1)],
+                        lhsT=prod[c, d][t][:, P * b : P * (b + 1)],
                         rhs=ident[:],
                         start=(d == 0),
                         stop=(d == 1),
@@ -234,8 +226,8 @@ def tile_picked_dime_none_p_kernel(
             )
             return z_bf
 
-        def project(c, v0, v1, z_bf, tag=""):
-            zq = quantize("zq%d_%d" % (c, v0), z_bf[:], tag)
+        def project(c, v0, v1, z_bf):
+            zq = quantize("zq%d_%d" % (c, v0), z_bf[:])
             o_ps = bank("o_ps%d_%d" % (c, v0), 7 - c - v0 // P)
             nc.tensor.matmul_mx(
                 out=o_ps[:, 0 : v1 - v0],
@@ -250,56 +242,63 @@ def tile_picked_dime_none_p_kernel(
             nc.scalar.copy(o_sb[:], o_ps[:, 0 : v1 - v0])
             nc.sync.dma_start(out=out[:, HALF_V * c + v0 : HALF_V * c + v1], in_=o_sb[:])
 
-        w3_bf = [sb("w3_bf0", [P, 2 * H], BF16, "w1_bf1_1"), sb("w3_bf1", [P, 2 * H], BF16, "w1_bf0_1")]
+        a_bf = sb("a_bf0_0", [P, PACK * HALF_V], BF16, "w1_bf1_0")
+        cast_angles(nc.vector.tensor_copy, a_bf[:], 0, 0)
+        aq = quantize("aq00", a_bf[:])
+        w3_bf = [sb("w3_bf%d" % u, [P, 2 * H], BF16) for u in range(2)]
         for u in range(2):
             cast_weight(nc.vector.tensor_copy, w3_bf[u], w3_raw, u)
-        a_bf = sb("a_bf0_0", [P, PACK * HALF_V], BF16)
-        cast_angles(nc.vector.tensor_copy, a_bf[:], 0, 0)
-        w3q = [quantize("w3q0", w3_bf[0][:], "a_raw0_0")]
-        aq = quantize("aq00", a_bf[:], offset=7168)
-        f00 = [unload(0, 0, 0, filters(0, 0, 0, aq), 0)]
-        a_bf = new_product(0, 0)
-        cast_angles(nc.vector.tensor_copy, a_bf, 0, 1)
-        w3q.append(quantize("w3q1", w3_bf[1][:], offset=2048))
-        f00.append(unload(0, 0, 1, filters(0, 0, 1, aq)))
-        h.append(sb_at("h3", [P, S], F32, 4096))
+        w3q = [quantize("w3q0", w3_bf[0][:])]
+        f00 = unload("f00_0", filters("f_ps00_0", (0,), aq, 0)) + unload("f00_1", filters("f_ps00_1", (1,), aq, 1))
+        a_bf = sb("a_bf0_1", [P, PACK * HALF_V], BF16)
+        cast_angles(nc.vector.tensor_copy, a_bf[:], 0, 1)
+        w3q.append(quantize("w3q1", w3_bf[1][:]))
+        f00 = f00 + unload("f00_2", filters("f_ps00_2", (2, 3), aq, 2))
+        h.append(sb("h3", [P, S], F32, "a_raw0_1"))
         silu(PACK - 1)
-        aq = quantize("aq01", a_bf)
-        f_ps = [filters(0, 1, u, aq) for u in range(2)]
+        aq = quantize("aq01", a_bf[:])
+        f_ps = [filters("f_ps01_0", (0, 1), aq, 3), filters("f_ps01_1", (2, 3), aq, 0)]
+        prod[0, 0] = [sb("prod00_%d" % t, [P, HALF_V], F32)[:] for t in range(PACK)]
         for t in range(PACK):
             gather_product(0, 0, t, f00)
 
-        f01 = [unload(0, 1, 0, f_ps[0])]
-        a_bf = new_product(0, 1, "aq01_codes")
-        cast_angles(nc.scalar.copy, a_bf, 1, 0)
-        f01.append(unload(0, 1, 1, f_ps[1]))
+        f01 = unload("f01_0", f_ps[0])
+        a_bf = sb("a_bf1_0", [P, PACK * HALF_V], BF16, "aq01_codes")
+        cast_angles(nc.scalar.copy, a_bf[:], 1, 0)
+        f01 = f01 + unload("f01_1", f_ps[1])
+        prod[0, 1] = [sb("prod01_0", [P, HALF_V], F32)[:]]
         gather_product(0, 1, 0, f01)
-        aq = quantize("aq10", a_bf)
-        f_ps = [filters(1, 0, u, aq) for u in range(2)]
-        for t in range(1, PACK):
+        aq = quantize("aq10", a_bf[:])
+        f_ps = [filters("f_ps10_0", (0, 1), aq, 1), filters("f_ps10_1", (2, 3), aq, 2)]
+        for t, tag in ((1, "a_raw1_0"), (2, ""), (3, "")):
+            prod[0, 1].append(sb("prod01_%d" % t, [P, HALF_V], F32, tag)[:])
             gather_product(0, 1, t, f01)
 
         sums = [add_turned(0, b) for b in range(2)]
-        f10 = [unload(1, 0, 0, f_ps[0])]
-        a_bf = new_product(1, 0, "aq10_codes")
-        cast_angles(nc.scalar.copy, a_bf, 1, 1)
-        f10.append(unload(1, 0, 1, f_ps[1]))
+        f10 = unload("f10_0", f_ps[0])
+        a_bf = sb("a_bf1_1", [P, PACK * HALF_V], BF16, "aq10_codes")
+        cast_angles(nc.scalar.copy, a_bf[:], 1, 1)
+        f10 = f10 + unload("f10_1", f_ps[1])
+        prod[1, 0] = [last_first[:, HALF_V * t : HALF_V * (t + 1)] for t in range(PACK)]
         gather_product(1, 0, 0, f10)
-        aq = quantize("aq11", a_bf)
-        f_ps = [filters(1, 1, u, aq) for u in range(2)]
+        aq = quantize("aq11", a_bf[:])
+        f_ps = [filters("f_ps11_0", (0, 1), aq, 3), filters("f_ps11_1", (2, 3), aq, 0)]
         for t in range(1, PACK):
             gather_product(1, 0, t, f10)
 
-        f11 = [unload(1, 1, u, f_ps[u]) for u in range(2)]
+        f11 = unload("f11_0", f_ps[0]) + unload("f11_1", f_ps[1])
         back = bank("back0", 6)
         for b in range(2):
             turn_back(0, b, sums[b], back)
         z0 = weave_words(0, back)
-        new_product(1, 1)
-        for t in range(PACK):
+        last_second = sb("last_second", [P, PACK * HALF_V], F32)
+        prod[1, 1] = [last_second[:, HALF_V * t : HALF_V * (t + 1)] for t in range(PACK)]
+        for t in range(PACK - 1):
             gather_product(1, 1, t, f11)
-        project(0, 0, HALF_V, z0)
         ends = ((0, HALF_V // 2), (HALF_V // 2, HALF_V))
-        z1 = [add_neighbours(1, v0, v1, "" if v0 else "z_bf0") for v0, v1 in ends]
+        for v0, v1 in ends:
+            gather_product(1, 1, PACK - 1, f11, v0, v1)
+        project(0, 0, HALF_V, z0)
+        z1 = [add_neighbours(last_first[:, 0 : PACK * HALF_V], last_second[:], v0, v1) for v0, v1 in ends]
         for (v0, v1), z_bf in zip(ends, z1):
             project(1, v0, v1, z_bf)

@@ -20,9 +20,13 @@ ADD = mybir.AluOpType.add
 
 P = 128
 PACK = 4
+K_PASS = P * PACK
 BANK = 512
+QUADRANT = 32
+ROWS = 4
 PER_COL = 16
 HALF_V = V // 2
+FILTER_BANKS, SUMS_BANK, BACK_BANK, OUT_BANK = 4, 4, 6, 7
 
 
 def tile_picked_dime_none_p_kernel(
@@ -45,14 +49,13 @@ def tile_picked_dime_none_p_kernel(
         xs = sb("xs", [P, T], U8)
         w1_raw = [sb("w1_raw%d" % g, [P, PACK, H], F32) for g in range(2)]
         w3_raw = sb("w3_raw", [P, PACK, H], F32)
-        last_first = sb("last_first", [P, (PACK + 1) * HALF_V], F32)
-        a_raw = [
-            [sb("a_raw0_%d" % d, [P, PACK, HALF_V], F32)[:] for d in range(2)],
-            [
-                sb("a_raw1_0", [P, PACK, HALF_V], F32)[:],
-                last_first[:, HALF_V:].rearrange("p (j c) -> p j c", j=PACK),
-            ],
-        ]
+        prod10 = sb("prod10", [P, (PACK + 1) * HALF_V], F32)
+        a_raw = {
+            (0, 0): sb("a_raw00", [P, PACK, HALF_V], F32)[:],
+            (0, 1): sb("a_raw01", [P, PACK, HALF_V], F32)[:],
+            (1, 0): sb("a_raw10", [P, PACK, HALF_V], F32)[:],
+            (1, 1): prod10[:, HALF_V:].rearrange("p (j c) -> p j c", j=PACK),
+        }
         w2w = sb("w2w", [P, 2 * N], U8)
         w2s = sb("w2s", [P, N], U8)
         warm = sb("warm", [P, 8], F32)
@@ -73,15 +76,18 @@ def tile_picked_dime_none_p_kernel(
             nc.sync.dma_start(out=raw, in_=rows.rearrange("(p j) c -> p j c", j=PACK))
 
         def load_angles(c, d):
-            load_rows(a_raw[c][d], aT[:, V * d + HALF_V * c : V * d + HALF_V * (c + 1)])
+            load_rows(a_raw[c, d], aT[:, V * d + HALF_V * c : V * d + HALF_V * (c + 1)])
 
         nc.sync.dma_start(offs_t[:], offs)
         load_words(0)
-        for q in range(4):
-            nc.sync.dma_start(out=xs[32 * q : 32 * q + 8, :].bitcast(I32), in_=x_scales[:, 4 * q : 4 * q + 4, :].bitcast(I32))
-        load_rows(w1_raw[0][:], w1[0:512, :])
+        for q in range(P // QUADRANT):
+            nc.sync.dma_start(
+                out=xs[QUADRANT * q : QUADRANT * q + 2 * ROWS, :].bitcast(I32),
+                in_=x_scales[:, ROWS * q : ROWS * (q + 1), :].bitcast(I32),
+            )
+        load_rows(w1_raw[0][:], w1[0:K_PASS, :])
         load_words(1)
-        load_rows(w1_raw[1][:], w1[512:1024, :])
+        load_rows(w1_raw[1][:], w1[K_PASS:K, :])
         load_angles(0, 0)
         load_rows(w3_raw[:], w3)
         load_angles(0, 1)
@@ -89,10 +95,12 @@ def tile_picked_dime_none_p_kernel(
         nc.sync.dma_start(pos_t[1][:], pos2)
         load_angles(1, 0)
         load_angles(1, 1)
-
         nc.sync.dma_start(out=w2w[:].bitcast(I32), in_=w2_words[0].bitcast(I32))
-        for q in range(4):
-            nc.sync.dma_start(out=w2s[32 * q : 32 * q + 4, :].bitcast(I32), in_=w2_scales[0, 4 * q : 4 * q + 4, :].bitcast(I32))
+        for q in range(P // QUADRANT):
+            nc.sync.dma_start(
+                out=w2s[QUADRANT * q : QUADRANT * q + ROWS, :].bitcast(I32),
+                in_=w2_scales[0, ROWS * q : ROWS * (q + 1), :].bitcast(I32),
+            )
 
         def cast_weight(copy, dst, raw, u, m0=0, m1=P):
             copy(
@@ -100,17 +108,19 @@ def tile_picked_dime_none_p_kernel(
                 raw[:].rearrange("p j (m t) -> p m j t", t=PACK)[:, m0:m1, :, 2 * u : 2 * u + 2],
             )
 
-        def cast_angles(copy, dst, c, d):
+        def cast_angles(copy, c, d, tag=""):
+            a_bf = sb("a_bf%d%d" % (c, d), [P, PACK * HALF_V], BF16, tag)
             copy(
-                dst.rearrange("p (c i j) -> p c j i", i=2, j=PACK),
-                a_raw[c][d].rearrange("p j (c i) -> p c j i", i=2),
+                a_bf[:].rearrange("p (v e j) -> p v j e", e=2, j=PACK),
+                a_raw[c, d].rearrange("p j (v e) -> p v j e", e=2),
             )
+            return a_bf
 
         def quantize(name, src, tag=""):
             cols = src.shape[1] // PACK
             codes = sb(name + "_codes", [P, cols], U32, tag)
             scales = sb(name + "_scales", [P, cols], U8)
-            nc.vector.quantize_mx(out=codes[:].bitcast(FP8X4), scales=scales[:], in_=src)
+            nc.vector.quantize_mx(out=codes[:].bitcast(FP8X4), scales=scales[:], in_=src[:])
             return codes, scales
 
         h = [sb("h%d" % t, [P, S], F32) for t in range(PACK - 1)]
@@ -119,15 +129,15 @@ def tile_picked_dime_none_p_kernel(
         gs = sb("gs", [P, S], U8)
 
         def h_pass(wq, g, u):
-            for i in range(2):
+            for e in range(2):
                 for s in range(2):
                     cols = slice(BANK * s, BANK * (s + 1))
                     nc.tensor.matmul_mx(
-                        out=h_ps[2 * u + i][s][:],
-                        lhsT=wq[0][:, P * i : P * (i + 1)].bitcast(FP8X4),
-                        lhsT_scale=wq[1][:, P * i : P * (i + 1)],
+                        out=h_ps[2 * u + e][s][:],
+                        lhsT=wq[0][:, P * e : P * (e + 1)].bitcast(FP8X4),
+                        lhsT_scale=wq[1][:, P * e : P * (e + 1)],
                         rhs=gw[g][:, cols].bitcast(FP8X4),
-                        rhs_scale=gs[4 * g : P, cols],
+                        rhs_scale=gs[ROWS * g : P, cols],
                         start=(g == 0),
                         stop=(g == 1),
                     )
@@ -138,27 +148,34 @@ def tile_picked_dime_none_p_kernel(
 
         nc.vector.tensor_copy(gw[0][:], xw[0][:].indirect(offs_t[:]))
         nc.vector.tensor_copy(gs[:], xs[:].indirect(offs_t[:]))
-        w1_bf = [[sb("w1_bf%d_%d" % (g, u), [P, 2 * H], BF16) for u in range(2)] for g in range(2)]
+        w1_bf = [[sb("w1_bf%d%d" % (g, u), [P, 2 * H], BF16) for u in range(2)] for g in range(2)]
         for u in range(2):
             cast_weight(nc.scalar.copy, w1_bf[0][u], w1_raw[0], u)
-        h_pass(quantize("w1q00", w1_bf[0][0][:]), 0, 0)
+        h_pass(quantize("w1q00", w1_bf[0][0]), 0, 0)
         nc.vector.tensor_copy(gw[1][:], xw[1][:].indirect(offs_t[:]))
         for u in range(2):
             cast_weight(nc.scalar.copy, w1_bf[1][u], w1_raw[1], u, 0, P // 2)
             cast_weight(nc.vector.tensor_copy, w1_bf[1][u], w1_raw[1], u, P // 2, P)
-        h_pass(quantize("w1q10", w1_bf[1][0][:]), 1, 0)
-        h_pass(quantize("w1q01", w1_bf[0][1][:], "w1_raw1"), 0, 1)
-        h_pass(quantize("w1q11", w1_bf[1][1][:]), 1, 1)
+        a_bf = cast_angles(nc.scalar.copy, 0, 0)
+        h_pass(quantize("w1q10", w1_bf[1][0]), 1, 0)
+        h_pass(quantize("w1q01", w1_bf[0][1], "w1_raw1"), 0, 1)
+        h_pass(quantize("w1q11", w1_bf[1][1]), 1, 1)
         for t in range(PACK - 1):
             silu(t)
 
-        def filters(name, tiles, aq, n):
-            f_ps = bank(name, n)
-            for i, t in enumerate(tiles):
+        filter_banks = []
+
+        def filters(tiles, aq):
+            n = len(filter_banks)
+            f_ps = bank("f_ps%d" % n, n % FILTER_BANKS)
+            filter_banks.append(f_ps)
+            for e, t in enumerate(tiles):
+                codes, scales = w3q[t // 2]
+                cols = slice(P * (t % 2), P * (t % 2 + 1))
                 nc.tensor.matmul_mx(
-                    out=f_ps[:, HALF_V * i : HALF_V * (i + 1)],
-                    lhsT=w3q[t // 2][0][:, P * (t % 2) : P * (t % 2 + 1)].bitcast(FP8X4),
-                    lhsT_scale=w3q[t // 2][1][:, P * (t % 2) : P * (t % 2 + 1)],
+                    out=f_ps[:, HALF_V * e : HALF_V * (e + 1)],
+                    lhsT=codes[:, cols].bitcast(FP8X4),
+                    lhsT_scale=scales[:, cols],
                     rhs=aq[0][:].bitcast(FP8X4),
                     rhs_scale=aq[1][:],
                     start=True,
@@ -181,23 +198,23 @@ def tile_picked_dime_none_p_kernel(
                 MULT,
             )
 
-        def add_neighbours(first, second, v0, v1):
+        def add_on_vector(first, second, v0, v1):
             z_bf = sb("z_bf1_%d" % v0, [P, PACK * (v1 - v0)], BF16)
             nc.vector.tensor_tensor(
-                z_bf[:].rearrange("p (c i t) -> p c t i", i=2, t=PACK),
-                first.rearrange("p (t c i) -> p c t i", i=2, t=PACK)[:, v0 // 2 : v1 // 2],
-                second.rearrange("p (t c i) -> p c t i", i=2, t=PACK)[:, v0 // 2 : v1 // 2],
+                z_bf[:].rearrange("p (v e t) -> p v t e", e=2, t=PACK),
+                first.rearrange("p (t v e) -> p v t e", e=2, t=PACK)[:, v0 // 2 : v1 // 2],
+                second.rearrange("p (t v e) -> p v t e", e=2, t=PACK)[:, v0 // 2 : v1 // 2],
                 ADD,
             )
             return z_bf
 
-        def add_turned(c, b):
-            sums = bank("sums%d_%d" % (c, b), 4 + b)
+        def add_turned(b):
+            sums = bank("sums%d" % b, SUMS_BANK + b)
             for t in range(PACK):
                 for d in range(2):
                     nc.tensor.matmul(
                         sums[:, P * t : P * (t + 1)],
-                        lhsT=prod[c, d][t][:, P * b : P * (b + 1)],
+                        lhsT=prod[0, d][t][:, P * b : P * (b + 1)],
                         rhs=ident[:],
                         start=(d == 0),
                         stop=(d == 1),
@@ -205,8 +222,8 @@ def tile_picked_dime_none_p_kernel(
                     )
             return sums
 
-        def turn_back(c, b, sums, back):
-            turned = sb("turned%d_%d" % (c, b), [P, PACK * P], BF16)
+        def turn_back(b, sums, back):
+            turned = sb("turned%d" % b, [P, PACK * P], BF16)
             nc.scalar.copy(
                 turned[:].rearrange("v (u p e) -> v u p e", u=2, e=2),
                 sums[:].rearrange("v (u e p) -> v u p e", u=2, e=2),
@@ -218,87 +235,81 @@ def tile_picked_dime_none_p_kernel(
                     ident[:],
                 )
 
-        def weave_words(c, back):
-            z_bf = sb("z_bf%d" % c, [P, PACK * HALF_V], BF16)
+        def weave_words(back):
+            z_bf = sb("z_bf0", [P, PACK * HALF_V], BF16)
             nc.scalar.copy(
                 z_bf[:].bitcast(F32).rearrange("p (b v u) -> p b v u", b=2, u=2),
                 back[:].rearrange("p (b u v) -> p b v u", b=2, u=2),
             )
             return z_bf
 
-        def project(c, v0, v1, z_bf):
-            zq = quantize("zq%d_%d" % (c, v0), z_bf[:])
-            o_ps = bank("o_ps%d_%d" % (c, v0), 7 - c - v0 // P)
+        def project(n, v0, v1, z_bf):
+            codes, scales = quantize("zq%d" % n, z_bf)
+            o_ps = bank("o_ps%d" % n, OUT_BANK - n)
             nc.tensor.matmul_mx(
                 out=o_ps[:, 0 : v1 - v0],
                 lhsT=w2w[:].bitcast(FP4X4),
                 lhsT_scale=w2s[:],
-                rhs=zq[0][:].bitcast(FP8X4),
-                rhs_scale=zq[1][:],
+                rhs=codes[:].bitcast(FP8X4),
+                rhs_scale=scales[:],
                 start=True,
                 stop=True,
             )
-            o_sb = sb("o_sb%d_%d" % (c, v0), [P, v1 - v0], F32)
+            o_sb = sb("o_sb%d" % n, [P, v1 - v0], F32)
             nc.scalar.copy(o_sb[:], o_ps[:, 0 : v1 - v0])
-            nc.sync.dma_start(out=out[:, HALF_V * c + v0 : HALF_V * c + v1], in_=o_sb[:])
+            nc.sync.dma_start(out=out[:, v0:v1], in_=o_sb[:])
 
-        a_bf = sb("a_bf0_0", [P, PACK * HALF_V], BF16, "w1_bf1_0")
-        cast_angles(nc.vector.tensor_copy, a_bf[:], 0, 0)
-        aq = quantize("aq00", a_bf[:])
+        aq = quantize("aq00", a_bf)
         w3_bf = [sb("w3_bf%d" % u, [P, 2 * H], BF16) for u in range(2)]
         for u in range(2):
             cast_weight(nc.vector.tensor_copy, w3_bf[u], w3_raw, u)
-        w3q = [quantize("w3q0", w3_bf[0][:])]
-        f00 = unload("f00_0", filters("f_ps00_0", (0,), aq, 0)) + unload("f00_1", filters("f_ps00_1", (1,), aq, 1))
-        a_bf = sb("a_bf0_1", [P, PACK * HALF_V], BF16)
-        cast_angles(nc.vector.tensor_copy, a_bf[:], 0, 1)
-        w3q.append(quantize("w3q1", w3_bf[1][:]))
-        f00 = f00 + unload("f00_2", filters("f_ps00_2", (2, 3), aq, 2))
-        h.append(sb("h3", [P, S], F32, "a_raw0_1"))
+        w3q = [quantize("w3q0", w3_bf[0])]
+        f00 = unload("f00_0", filters((0,), aq)) + unload("f00_1", filters((1,), aq))
+        a_bf = cast_angles(nc.vector.tensor_copy, 0, 1)
+        w3q.append(quantize("w3q1", w3_bf[1]))
+        f00 = f00 + unload("f00_2", filters((2, 3), aq))
+        h.append(sb("h3", [P, S], F32, "a_raw01"))
         silu(PACK - 1)
-        aq = quantize("aq01", a_bf[:])
-        f_ps = [filters("f_ps01_0", (0, 1), aq, 3), filters("f_ps01_1", (2, 3), aq, 0)]
         prod[0, 0] = [sb("prod00_%d" % t, [P, HALF_V], F32)[:] for t in range(PACK)]
-        for t in range(PACK):
+        gather_product(0, 0, 0, f00)
+        aq = quantize("aq01", a_bf)
+        f_ps = [filters((2 * u, 2 * u + 1), aq) for u in range(2)]
+        for t in range(1, PACK):
             gather_product(0, 0, t, f00)
 
         f01 = unload("f01_0", f_ps[0])
-        a_bf = sb("a_bf1_0", [P, PACK * HALF_V], BF16, "aq01_codes")
-        cast_angles(nc.scalar.copy, a_bf[:], 1, 0)
+        a_bf = cast_angles(nc.scalar.copy, 1, 0, "aq01_codes")
         f01 = f01 + unload("f01_1", f_ps[1])
-        prod[0, 1] = [sb("prod01_0", [P, HALF_V], F32)[:]]
+        prod[0, 1] = [sb("prod01_%d" % t, [P, HALF_V], F32, "a_raw10" if t == 1 else "")[:] for t in range(PACK)]
         gather_product(0, 1, 0, f01)
-        aq = quantize("aq10", a_bf[:])
-        f_ps = [filters("f_ps10_0", (0, 1), aq, 1), filters("f_ps10_1", (2, 3), aq, 2)]
-        for t, tag in ((1, "a_raw1_0"), (2, ""), (3, "")):
-            prod[0, 1].append(sb("prod01_%d" % t, [P, HALF_V], F32, tag)[:])
+        aq = quantize("aq10", a_bf)
+        f_ps = [filters((2 * u, 2 * u + 1), aq) for u in range(2)]
+        for t in range(1, PACK):
             gather_product(0, 1, t, f01)
+        sums = [add_turned(b) for b in range(2)]
 
-        sums = [add_turned(0, b) for b in range(2)]
         f10 = unload("f10_0", f_ps[0])
-        a_bf = sb("a_bf1_1", [P, PACK * HALF_V], BF16, "aq10_codes")
-        cast_angles(nc.scalar.copy, a_bf[:], 1, 1)
+        a_bf = cast_angles(nc.scalar.copy, 1, 1, "aq10_codes")
         f10 = f10 + unload("f10_1", f_ps[1])
-        prod[1, 0] = [last_first[:, HALF_V * t : HALF_V * (t + 1)] for t in range(PACK)]
+        prod[1, 0] = [prod10[:, HALF_V * t : HALF_V * (t + 1)] for t in range(PACK)]
         gather_product(1, 0, 0, f10)
-        aq = quantize("aq11", a_bf[:])
-        f_ps = [filters("f_ps11_0", (0, 1), aq, 3), filters("f_ps11_1", (2, 3), aq, 0)]
+        aq = quantize("aq11", a_bf)
+        f_ps = [filters((2 * u, 2 * u + 1), aq) for u in range(2)]
         for t in range(1, PACK):
             gather_product(1, 0, t, f10)
 
         f11 = unload("f11_0", f_ps[0]) + unload("f11_1", f_ps[1])
-        back = bank("back0", 6)
+        back = bank("back", BACK_BANK)
         for b in range(2):
-            turn_back(0, b, sums[b], back)
-        z0 = weave_words(0, back)
-        last_second = sb("last_second", [P, PACK * HALF_V], F32)
-        prod[1, 1] = [last_second[:, HALF_V * t : HALF_V * (t + 1)] for t in range(PACK)]
+            turn_back(b, sums[b], back)
+        z0 = weave_words(back)
+        prod11 = sb("prod11", [P, PACK * HALF_V], F32)
+        prod[1, 1] = [prod11[:, HALF_V * t : HALF_V * (t + 1)] for t in range(PACK)]
         for t in range(PACK - 1):
             gather_product(1, 1, t, f11)
-        ends = ((0, HALF_V // 2), (HALF_V // 2, HALF_V))
-        for v0, v1 in ends:
-            gather_product(1, 1, PACK - 1, f11, v0, v1)
+        for b in range(2):
+            gather_product(1, 1, PACK - 1, f11, P * b, P * (b + 1))
         project(0, 0, HALF_V, z0)
-        z1 = [add_neighbours(last_first[:, 0 : PACK * HALF_V], last_second[:], v0, v1) for v0, v1 in ends]
-        for (v0, v1), z_bf in zip(ends, z1):
-            project(1, v0, v1, z_bf)
+        z1 = [add_on_vector(prod10[:, 0 : PACK * HALF_V], prod11[:], P * b, P * (b + 1)) for b in range(2)]
+        for b in range(2):
+            project(1 + b, HALF_V + P * b, HALF_V + P * (b + 1), z1[b])

@@ -268,13 +268,11 @@ def tile_picked_dime_none_p_kernel(
         a_bf = cast_angles(nc.vector.tensor_copy, 0, 1)
         w3q.append(quantize("w3q1", w3_bf[1]))
         f00 = f00 + unload("f00_2", filters((2, 3), aq))
-        h.append(sb("h3", [P, S], F32, "a_raw01"))
-        silu(PACK - 1)
         prod[0, 0] = [sb("prod00_%d" % t, [P, HALF_V], F32)[:] for t in range(PACK)]
         gather_product(0, 0, 0, f00)
         aq = quantize("aq01", a_bf)
         f_ps = [filters((2 * u, 2 * u + 1), aq) for u in range(2)]
-        for t in range(1, PACK):
+        for t in range(1, PACK - 1):
             gather_product(0, 0, t, f00)
 
         f01 = unload("f01_0", f_ps[0])
@@ -284,8 +282,12 @@ def tile_picked_dime_none_p_kernel(
         gather_product(0, 1, 0, f01)
         aq = quantize("aq10", a_bf)
         f_ps = [filters((2 * u, 2 * u + 1), aq) for u in range(2)]
-        for t in range(1, PACK):
+        h.append(sb("h3", [P, S], F32, "aq01_codes"))
+        silu(PACK - 1)
+        for t in range(1, PACK - 1):
             gather_product(0, 1, t, f01)
+        for d, f_sb in enumerate((f00, f01)):
+            gather_product(0, d, PACK - 1, f_sb)
         sums = [add_turned(b) for b in range(2)]
 
         f10 = unload("f10_0", f_ps[0])

@@ -149,17 +149,17 @@ def tile_picked_dime_none_p_kernel(
         nc.vector.tensor_copy(gw[0][:], xw[0][:].indirect(offs_t[:]))
         nc.vector.tensor_copy(gs[:], xs[:].indirect(offs_t[:]))
         w1_bf = [[sb("w1_bf%d%d" % (g, u), [P, 2 * H], BF16) for u in range(2)] for g in range(2)]
+        for u, copy in enumerate((nc.scalar.copy, nc.vector.tensor_copy)):
+            cast_weight(copy, w1_bf[0][u], w1_raw[0], u)
         for u in range(2):
-            cast_weight(nc.scalar.copy, w1_bf[0][u], w1_raw[0], u)
-        h_pass(quantize("w1q00", w1_bf[0][0]), 0, 0)
+            h_pass(quantize("w1q0%d" % u, w1_bf[0][u]), 0, u)
         nc.vector.tensor_copy(gw[1][:], xw[1][:].indirect(offs_t[:]))
         for u in range(2):
             cast_weight(nc.scalar.copy, w1_bf[1][u], w1_raw[1], u, 0, P // 2)
             cast_weight(nc.vector.tensor_copy, w1_bf[1][u], w1_raw[1], u, P // 2, P)
         a_bf = cast_angles(nc.scalar.copy, 0, 0)
-        h_pass(quantize("w1q10", w1_bf[1][0]), 1, 0)
-        h_pass(quantize("w1q01", w1_bf[0][1], "w1_raw1"), 0, 1)
-        h_pass(quantize("w1q11", w1_bf[1][1]), 1, 1)
+        for u in range(2):
+            h_pass(quantize("w1q1%d" % u, w1_bf[1][u]), 1, u)
         for t in range(PACK - 1):
             silu(t)
 

@@ -149,8 +149,9 @@ def tile_picked_dime_none_p_kernel(
         nc.vector.tensor_copy(gw[0][:], xw[0][:].indirect(offs_t[:]))
         nc.vector.tensor_copy(gs[:], xs[:].indirect(offs_t[:]))
         w1_bf = [[sb("w1_bf%d%d" % (g, u), [P, 2 * H], BF16) for u in range(2)] for g in range(2)]
-        for u, copy in enumerate((nc.scalar.copy, nc.vector.tensor_copy)):
-            cast_weight(copy, w1_bf[0][u], w1_raw[0], u)
+        cast_weight(nc.scalar.copy, w1_bf[0][0], w1_raw[0], 0)
+        cast_weight(nc.scalar.copy, w1_bf[0][1], w1_raw[0], 1, 0, P // 2)
+        cast_weight(nc.vector.tensor_copy, w1_bf[0][1], w1_raw[0], 1, P // 2, P)
         for u in range(2):
             h_pass(quantize("w1q0%d" % u, w1_bf[0][u]), 0, u)
         nc.vector.tensor_copy(gw[1][:], xw[1][:].indirect(offs_t[:]))

@@ -1,7 +1,6 @@
 from contextlib import ExitStack
 
 import concourse.mybir as mybir
-from concourse.masks import make_identity
 
 K, T, S, V, H, N, J, U = 1024, 2048, 1024, 512, 512, 128, 512, 1024
 FLOPS = 2 * (K * H * S + J * H * U + H * N * V)
@@ -15,6 +14,7 @@ U8 = mybir.dt.uint8
 FP8X4 = mybir.dt.float8_e4m3fn_x4
 FP4X4 = mybir.dt.float4_e2m1fn_x4
 SILU = mybir.ActivationFunctionType.Silu
+COPY = mybir.ActivationFunctionType.Copy
 MULT = mybir.AluOpType.mult
 ADD = mybir.AluOpType.add
 
@@ -26,7 +26,6 @@ QUADRANT = 32
 ROWS = 4
 PER_COL = 16
 HALF_V = V // 2
-FILTER_BANKS, SUMS_BANK, BACK_BANK, OUT_BANK = 4, 4, 6, 7
 
 
 def tile_picked_dime_none_p_kernel(
@@ -49,12 +48,12 @@ def tile_picked_dime_none_p_kernel(
         xs = sb("xs", [P, T], U8)
         w1_raw = [sb("w1_raw%d" % g, [P, PACK, H], F32) for g in range(2)]
         w3_raw = sb("w3_raw", [P, PACK, H], F32)
-        prod10 = sb("prod10", [P, (PACK + 1) * HALF_V], F32)
+        prod0 = sb("prod0", [P, 2 * PACK * HALF_V], F32)
         a_raw = {
             (0, 0): sb("a_raw00", [P, PACK, HALF_V], F32)[:],
             (0, 1): sb("a_raw01", [P, PACK, HALF_V], F32)[:],
-            (1, 0): sb("a_raw10", [P, PACK, HALF_V], F32)[:],
-            (1, 1): prod10[:, HALF_V:].rearrange("p (j c) -> p j c", j=PACK),
+            (1, 0): prod0[:, 2 * HALF_V : 6 * HALF_V].rearrange("p (j c) -> p j c", j=PACK),
+            (1, 1): sb("a_raw11", [P, PACK, HALF_V], F32)[:],
         }
         w2w = sb("w2w", [P, 2 * N], U8)
         w2s = sb("w2s", [P, N], U8)
@@ -65,9 +64,6 @@ def tile_picked_dime_none_p_kernel(
         nc.gpsimd.memset(warm[:], 0.0)
         nc.gpsimd.memset(w2s[:].bitcast(I32), 0)
         nc.scalar.activation(warm_out[:], warm[:], SILU)
-
-        ident = sb("ident", [P, P], F32)
-        make_identity(nc, ident[:])
 
         def load_words(g):
             nc.sync.dma_start(out=xw[g][:].bitcast(I32), in_=x_words[g].rearrange("p n t -> p (n t)").bitcast(I32))
@@ -123,7 +119,7 @@ def tile_picked_dime_none_p_kernel(
             nc.vector.quantize_mx(out=codes[:].bitcast(FP8X4), scales=scales[:], in_=src[:])
             return codes, scales
 
-        h = [sb("h%d" % t, [P, S], F32) for t in range(PACK - 1)]
+        h = [sb("h%d" % t, [P, S], F32) for t in range(PACK)]
         h_ps = [[bank("h_ps%d_%d" % (t, s), 2 * t + s) for s in range(2)] for t in range(PACK)]
         gw = [sb("gw%d" % g, [P, S], U32) for g in range(2)]
         gs = sb("gs", [P, S], U8)
@@ -161,92 +157,69 @@ def tile_picked_dime_none_p_kernel(
         a_bf = cast_angles(nc.scalar.copy, 0, 0)
         for u in range(2):
             h_pass(quantize("w1q1%d" % u, w1_bf[1][u]), 1, u)
-        for t in range(PACK - 1):
+        for t in range(PACK):
             silu(t)
 
-        filter_banks = []
+        def filters(c, d, aq):
+            banks = []
+            for u in range(2):
+                f_ps = bank("f_ps%d%d%d" % (c, d, u), 4 * c + 2 * d + u)
+                codes, scales = w3q[u]
+                for e in range(2):
+                    cols = slice(P * e, P * (e + 1))
+                    nc.tensor.matmul_mx(
+                        out=f_ps[:, HALF_V * e : HALF_V * (e + 1)],
+                        lhsT=codes[:, cols].bitcast(FP8X4),
+                        lhsT_scale=scales[:, cols],
+                        rhs=aq[0][:].bitcast(FP8X4),
+                        rhs_scale=aq[1][:],
+                        start=True,
+                        stop=True,
+                    )
+                banks.append(f_ps)
+            return banks
 
-        def filters(tiles, aq):
-            n = len(filter_banks)
-            f_ps = bank("f_ps%d" % n, n % FILTER_BANKS)
-            filter_banks.append(f_ps)
-            for e, t in enumerate(tiles):
-                codes, scales = w3q[t // 2]
-                cols = slice(P * (t % 2), P * (t % 2 + 1))
-                nc.tensor.matmul_mx(
-                    out=f_ps[:, HALF_V * e : HALF_V * (e + 1)],
-                    lhsT=codes[:, cols].bitcast(FP8X4),
-                    lhsT_scale=scales[:, cols],
-                    rhs=aq[0][:].bitcast(FP8X4),
-                    rhs_scale=aq[1][:],
-                    start=True,
-                    stop=True,
-                )
-            return f_ps[:, 0 : HALF_V * len(tiles)]
+        picked = {}
+        prod = {(0, d): prod0[:, PACK * HALF_V * d : PACK * HALF_V * (d + 1)] for d in range(2)}
+        for d in range(2):
+            prod[1, d] = sb("prod1%d" % d, [P, PACK * HALF_V], F32)[:]
 
-        def unload(name, f_ps):
-            f_sb = sb(name, [P, f_ps.shape[1]], F32)
-            nc.scalar.copy(f_sb[:], f_ps)
-            return [f_sb[:, v : v + HALF_V] for v in range(0, f_ps.shape[1], HALF_V)]
+        def window(c, d, t, v0, v1):
+            return h[t][:].indirect(pos_t[d][:, (HALF_V * c + v0) // PER_COL : (HALF_V * c + v1) // PER_COL])
 
-        prod = {}
+        def slot(c, d, t, v0, v1):
+            if (c, d, t // 2) not in picked:
+                tag = {(0, 0, 0): "w3_raw", (0, 1, 1): "a_raw01"}.get((c, d, t // 2), "")
+                picked[c, d, t // 2] = sb("picked%d%d%d" % (c, d, t // 2), [P, 2 * HALF_V], F32, tag)
+            return picked[c, d, t // 2][:, HALF_V * (t % 2) + v0 : HALF_V * (t % 2) + v1]
 
-        def gather_product(c, d, t, f_sb, v0=0, v1=HALF_V):
+        def gather_vector(c, d, t, v0=0, v1=HALF_V):
+            nc.vector.tensor_copy(slot(c, d, t, v0, v1), window(c, d, t, v0, v1))
+
+        def gather_scalar(c, d, t, v0=0, v1=HALF_V):
+            nc.scalar.activation(slot(c, d, t, v0, v1), window(c, d, t, v0, v1), COPY)
+
+        def product(c, d, u, f_ps, v0=0, v1=HALF_V):
             nc.vector.tensor_tensor(
-                prod[c, d][t][:, v0:v1],
-                h[t][:].indirect(pos_t[d][:, (HALF_V * c + v0) // PER_COL : (HALF_V * c + v1) // PER_COL]),
-                f_sb[t][:, v0:v1],
+                prod[c, d].rearrange("p (t v) -> p t v", t=PACK)[:, 2 * u : 2 * u + 2, v0:v1],
+                picked[c, d, u][:].rearrange("p (e v) -> p e v", e=2)[:, :, v0:v1],
+                f_ps[u][:].rearrange("p (e v) -> p e v", e=2)[:, :, v0:v1],
                 MULT,
             )
 
-        def add_on_vector(first, second, v0, v1):
-            z_bf = sb("z_bf1_%d" % v0, [P, PACK * (v1 - v0)], BF16)
+        def add(c, v0, v1):
+            z_bf = sb("z_bf%d_%d" % (c, v0), [P, PACK * (v1 - v0)], BF16)
             nc.vector.tensor_tensor(
                 z_bf[:].rearrange("p (v e t) -> p v t e", e=2, t=PACK),
-                first.rearrange("p (t v e) -> p v t e", e=2, t=PACK)[:, v0 // 2 : v1 // 2],
-                second.rearrange("p (t v e) -> p v t e", e=2, t=PACK)[:, v0 // 2 : v1 // 2],
+                prod[c, 0].rearrange("p (t v e) -> p v t e", e=2, t=PACK)[:, v0 // 2 : v1 // 2],
+                prod[c, 1].rearrange("p (t v e) -> p v t e", e=2, t=PACK)[:, v0 // 2 : v1 // 2],
                 ADD,
-            )
-            return z_bf
-
-        def add_turned(b):
-            sums = bank("sums%d" % b, SUMS_BANK + b)
-            for t in range(PACK):
-                for d in range(2):
-                    nc.tensor.matmul(
-                        sums[:, P * t : P * (t + 1)],
-                        lhsT=prod[0, d][t][:, P * b : P * (b + 1)],
-                        rhs=ident[:],
-                        start=(d == 0),
-                        stop=(d == 1),
-                        is_transpose=True,
-                    )
-            return sums
-
-        def turn_back(b, sums, back):
-            turned = sb("turned%d" % b, [P, PACK * P], BF16)
-            nc.scalar.copy(
-                turned[:].rearrange("v (u p e) -> v u p e", u=2, e=2),
-                sums[:].rearrange("v (u e p) -> v u p e", u=2, e=2),
-            )
-            for u in range(2):
-                nc.tensor.transpose(
-                    back[:, P * (2 * b + u) : P * (2 * b + u + 1)],
-                    turned[:].bitcast(F32)[:, P * u : P * (u + 1)],
-                    ident[:],
-                )
-
-        def weave_words(back):
-            z_bf = sb("z_bf0", [P, PACK * HALF_V], BF16)
-            nc.scalar.copy(
-                z_bf[:].bitcast(F32).rearrange("p (b v u) -> p b v u", b=2, u=2),
-                back[:].rearrange("p (b u v) -> p b v u", b=2, u=2),
             )
             return z_bf
 
         def project(n, v0, v1, z_bf):
             codes, scales = quantize("zq%d" % n, z_bf)
-            o_ps = bank("o_ps%d" % n, OUT_BANK - n)
+            o_ps = bank("o_ps%d" % n, n)
             nc.tensor.matmul_mx(
                 out=o_ps[:, 0 : v1 - v0],
                 lhsT=w2w[:].bitcast(FP4X4),
@@ -260,59 +233,54 @@ def tile_picked_dime_none_p_kernel(
             nc.scalar.copy(o_sb[:], o_ps[:, 0 : v1 - v0])
             nc.sync.dma_start(out=out[:, v0:v1], in_=o_sb[:])
 
-        aq = quantize("aq00", a_bf)
+        for d, t in ((0, 2), (0, 3), (1, 0), (1, 1)):
+            gather_scalar(0, d, t)
+        for t in range(PACK):
+            gather_scalar(1, 0, t)
+        for b in range(2):
+            for t in range(PACK):
+                gather_scalar(1, 1, t, P * b, P * (b + 1))
+
+        def cast_on_gpsimd(c, d):
+            a_bf = sb("a_bf%d%d" % (c, d), [P, PACK * HALF_V], BF16, "w3_bf1")
+            nc.gpsimd.tensor_scalar(
+                a_bf[:].rearrange("p (v j) -> p v j", j=PACK),
+                a_raw[c, d].rearrange("p j v -> p v j"),
+                1.0,
+                0.0,
+                MULT,
+                ADD,
+            )
+            return a_bf
+
+        f = {}
+        aq00 = quantize("aq00", a_bf)
         w3_bf = [sb("w3_bf%d" % u, [P, 2 * H], BF16) for u in range(2)]
         for u in range(2):
             cast_weight(nc.vector.tensor_copy, w3_bf[u], w3_raw, u)
-        w3q = [quantize("w3q0", w3_bf[0])]
-        f00 = unload("f00_0", filters((0,), aq)) + unload("f00_1", filters((1,), aq))
-        a_bf = cast_angles(nc.vector.tensor_copy, 0, 1)
-        w3q.append(quantize("w3q1", w3_bf[1]))
-        f00 = f00 + unload("f00_2", filters((2, 3), aq))
-        prod[0, 0] = [sb("prod00_%d" % t, [P, HALF_V], F32)[:] for t in range(PACK)]
-        gather_product(0, 0, 0, f00)
-        aq = quantize("aq01", a_bf)
-        f_ps = [filters((2 * u, 2 * u + 1), aq) for u in range(2)]
-        for t in range(1, PACK - 1):
-            gather_product(0, 0, t, f00)
-
-        f01 = unload("f01_0", f_ps[0])
-        a_bf = cast_angles(nc.scalar.copy, 1, 0, "aq01_codes")
-        f01 = f01 + unload("f01_1", f_ps[1])
-        prod[0, 1] = [sb("prod01_%d" % t, [P, HALF_V], F32, "a_raw10" if t == 1 else "")[:] for t in range(PACK)]
-        gather_product(0, 1, 0, f01)
-        aq = quantize("aq10", a_bf)
-        f_ps = [filters((2 * u, 2 * u + 1), aq) for u in range(2)]
-        h.append(sb("h3", [P, S], F32, "aq01_codes"))
-        silu(PACK - 1)
-        for t in range(1, PACK - 1):
-            gather_product(0, 1, t, f01)
-        for d, f_sb in enumerate((f00, f01)):
-            gather_product(0, d, PACK - 1, f_sb)
-        sums = [add_turned(b) for b in range(2)]
-
-        f10 = unload("f10_0", f_ps[0])
-        a_bf = cast_angles(nc.scalar.copy, 1, 1, "aq10_codes")
-        f10 = f10 + unload("f10_1", f_ps[1])
-        prod[1, 0] = [prod10[:, HALF_V * t : HALF_V * (t + 1)] for t in range(PACK)]
-        gather_product(1, 0, 0, f10)
-        aq = quantize("aq11", a_bf)
-        f_ps = [filters((2 * u, 2 * u + 1), aq) for u in range(2)]
-        for t in range(1, PACK):
-            gather_product(1, 0, t, f10)
-
-        f11 = unload("f11_0", f_ps[0]) + unload("f11_1", f_ps[1])
-        back = bank("back", BACK_BANK)
-        for b in range(2):
-            turn_back(b, sums[b], back)
-        z0 = weave_words(back)
-        prod11 = sb("prod11", [P, PACK * HALF_V], F32)
-        prod[1, 1] = [prod11[:, HALF_V * t : HALF_V * (t + 1)] for t in range(PACK)]
-        for t in range(PACK - 1):
-            gather_product(1, 1, t, f11)
-        for b in range(2):
-            gather_product(1, 1, PACK - 1, f11, P * b, P * (b + 1))
+        w3q = [quantize("w3q%d" % u, w3_bf[u]) for u in range(2)]
+        f[0, 0] = filters(0, 0, aq00)
+        a_bf = cast_on_gpsimd(0, 1)
+        for t in range(2):
+            gather_vector(0, 0, t)
+        product(0, 0, 0, f[0, 0])
+        f[0, 1] = filters(0, 1, quantize("aq01", a_bf))
+        a_bf = cast_on_gpsimd(1, 0)
+        for t in range(2, PACK):
+            gather_vector(0, 1, t)
+        product(0, 1, 1, f[0, 1])
+        f[1, 0] = filters(1, 0, quantize("aq10", a_bf))
+        a_bf = cast_on_gpsimd(1, 1)
+        product(0, 0, 1, f[0, 0])
+        product(0, 1, 0, f[0, 1])
+        f[1, 1] = filters(1, 1, quantize("aq11", a_bf))
+        z0 = add(0, 0, HALF_V)
+        product(1, 0, 0, f[1, 0])
         project(0, 0, HALF_V, z0)
-        z1 = [add_on_vector(prod10[:, 0 : PACK * HALF_V], prod11[:], P * b, P * (b + 1)) for b in range(2)]
+        product(1, 0, 1, f[1, 0])
+        for b in range(2):
+            for u in range(2):
+                product(1, 1, u, f[1, 1], P * b, P * (b + 1))
+        z1 = [add(1, P * b, P * (b + 1)) for b in range(2)]
         for b in range(2):
             project(1 + b, HALF_V + P * b, HALF_V + P * (b + 1), z1[b])

@@ -48,11 +48,11 @@ def tile_picked_dime_none_p_kernel(
         xs = sb("xs", [P, T], U8)
         w1_raw = [sb("w1_raw%d" % g, [P, PACK, H], F32) for g in range(2)]
         w3_raw = sb("w3_raw", [P, PACK, H], F32)
-        prod0 = sb("prod0", [P, 2 * PACK * HALF_V], F32)
+        prod0 = sb("prod0", [P, 10 * HALF_V], F32)
         a_raw = {
             (0, 0): sb("a_raw00", [P, PACK, HALF_V], F32)[:],
-            (0, 1): sb("a_raw01", [P, PACK, HALF_V], F32)[:],
-            (1, 0): prod0[:, 2 * HALF_V : 6 * HALF_V].rearrange("p (j c) -> p j c", j=PACK),
+            (0, 1): prod0[:, 2 * HALF_V : 6 * HALF_V].rearrange("p (j c) -> p j c", j=PACK),
+            (1, 0): prod0[:, 6 * HALF_V : 10 * HALF_V].rearrange("p (j c) -> p j c", j=PACK),
             (1, 1): sb("a_raw11", [P, PACK, HALF_V], F32)[:],
         }
         w2w = sb("w2w", [P, 2 * N], U8)
@@ -74,8 +74,8 @@ def tile_picked_dime_none_p_kernel(
         def load_angles(c, d):
             load_rows(a_raw[c, d], aT[:, V * d + HALF_V * c : V * d + HALF_V * (c + 1)])
 
-        nc.sync.dma_start(offs_t[:], offs)
         load_words(0)
+        nc.sync.dma_start(offs_t[:], offs)
         for q in range(P // QUADRANT):
             nc.sync.dma_start(
                 out=xs[QUADRANT * q : QUADRANT * q + 2 * ROWS, :].bitcast(I32),
@@ -84,10 +84,10 @@ def tile_picked_dime_none_p_kernel(
         load_rows(w1_raw[0][:], w1[0:K_PASS, :])
         load_words(1)
         load_rows(w1_raw[1][:], w1[K_PASS:K, :])
-        load_angles(0, 0)
         load_rows(w3_raw[:], w3)
-        load_angles(0, 1)
+        load_angles(0, 0)
         nc.sync.dma_start(pos_t[0][:], pos1)
+        load_angles(0, 1)
         nc.sync.dma_start(pos_t[1][:], pos2)
         load_angles(1, 0)
         load_angles(1, 1)
@@ -147,14 +147,20 @@ def tile_picked_dime_none_p_kernel(
         w1_bf = [[sb("w1_bf%d%d" % (g, u), [P, 2 * H], BF16) for u in range(2)] for g in range(2)]
         cast_weight(nc.scalar.copy, w1_bf[0][0], w1_raw[0], 0)
         cast_weight(nc.scalar.copy, w1_bf[0][1], w1_raw[0], 1, 0, P // 2)
-        cast_weight(nc.vector.tensor_copy, w1_bf[0][1], w1_raw[0], 1, P // 2, P)
+        nc.gpsimd.tensor_scalar(
+            w1_bf[0][1][:].rearrange("p (t m j) -> p m t j", t=2, j=PACK)[:, P // 2 : P],
+            w1_raw[0][:].rearrange("p j (m t) -> p m t j", t=PACK)[:, P // 2 : P, 2:4],
+            1.0,
+            0.0,
+            MULT,
+            ADD,
+        )
         for u in range(2):
             h_pass(quantize("w1q0%d" % u, w1_bf[0][u]), 0, u)
         nc.vector.tensor_copy(gw[1][:], xw[1][:].indirect(offs_t[:]))
         for u in range(2):
-            cast_weight(nc.scalar.copy, w1_bf[1][u], w1_raw[1], u, 0, P // 2)
-            cast_weight(nc.vector.tensor_copy, w1_bf[1][u], w1_raw[1], u, P // 2, P)
-        a_bf = cast_angles(nc.scalar.copy, 0, 0)
+            cast_weight(nc.scalar.copy, w1_bf[1][u], w1_raw[1], u, 0, 3 * P // 4)
+            cast_weight(nc.vector.tensor_copy, w1_bf[1][u], w1_raw[1], u, 3 * P // 4, P)
         for u in range(2):
             h_pass(quantize("w1q1%d" % u, w1_bf[1][u]), 1, u)
         for t in range(PACK):
@@ -179,8 +185,8 @@ def tile_picked_dime_none_p_kernel(
                 banks.append(f_ps)
             return banks
 
-        picked = {}
-        prod = {(0, d): prod0[:, PACK * HALF_V * d : PACK * HALF_V * (d + 1)] for d in range(2)}
+        picked = {(0, 1, 1): prod0[:, 4 * HALF_V : 6 * HALF_V]}
+        prod = {(0, d): prod0[:, 6 * HALF_V * d : 6 * HALF_V * d + PACK * HALF_V] for d in range(2)}
         for d in range(2):
             prod[1, d] = sb("prod1%d" % d, [P, PACK * HALF_V], F32)[:]
 
@@ -189,8 +195,8 @@ def tile_picked_dime_none_p_kernel(
 
         def slot(c, d, t, v0, v1):
             if (c, d, t // 2) not in picked:
-                tag = {(0, 0, 0): "w3_raw", (0, 1, 1): "a_raw01"}.get((c, d, t // 2), "")
-                picked[c, d, t // 2] = sb("picked%d%d%d" % (c, d, t // 2), [P, 2 * HALF_V], F32, tag)
+                tag = "a_raw00" if (c, d, t // 2) == (0, 0, 0) else ""
+                picked[c, d, t // 2] = sb("picked%d%d%d" % (c, d, t // 2), [P, 2 * HALF_V], F32, tag)[:]
             return picked[c, d, t // 2][:, HALF_V * (t % 2) + v0 : HALF_V * (t % 2) + v1]
 
         def gather_vector(c, d, t, v0=0, v1=HALF_V):
@@ -202,20 +208,18 @@ def tile_picked_dime_none_p_kernel(
         def product(c, d, u, f_ps, v0=0, v1=HALF_V):
             nc.vector.tensor_tensor(
                 prod[c, d].rearrange("p (t v) -> p t v", t=PACK)[:, 2 * u : 2 * u + 2, v0:v1],
-                picked[c, d, u][:].rearrange("p (e v) -> p e v", e=2)[:, :, v0:v1],
+                picked[c, d, u].rearrange("p (e v) -> p e v", e=2)[:, :, v0:v1],
                 f_ps[u][:].rearrange("p (e v) -> p e v", e=2)[:, :, v0:v1],
                 MULT,
             )
 
-        def add(c, v0, v1):
-            z_bf = sb("z_bf%d_%d" % (c, v0), [P, PACK * (v1 - v0)], BF16)
+        def add(z_bf, c, v0, v1):
             nc.vector.tensor_tensor(
-                z_bf[:].rearrange("p (v e t) -> p v t e", e=2, t=PACK),
+                z_bf.rearrange("p (v e t) -> p v t e", e=2, t=PACK),
                 prod[c, 0].rearrange("p (t v e) -> p v t e", e=2, t=PACK)[:, v0 // 2 : v1 // 2],
                 prod[c, 1].rearrange("p (t v e) -> p v t e", e=2, t=PACK)[:, v0 // 2 : v1 // 2],
                 ADD,
             )
-            return z_bf
 
         def project(n, v0, v1, z_bf):
             codes, scales = quantize("zq%d" % n, z_bf)
@@ -242,7 +246,7 @@ def tile_picked_dime_none_p_kernel(
                 gather_scalar(1, 1, t, P * b, P * (b + 1))
 
         def cast_on_gpsimd(c, d):
-            a_bf = sb("a_bf%d%d" % (c, d), [P, PACK * HALF_V], BF16, "w3_bf1")
+            a_bf = sb("a_bf%d%d" % (c, d), [P, PACK * HALF_V], BF16, "a_bf00")
             nc.gpsimd.tensor_scalar(
                 a_bf[:].rearrange("p (v j) -> p v j", j=PACK),
                 a_raw[c, d].rearrange("p j v -> p v j"),
@@ -254,12 +258,13 @@ def tile_picked_dime_none_p_kernel(
             return a_bf
 
         f = {}
-        aq00 = quantize("aq00", a_bf)
         w3_bf = [sb("w3_bf%d" % u, [P, 2 * H], BF16) for u in range(2)]
         for u in range(2):
             cast_weight(nc.vector.tensor_copy, w3_bf[u], w3_raw, u)
-        w3q = [quantize("w3q%d" % u, w3_bf[u]) for u in range(2)]
-        f[0, 0] = filters(0, 0, aq00)
+        w3q = [quantize("w3q0", w3_bf[0])]
+        a_bf = cast_angles(nc.vector.tensor_copy, 0, 0)
+        w3q.append(quantize("w3q1", w3_bf[1]))
+        f[0, 0] = filters(0, 0, quantize("aq00", a_bf))
         a_bf = cast_on_gpsimd(0, 1)
         for t in range(2):
             gather_vector(0, 0, t)
@@ -268,19 +273,23 @@ def tile_picked_dime_none_p_kernel(
         a_bf = cast_on_gpsimd(1, 0)
         for t in range(2, PACK):
             gather_vector(0, 1, t)
-        product(0, 1, 1, f[0, 1])
+        product(0, 0, 1, f[0, 0])
         f[1, 0] = filters(1, 0, quantize("aq10", a_bf))
         a_bf = cast_on_gpsimd(1, 1)
-        product(0, 0, 1, f[0, 0])
-        product(0, 1, 0, f[0, 1])
-        f[1, 1] = filters(1, 1, quantize("aq11", a_bf))
-        z0 = add(0, 0, HALF_V)
+        for u in (1, 0):
+            product(0, 1, u, f[0, 1])
         product(1, 0, 0, f[1, 0])
-        project(0, 0, HALF_V, z0)
+        f[1, 1] = filters(1, 1, quantize("aq11", a_bf))
+        z0 = sb("z0", [P, PACK * HALF_V], BF16, "a_raw11")
+        add(z0[:], 0, 0, HALF_V)
         product(1, 0, 1, f[1, 0])
-        for b in range(2):
-            for u in range(2):
-                product(1, 1, u, f[1, 1], P * b, P * (b + 1))
-        z1 = [add(1, P * b, P * (b + 1)) for b in range(2)]
-        for b in range(2):
-            project(1 + b, HALF_V + P * b, HALF_V + P * (b + 1), z1[b])
+        product(1, 1, 0, f[1, 1], 0, P)
+        project(0, 0, HALF_V, z0)
+        product(1, 1, 1, f[1, 1], 0, P)
+        product(1, 1, 0, f[1, 1], P, HALF_V)
+        z1 = [sb("z1_%d" % b, [P, PACK * P], BF16) for b in range(2)]
+        add(z1[0][:], 1, 0, P)
+        product(1, 1, 1, f[1, 1], P, HALF_V)
+        project(1, HALF_V, HALF_V + P, z1[0])
+        add(z1[1][:], 1, P, HALF_V)
+        project(2, HALF_V + P, V, z1[1])

@@ -48,13 +48,12 @@ def tile_picked_dime_none_p_kernel(
         xs = sb("xs", [P, T], U8)
         w1_raw = [sb("w1_raw%d" % g, [P, PACK, H], F32) for g in range(2)]
         w3_raw = sb("w3_raw", [P, PACK, H], F32)
-        prod0 = sb("prod0", [P, 10 * HALF_V], F32)
-        a_raw = {
-            (0, 0): sb("a_raw00", [P, PACK, HALF_V], F32)[:],
-            (0, 1): prod0[:, 2 * HALF_V : 6 * HALF_V].rearrange("p (j c) -> p j c", j=PACK),
-            (1, 0): prod0[:, 6 * HALF_V : 10 * HALF_V].rearrange("p (j c) -> p j c", j=PACK),
-            (1, 1): sb("a_raw11", [P, PACK, HALF_V], F32)[:],
-        }
+        stage = sb("stage", [P, 15 * HALF_V], F32)
+
+        def rows(start):
+            return stage[:, start * HALF_V : (start + PACK) * HALF_V].rearrange("p (j c) -> p j c", j=PACK)
+
+        a_raw = {(0, 0): rows(7), (0, 1): rows(3), (1, 0): rows(11), (1, 1): sb("a_raw11", [P, PACK, HALF_V], F32)[:]}
         w2w = sb("w2w", [P, 2 * N], U8)
         w2s = sb("w2s", [P, N], U8)
         warm = sb("warm", [P, 8], F32)
@@ -185,8 +184,12 @@ def tile_picked_dime_none_p_kernel(
                 banks.append(f_ps)
             return banks
 
-        picked = {(0, 1, 1): prod0[:, 4 * HALF_V : 6 * HALF_V]}
-        prod = {(0, d): prod0[:, 6 * HALF_V * d : 6 * HALF_V * d + PACK * HALF_V] for d in range(2)}
+        picked = {
+            (0, 0, 0): stage[:, 9 * HALF_V : 11 * HALF_V],
+            (0, 1, 1): stage[:, 4 * HALF_V : 6 * HALF_V],
+            (1, 0, 0): stage[:, 7 * HALF_V - P : 9 * HALF_V - P],
+        }
+        prod = {(0, d): stage[:, 11 * HALF_V * d : 11 * HALF_V * d + PACK * HALF_V] for d in range(2)}
         for d in range(2):
             prod[1, d] = sb("prod1%d" % d, [P, PACK * HALF_V], F32)[:]
 
@@ -195,8 +198,7 @@ def tile_picked_dime_none_p_kernel(
 
         def slot(c, d, t, v0, v1):
             if (c, d, t // 2) not in picked:
-                tag = "a_raw00" if (c, d, t // 2) == (0, 0, 0) else ""
-                picked[c, d, t // 2] = sb("picked%d%d%d" % (c, d, t // 2), [P, 2 * HALF_V], F32, tag)[:]
+                picked[c, d, t // 2] = sb("picked%d%d%d" % (c, d, t // 2), [P, 2 * HALF_V], F32)[:]
             return picked[c, d, t // 2][:, HALF_V * (t % 2) + v0 : HALF_V * (t % 2) + v1]
 
         def gather_vector(c, d, t, v0=0, v1=HALF_V):
@@ -205,11 +207,11 @@ def tile_picked_dime_none_p_kernel(
         def gather_scalar(c, d, t, v0=0, v1=HALF_V):
             nc.scalar.activation(slot(c, d, t, v0, v1), window(c, d, t, v0, v1), COPY)
 
-        def product(c, d, u, f_ps, v0=0, v1=HALF_V):
+        def product(c, d, u, f_ps, v0=0, v1=HALF_V, e0=0, e1=2):
             nc.vector.tensor_tensor(
-                prod[c, d].rearrange("p (t v) -> p t v", t=PACK)[:, 2 * u : 2 * u + 2, v0:v1],
-                picked[c, d, u].rearrange("p (e v) -> p e v", e=2)[:, :, v0:v1],
-                f_ps[u][:].rearrange("p (e v) -> p e v", e=2)[:, :, v0:v1],
+                prod[c, d].rearrange("p (t v) -> p t v", t=PACK)[:, 2 * u + e0 : 2 * u + e1, v0:v1],
+                picked[c, d, u].rearrange("p (e v) -> p e v", e=2)[:, e0:e1, v0:v1],
+                f_ps[u][:].rearrange("p (e v) -> p e v", e=2)[:, e0:e1, v0:v1],
                 MULT,
             )
 
@@ -221,7 +223,7 @@ def tile_picked_dime_none_p_kernel(
                 ADD,
             )
 
-        def project(n, v0, v1, z_bf):
+        def project(n, v0, v1, z_bf, copy=nc.scalar.copy):
             codes, scales = quantize("zq%d" % n, z_bf)
             o_ps = bank("o_ps%d" % n, n)
             nc.tensor.matmul_mx(
@@ -234,16 +236,8 @@ def tile_picked_dime_none_p_kernel(
                 stop=True,
             )
             o_sb = sb("o_sb%d" % n, [P, v1 - v0], F32)
-            nc.scalar.copy(o_sb[:], o_ps[:, 0 : v1 - v0])
+            copy(o_sb[:], o_ps[:, 0 : v1 - v0])
             nc.sync.dma_start(out=out[:, v0:v1], in_=o_sb[:])
-
-        for d, t in ((0, 2), (0, 3), (1, 0), (1, 1)):
-            gather_scalar(0, d, t)
-        for t in range(PACK):
-            gather_scalar(1, 0, t)
-        for b in range(2):
-            for t in range(PACK):
-                gather_scalar(1, 1, t, P * b, P * (b + 1))
 
         def cast_on_gpsimd(c, d):
             a_bf = sb("a_bf%d%d" % (c, d), [P, PACK * HALF_V], BF16, "a_bf00")
@@ -266,23 +260,34 @@ def tile_picked_dime_none_p_kernel(
         w3q.append(quantize("w3q1", w3_bf[1]))
         f[0, 0] = filters(0, 0, quantize("aq00", a_bf))
         a_bf = cast_on_gpsimd(0, 1)
+        for d, t in ((0, 2), (0, 3), (1, 0), (1, 1)):
+            gather_scalar(0, d, t)
+        for t in range(1, PACK):
+            gather_scalar(1, 0, t)
+        for b in range(2):
+            for t in range(PACK):
+                gather_scalar(1, 1, t, P * b, P * (b + 1))
+
         for t in range(2):
             gather_vector(0, 0, t)
         product(0, 0, 0, f[0, 0])
+        gather_vector(1, 0, 0, P, HALF_V)
         f[0, 1] = filters(0, 1, quantize("aq01", a_bf))
         a_bf = cast_on_gpsimd(1, 0)
         for t in range(2, PACK):
             gather_vector(0, 1, t)
         product(0, 0, 1, f[0, 0])
+        gather_vector(1, 0, 0, 0, P)
         f[1, 0] = filters(1, 0, quantize("aq10", a_bf))
         a_bf = cast_on_gpsimd(1, 1)
         for u in (1, 0):
             product(0, 1, u, f[0, 1])
         product(1, 0, 0, f[1, 0])
+        product(1, 0, 1, f[1, 0], e1=1)
         f[1, 1] = filters(1, 1, quantize("aq11", a_bf))
         z0 = sb("z0", [P, PACK * HALF_V], BF16, "a_raw11")
         add(z0[:], 0, 0, HALF_V)
-        product(1, 0, 1, f[1, 0])
+        product(1, 0, 1, f[1, 0], e0=1)
         product(1, 1, 0, f[1, 1], 0, P)
         project(0, 0, HALF_V, z0)
         product(1, 1, 1, f[1, 1], 0, P)

@@ -264,14 +264,16 @@ def tile_picked_dime_none_p_kernel(
             gather_scalar(0, d, t)
         for t in range(1, PACK):
             gather_scalar(1, 0, t)
+        for t in range(2):
+            gather_scalar(1, 1, t)
         for b in range(2):
-            for t in range(PACK):
+            for t in range(2, PACK):
                 gather_scalar(1, 1, t, P * b, P * (b + 1))
 
         for t in range(2):
             gather_vector(0, 0, t)
-        product(0, 0, 0, f[0, 0])
         gather_vector(1, 0, 0, P, HALF_V)
+        product(0, 0, 0, f[0, 0])
         f[0, 1] = filters(0, 1, quantize("aq01", a_bf))
         a_bf = cast_on_gpsimd(1, 0)
         for t in range(2, PACK):
@@ -288,13 +290,12 @@ def tile_picked_dime_none_p_kernel(
         z0 = sb("z0", [P, PACK * HALF_V], BF16, "a_raw11")
         add(z0[:], 0, 0, HALF_V)
         product(1, 0, 1, f[1, 0], e0=1)
-        product(1, 1, 0, f[1, 1], 0, P)
+        product(1, 1, 0, f[1, 1])
         project(0, 0, HALF_V, z0)
         product(1, 1, 1, f[1, 1], 0, P)
-        product(1, 1, 0, f[1, 1], P, HALF_V)
         z1 = [sb("z1_%d" % b, [P, PACK * P], BF16) for b in range(2)]
-        add(z1[0][:], 1, 0, P)
         product(1, 1, 1, f[1, 1], P, HALF_V)
+        for b in range(2):
+            add(z1[b][:], 1, P * b, P * (b + 1))
         project(1, HALF_V, HALF_V + P, z1[0])
-        add(z1[1][:], 1, P, HALF_V)
-        project(2, HALF_V + P, V, z1[1])
+        project(2, HALF_V + P, V, z1[1], nc.vector.tensor_copy)

@@ -26,6 +26,7 @@ QUADRANT = 32
 ROWS = 4
 PER_COL = 16
 HALF_V = V // 2
+SCALAR_M = 3 * P // 4
 
 
 def tile_picked_dime_none_p_kernel(
@@ -36,8 +37,8 @@ def tile_picked_dime_none_p_kernel(
         keep = ctx.enter_context(tc.tile_pool(name="keep", bufs=1))
         psum = ctx.enter_context(tc.psum_pool(name="psum", bufs=1))
 
-        def sb(name, shape, dtype, tag=""):
-            return keep.tile(shape, dtype, name=name, tag=tag or name, align_bytes=64)
+        def sb(name, shape, dtype):
+            return keep.tile(shape, dtype, name=name, align_bytes=64)
 
         def bank(name, n):
             return psum.tile([P, BANK], F32, name=name, tag="bank%d" % n)
@@ -48,12 +49,21 @@ def tile_picked_dime_none_p_kernel(
         xs = sb("xs", [P, T], U8)
         w1_raw = [sb("w1_raw%d" % g, [P, PACK, H], F32) for g in range(2)]
         w3_raw = sb("w3_raw", [P, PACK, H], F32)
-        stage = sb("stage", [P, 15 * HALF_V], F32)
 
-        def rows(start):
-            return stage[:, start * HALF_V : (start + PACK) * HALF_V].rearrange("p (j c) -> p j c", j=PACK)
+        shared = sb("shared", [P, 32 * P], F32)
 
-        a_raw = {(0, 0): rows(7), (0, 1): rows(3), (1, 0): rows(11), (1, 1): sb("a_raw11", [P, PACK, HALF_V], F32)[:]}
+        def blocks(first, count):
+            return shared[:, first * P : (first + count) * P]
+
+        stage_blocks = PACK * HALF_V // P
+        a_raw = {
+            stage: blocks(first, stage_blocks).rearrange("p (j c) -> p j c", j=PACK)
+            for stage, first in (((0, 0), 14), ((0, 1), 6), ((1, 0), 22))
+        }
+        a_raw[1, 1] = sb("a_raw11", [P, PACK, HALF_V], F32)[:]
+        rounded = sb("rounded", [P, PACK * (HALF_V + P)], BF16)
+        a_bf = rounded[:, 0 : PACK * HALF_V]
+        z0 = rounded[:, PACK * P :]
         w2w = sb("w2w", [P, 2 * N], U8)
         w2s = sb("w2s", [P, N], U8)
         warm = sb("warm", [P, 8], F32)
@@ -99,23 +109,18 @@ def tile_picked_dime_none_p_kernel(
 
         def cast_weight(copy, dst, raw, u, m0=0, m1=P):
             copy(
-                dst[:].rearrange("p (t m j) -> p m j t", t=2, j=PACK)[:, m0:m1],
+                dst[:].rearrange("p (e m j) -> p m j e", e=2, j=PACK)[:, m0:m1],
                 raw[:].rearrange("p j (m t) -> p m j t", t=PACK)[:, m0:m1, :, 2 * u : 2 * u + 2],
             )
 
-        def cast_angles(copy, c, d, tag=""):
-            a_bf = sb("a_bf%d%d" % (c, d), [P, PACK * HALF_V], BF16, tag)
-            copy(
-                a_bf[:].rearrange("p (v e j) -> p v j e", e=2, j=PACK),
-                a_raw[c, d].rearrange("p j (v e) -> p v j e", e=2),
-            )
-            return a_bf
+        def round_on_gpsimd(dst, src):
+            nc.gpsimd.tensor_scalar(dst, src, 1.0, 0.0, MULT, ADD)
 
-        def quantize(name, src, tag=""):
+        def quantize(name, src):
             cols = src.shape[1] // PACK
-            codes = sb(name + "_codes", [P, cols], U32, tag)
+            codes = sb(name + "_codes", [P, cols], U32)
             scales = sb(name + "_scales", [P, cols], U8)
-            nc.vector.quantize_mx(out=codes[:].bitcast(FP8X4), scales=scales[:], in_=src[:])
+            nc.vector.quantize_mx(out=codes[:].bitcast(FP8X4), scales=scales[:], in_=src)
             return codes, scales
 
         h = [sb("h%d" % t, [P, S], F32) for t in range(PACK)]
@@ -137,43 +142,51 @@ def tile_picked_dime_none_p_kernel(
                         stop=(g == 1),
                     )
 
-        def silu(t):
-            for s in range(2):
-                nc.scalar.activation(h[t][:, BANK * s : BANK * (s + 1)], h_ps[t][s][:], SILU)
-
         nc.vector.tensor_copy(gw[0][:], xw[0][:].indirect(offs_t[:]))
         nc.vector.tensor_copy(gs[:], xs[:].indirect(offs_t[:]))
         w1_bf = [[sb("w1_bf%d%d" % (g, u), [P, 2 * H], BF16) for u in range(2)] for g in range(2)]
         cast_weight(nc.scalar.copy, w1_bf[0][0], w1_raw[0], 0)
         cast_weight(nc.scalar.copy, w1_bf[0][1], w1_raw[0], 1, 0, P // 2)
-        nc.gpsimd.tensor_scalar(
-            w1_bf[0][1][:].rearrange("p (t m j) -> p m t j", t=2, j=PACK)[:, P // 2 : P],
-            w1_raw[0][:].rearrange("p j (m t) -> p m t j", t=PACK)[:, P // 2 : P, 2:4],
-            1.0,
-            0.0,
-            MULT,
-            ADD,
+        round_on_gpsimd(
+            w1_bf[0][1][:].rearrange("p (e m j) -> p m e j", e=2, j=PACK)[:, P // 2 : P],
+            w1_raw[0][:].rearrange("p j (m t) -> p m t j", t=PACK)[:, P // 2 : P, 2:PACK],
         )
         for u in range(2):
-            h_pass(quantize("w1q0%d" % u, w1_bf[0][u]), 0, u)
+            h_pass(quantize("w1q0%d" % u, w1_bf[0][u][:]), 0, u)
         nc.vector.tensor_copy(gw[1][:], xw[1][:].indirect(offs_t[:]))
         for u in range(2):
-            cast_weight(nc.scalar.copy, w1_bf[1][u], w1_raw[1], u, 0, 3 * P // 4)
-            cast_weight(nc.vector.tensor_copy, w1_bf[1][u], w1_raw[1], u, 3 * P // 4, P)
+            cast_weight(nc.scalar.copy, w1_bf[1][u], w1_raw[1], u, 0, SCALAR_M)
+            cast_weight(nc.vector.tensor_copy, w1_bf[1][u], w1_raw[1], u, SCALAR_M, P)
         for u in range(2):
-            h_pass(quantize("w1q1%d" % u, w1_bf[1][u]), 1, u)
+            h_pass(quantize("w1q1%d" % u, w1_bf[1][u][:]), 1, u)
         for t in range(PACK):
-            silu(t)
+            for s in range(2):
+                nc.scalar.activation(h[t][:, BANK * s : BANK * (s + 1)], h_ps[t][s][:], SILU)
 
-        def filters(c, d, aq):
-            banks = []
+        pair_blocks = 2 * HALF_V // P
+        picked = {
+            key: blocks(first, pair_blocks)
+            for key, first in (((0, 0, 0), 18), ((0, 1, 1), 8), ((1, 0, 0), 13), ((1, 1, 1), 20))
+        }
+        for key in ((0, 0, 1), (0, 1, 0), (1, 0, 1), (1, 1, 0)):
+            picked[key] = sb("picked%d%d%d" % key, [P, 2 * HALF_V], F32)[:]
+        prod = {(0, 0): blocks(0, stage_blocks), (0, 1): blocks(24, stage_blocks)}
+        for d in range(2):
+            prod[1, d] = sb("prod1%d" % d, [P, PACK * HALF_V], F32)[:]
+        f = {}
+
+        def round_angles(c, d):
+            round_on_gpsimd(a_bf.rearrange("p (v j) -> p v j", j=PACK), a_raw[c, d].rearrange("p j v -> p v j"))
+
+        def filters(c, d):
+            aq = quantize("aq%d%d" % (c, d), a_bf)
             for u in range(2):
-                f_ps = bank("f_ps%d%d%d" % (c, d, u), 4 * c + 2 * d + u)
+                f[c, d, u] = bank("f_ps%d%d%d" % (c, d, u), PACK * c + 2 * d + u)
                 codes, scales = w3q[u]
                 for e in range(2):
                     cols = slice(P * e, P * (e + 1))
                     nc.tensor.matmul_mx(
-                        out=f_ps[:, HALF_V * e : HALF_V * (e + 1)],
+                        out=f[c, d, u][:, HALF_V * e : HALF_V * (e + 1)],
                         lhsT=codes[:, cols].bitcast(FP8X4),
                         lhsT_scale=scales[:, cols],
                         rhs=aq[0][:].bitcast(FP8X4),
@@ -181,49 +194,36 @@ def tile_picked_dime_none_p_kernel(
                         start=True,
                         stop=True,
                     )
-                banks.append(f_ps)
-            return banks
 
-        picked = {
-            (0, 0, 0): stage[:, 9 * HALF_V : 11 * HALF_V],
-            (0, 1, 1): stage[:, 4 * HALF_V : 6 * HALF_V],
-            (1, 0, 0): stage[:, 7 * HALF_V - P : 9 * HALF_V - P],
-        }
-        prod = {(0, d): stage[:, 11 * HALF_V * d : 11 * HALF_V * d + PACK * HALF_V] for d in range(2)}
-        for d in range(2):
-            prod[1, d] = sb("prod1%d" % d, [P, PACK * HALF_V], F32)[:]
-
-        def window(c, d, t, v0, v1):
-            return h[t][:].indirect(pos_t[d][:, (HALF_V * c + v0) // PER_COL : (HALF_V * c + v1) // PER_COL])
-
-        def slot(c, d, t, v0, v1):
-            if (c, d, t // 2) not in picked:
-                picked[c, d, t // 2] = sb("picked%d%d%d" % (c, d, t // 2), [P, 2 * HALF_V], F32)[:]
-            return picked[c, d, t // 2][:, HALF_V * (t % 2) + v0 : HALF_V * (t % 2) + v1]
+        def gather_operands(c, d, t, v0, v1):
+            return (
+                picked[c, d, t // 2][:, HALF_V * (t % 2) + v0 : HALF_V * (t % 2) + v1],
+                h[t][:].indirect(pos_t[d][:, (HALF_V * c + v0) // PER_COL : (HALF_V * c + v1) // PER_COL]),
+            )
 
         def gather_vector(c, d, t, v0=0, v1=HALF_V):
-            nc.vector.tensor_copy(slot(c, d, t, v0, v1), window(c, d, t, v0, v1))
+            nc.vector.tensor_copy(*gather_operands(c, d, t, v0, v1))
 
         def gather_scalar(c, d, t, v0=0, v1=HALF_V):
-            nc.scalar.activation(slot(c, d, t, v0, v1), window(c, d, t, v0, v1), COPY)
+            nc.scalar.activation(*gather_operands(c, d, t, v0, v1), COPY)
 
-        def product(c, d, u, f_ps, v0=0, v1=HALF_V, e0=0, e1=2):
+        def product(c, d, u, v0=0, v1=HALF_V):
             nc.vector.tensor_tensor(
-                prod[c, d].rearrange("p (t v) -> p t v", t=PACK)[:, 2 * u + e0 : 2 * u + e1, v0:v1],
-                picked[c, d, u].rearrange("p (e v) -> p e v", e=2)[:, e0:e1, v0:v1],
-                f_ps[u][:].rearrange("p (e v) -> p e v", e=2)[:, e0:e1, v0:v1],
+                prod[c, d].rearrange("p (u v e) -> p u v e", u=2, e=2)[:, u, v0:v1],
+                picked[c, d, u].rearrange("p (e v) -> p v e", e=2)[:, v0:v1],
+                f[c, d, u][:].rearrange("p (e v) -> p v e", e=2)[:, v0:v1],
                 MULT,
             )
 
-        def add(z_bf, c, v0, v1):
-            nc.vector.tensor_tensor(
-                z_bf.rearrange("p (v e t) -> p v t e", e=2, t=PACK),
-                prod[c, 0].rearrange("p (t v e) -> p v t e", e=2, t=PACK)[:, v0 // 2 : v1 // 2],
-                prod[c, 1].rearrange("p (t v e) -> p v t e", e=2, t=PACK)[:, v0 // 2 : v1 // 2],
+        def add(engine, z_bf, c, b):
+            engine.tensor_tensor(
+                z_bf.rearrange("p (v u e) -> p v u e", u=2, e=2),
+                prod[c, 0].rearrange("p (u v e) -> p v u e", u=2, e=2)[:, P * b : P * (b + 1)],
+                prod[c, 1].rearrange("p (u v e) -> p v u e", u=2, e=2)[:, P * b : P * (b + 1)],
                 ADD,
             )
 
-        def project(n, v0, v1, z_bf, copy=nc.scalar.copy):
+        def project(n, v0, v1, z_bf, copy):
             codes, scales = quantize("zq%d" % n, z_bf)
             o_ps = bank("o_ps%d" % n, n)
             nc.tensor.matmul_mx(
@@ -239,63 +239,54 @@ def tile_picked_dime_none_p_kernel(
             copy(o_sb[:], o_ps[:, 0 : v1 - v0])
             nc.sync.dma_start(out=out[:, v0:v1], in_=o_sb[:])
 
-        def cast_on_gpsimd(c, d):
-            a_bf = sb("a_bf%d%d" % (c, d), [P, PACK * HALF_V], BF16, "a_bf00")
-            nc.gpsimd.tensor_scalar(
-                a_bf[:].rearrange("p (v j) -> p v j", j=PACK),
-                a_raw[c, d].rearrange("p j v -> p v j"),
-                1.0,
-                0.0,
-                MULT,
-                ADD,
-            )
-            return a_bf
-
-        f = {}
         w3_bf = [sb("w3_bf%d" % u, [P, 2 * H], BF16) for u in range(2)]
         for u in range(2):
             cast_weight(nc.vector.tensor_copy, w3_bf[u], w3_raw, u)
-        w3q = [quantize("w3q0", w3_bf[0])]
-        a_bf = cast_angles(nc.vector.tensor_copy, 0, 0)
-        w3q.append(quantize("w3q1", w3_bf[1]))
-        f[0, 0] = filters(0, 0, quantize("aq00", a_bf))
-        a_bf = cast_on_gpsimd(0, 1)
+        w3q = [quantize("w3q0", w3_bf[0][:])]
+        nc.vector.tensor_copy(
+            a_bf.rearrange("p (v e j) -> p v j e", e=2, j=PACK),
+            a_raw[0, 0].rearrange("p j (v e) -> p v j e", e=2),
+        )
+        w3q.append(quantize("w3q1", w3_bf[1][:]))
+        filters(0, 0)
+
+        round_angles(0, 1)
         for d, t in ((0, 2), (0, 3), (1, 0), (1, 1)):
             gather_scalar(0, d, t)
         for t in range(1, PACK):
             gather_scalar(1, 0, t)
         for t in range(2):
-            gather_scalar(1, 1, t)
-        for b in range(2):
-            for t in range(2, PACK):
-                gather_scalar(1, 1, t, P * b, P * (b + 1))
-
-        for t in range(2):
             gather_vector(0, 0, t)
         gather_vector(1, 0, 0, P, HALF_V)
-        product(0, 0, 0, f[0, 0])
-        f[0, 1] = filters(0, 1, quantize("aq01", a_bf))
-        a_bf = cast_on_gpsimd(1, 0)
+        product(0, 0, 0)
+        filters(0, 1)
+
+        round_angles(1, 0)
         for t in range(2, PACK):
             gather_vector(0, 1, t)
-        product(0, 0, 1, f[0, 0])
+        product(0, 0, 1)
         gather_vector(1, 0, 0, 0, P)
-        f[1, 0] = filters(1, 0, quantize("aq10", a_bf))
-        a_bf = cast_on_gpsimd(1, 1)
+        filters(1, 0)
+
+        round_angles(1, 1)
         for u in (1, 0):
-            product(0, 1, u, f[0, 1])
-        product(1, 0, 0, f[1, 0])
-        product(1, 0, 1, f[1, 0], e1=1)
-        f[1, 1] = filters(1, 1, quantize("aq11", a_bf))
-        z0 = sb("z0", [P, PACK * HALF_V], BF16, "a_raw11")
-        add(z0[:], 0, 0, HALF_V)
-        product(1, 0, 1, f[1, 0], e0=1)
-        product(1, 1, 0, f[1, 1])
-        project(0, 0, HALF_V, z0)
-        product(1, 1, 1, f[1, 1], 0, P)
-        z1 = [sb("z1_%d" % b, [P, PACK * P], BF16) for b in range(2)]
-        product(1, 1, 1, f[1, 1], P, HALF_V)
+            product(0, 1, u)
+        product(1, 0, 0)
+        gather_vector(1, 1, PACK - 1, 0, P)
+        for t in range(PACK - 1):
+            gather_scalar(1, 1, t)
+        gather_scalar(1, 1, PACK - 1, P, HALF_V)
+        filters(1, 1)
+
+        add(nc.vector, z0[:, PACK * P :], 0, 1)
+        add(nc.gpsimd, z0[:, 0 : PACK * P], 0, 0)
+        product(1, 0, 1)
+        product(1, 1, 0)
         for b in range(2):
-            add(z1[b][:], 1, P * b, P * (b + 1))
-        project(1, HALF_V, HALF_V + P, z1[0])
-        project(2, HALF_V + P, V, z1[1], nc.vector.tensor_copy)
+            product(1, 1, 1, P * b, P * (b + 1))
+        project(0, 0, HALF_V, z0, nc.scalar.copy)
+        z1 = [sb("z1_%d" % b, [P, PACK * P], BF16)[:] for b in range(2)]
+        for b in range(2):
+            add(nc.vector, z1[b], 1, b)
+        for b, copy in enumerate((nc.scalar.copy, nc.vector.tensor_copy)):
+            project(1 + b, HALF_V + P * b, HALF_V + P * (b + 1), z1[b], copy)

@@ -26,7 +26,7 @@ QUADRANT = 32
 ROWS = 4
 PER_COL = 16
 HALF_V = V // 2
-SCALAR_M = 3 * P // 4
+SCALAR_M = (5 * P // 8, 3 * P // 4)
 
 
 def tile_picked_dime_none_p_kernel(
@@ -116,9 +116,9 @@ def tile_picked_dime_none_p_kernel(
         def round_on_gpsimd(dst, src):
             nc.gpsimd.tensor_scalar(dst, src, 1.0, 0.0, MULT, ADD)
 
-        def quantize(name, src):
+        def quantize(name, src, tag=None):
             cols = src.shape[1] // PACK
-            codes = sb(name + "_codes", [P, cols], U32)
+            codes = keep.tile([P, cols], U32, name=name + "_codes", tag=tag or name + "_codes", align_bytes=64)
             scales = sb(name + "_scales", [P, cols], U8)
             nc.vector.quantize_mx(out=codes[:].bitcast(FP8X4), scales=scales[:], in_=src)
             return codes, scales
@@ -128,18 +128,19 @@ def tile_picked_dime_none_p_kernel(
         gw = [sb("gw%d" % g, [P, S], U32) for g in range(2)]
         gs = sb("gs", [P, S], U8)
 
-        def h_pass(wq, g, u):
-            for e in range(2):
+        def h_pass(wq, g, t0):
+            for e in range(wq[0].shape[1] // P):
+                first = int(t0 + e == PACK - 1)
                 for s in range(2):
                     cols = slice(BANK * s, BANK * (s + 1))
                     nc.tensor.matmul_mx(
-                        out=h_ps[2 * u + e][s][:],
+                        out=h_ps[t0 + e][s][:],
                         lhsT=wq[0][:, P * e : P * (e + 1)].bitcast(FP8X4),
                         lhsT_scale=wq[1][:, P * e : P * (e + 1)],
                         rhs=gw[g][:, cols].bitcast(FP8X4),
                         rhs_scale=gs[ROWS * g : P, cols],
-                        start=(g == 0),
-                        stop=(g == 1),
+                        start=(g == first),
+                        stop=(g != first),
                     )
 
         nc.vector.tensor_copy(gw[0][:], xw[0][:].indirect(offs_t[:]))
@@ -151,14 +152,16 @@ def tile_picked_dime_none_p_kernel(
             w1_bf[0][1][:].rearrange("p (e m j) -> p m e j", e=2, j=PACK)[:, P // 2 : P],
             w1_raw[0][:].rearrange("p j (m t) -> p m t j", t=PACK)[:, P // 2 : P, 2:PACK],
         )
-        for u in range(2):
-            h_pass(quantize("w1q0%d" % u, w1_bf[0][u][:]), 0, u)
+        h_pass(quantize("w1q00", w1_bf[0][0][:]), 0, 0)
+        h_pass(quantize("w1q02", w1_bf[0][1][:, 0:H]), 0, 2)
         nc.vector.tensor_copy(gw[1][:], xw[1][:].indirect(offs_t[:]))
         for u in range(2):
-            cast_weight(nc.scalar.copy, w1_bf[1][u], w1_raw[1], u, 0, SCALAR_M)
-            cast_weight(nc.vector.tensor_copy, w1_bf[1][u], w1_raw[1], u, SCALAR_M, P)
-        for u in range(2):
-            h_pass(quantize("w1q1%d" % u, w1_bf[1][u][:]), 1, u)
+            cast_weight(nc.scalar.copy, w1_bf[1][u], w1_raw[1], u, 0, SCALAR_M[u])
+            cast_weight(nc.vector.tensor_copy, w1_bf[1][u], w1_raw[1], u, SCALAR_M[u], P)
+        h_pass(quantize("w1q10", w1_bf[1][0][:]), 1, 0)
+        last = quantize("w1q03", w1_bf[0][1][:, H:], "w1_bf10")
+        h_pass(quantize("w1q11", w1_bf[1][1][:]), 1, 2)
+        h_pass(last, 0, PACK - 1)
         for t in range(PACK):
             for s in range(2):
                 nc.scalar.activation(h[t][:, BANK * s : BANK * (s + 1)], h_ps[t][s][:], SILU)

@@ -26,7 +26,7 @@ QUADRANT = 32
 ROWS = 4
 PER_COL = 16
 HALF_V = V // 2
-SCALAR_M = (5 * P // 8, 3 * P // 4)
+SCALAR_M = (3 * P // 8, 7 * P // 8)
 
 
 def tile_picked_dime_none_p_kernel(
@@ -37,8 +37,8 @@ def tile_picked_dime_none_p_kernel(
         keep = ctx.enter_context(tc.tile_pool(name="keep", bufs=1))
         psum = ctx.enter_context(tc.psum_pool(name="psum", bufs=1))
 
-        def sb(name, shape, dtype):
-            return keep.tile(shape, dtype, name=name, align_bytes=64)
+        def sb(name, shape, dtype, tag=None):
+            return keep.tile(shape, dtype, name=name, tag=tag or name, align_bytes=256)
 
         def bank(name, n):
             return psum.tile([P, BANK], F32, name=name, tag="bank%d" % n)
@@ -47,10 +47,45 @@ def tile_picked_dime_none_p_kernel(
         pos_t = [keep.tile([P, V // PER_COL], U16, name="pos%d_t" % d) for d in range(2)]
         xw = [sb("xw%d" % g, [P, T], U32) for g in range(2)]
         xs = sb("xs", [P, T], U8)
-        w1_raw = [sb("w1_raw%d" % g, [P, PACK, H], F32) for g in range(2)]
-        w3_raw = sb("w3_raw", [P, PACK, H], F32)
+        gs_rows = sb("gs_rows", [P, S], U8)
+        gs = sb("gs", [P, S], U8)
+        gw = [sb("gw%d" % g, [P, S], U32) for g in range(2)]
+        w1_raw = [sb("w1_raw0", [P, PACK, H], F32)[:]]
+        warm = sb("warm", [P, 8], F32)
+        warm_out = sb("warm_out", [P, 8], F32)
 
-        shared = sb("shared", [P, 32 * P], F32)
+        nc.vector.memset(xs[QUADRANT : 2 * QUADRANT, :].bitcast(I32), 0)
+        nc.gpsimd.memset(warm[:], 0.0)
+        nc.gpsimd.memset(xs[2 * QUADRANT : P, :].bitcast(I32), 0)
+        nc.vector.memset(gs[:].bitcast(I32), 0)
+        nc.scalar.activation(warm_out[:], warm[:], SILU)
+
+        def load_words(g):
+            nc.sync.dma_start(out=xw[g][:].bitcast(I32), in_=x_words[g].rearrange("p n t -> p (n t)").bitcast(I32))
+
+        def load_rows(raw, rows):
+            nc.sync.dma_start(out=raw, in_=rows.rearrange("(p j) c -> p j c", j=PACK))
+
+        nc.sync.dma_start(offs_t[:], offs)
+        for g in range(2):
+            nc.sync.dma_start(
+                out=xs[16 * g : 16 * (g + 1), :].bitcast(I32),
+                in_=x_scales[g].rearrange("(q r) c -> r q c", r=ROWS).bitcast(I32),
+            )
+        load_words(0)
+        nc.sync.dma_start(pos_t[0][:], pos1)
+        nc.sync.dma_start(pos_t[1][:], pos2)
+        load_rows(w1_raw[0], w1[0:K_PASS, :])
+        load_words(1)
+        nc.vector.tensor_copy(gs_rows[:], xs[:].indirect(offs_t[:]))
+        for q in range(P // QUADRANT):
+            nc.sync.dma_start(
+                out=gs[QUADRANT * q : QUADRANT * q + 2 * ROWS, :].bitcast(I32),
+                in_=gs_rows[q:QUADRANT:ROWS, :].bitcast(I32),
+            )
+
+        nc.vector.tensor_copy(gw[0][:], xw[0][:].indirect(offs_t[:]))
+        shared = sb("shared", [P, 56 * P], F32, "xw0")
 
         def blocks(first, count):
             return shared[:, first * P : (first + count) * P]
@@ -60,47 +95,24 @@ def tile_picked_dime_none_p_kernel(
             stage: blocks(first, stage_blocks).rearrange("p (j c) -> p j c", j=PACK)
             for stage, first in (((0, 0), 14), ((0, 1), 6), ((1, 0), 22))
         }
-        a_raw[1, 1] = sb("a_raw11", [P, PACK, HALF_V], F32)[:]
+        a_raw[1, 1] = blocks(32, stage_blocks).rearrange("p (j c) -> p j c", j=PACK)
+        w1_raw.append(sb("w1_raw1", [P, PACK, H], F32, "xs")[:])
+        w3_raw = blocks(40, 16).rearrange("p (j c) -> p j c", j=PACK)
         rounded = sb("rounded", [P, PACK * (HALF_V + P)], BF16)
         a_bf = rounded[:, 0 : PACK * HALF_V]
         z0 = rounded[:, PACK * P :]
-        w2w = sb("w2w", [P, 2 * N], U8)
-        w2s = sb("w2s", [P, N], U8)
-        warm = sb("warm", [P, 8], F32)
-        warm_out = sb("warm_out", [P, 8], F32)
-
-        nc.vector.memset(xs[:].bitcast(I32), 0)
-        nc.gpsimd.memset(warm[:], 0.0)
+        w2s = sb("w2s", [P, N], U8, "gs_rows")
         nc.gpsimd.memset(w2s[:].bitcast(I32), 0)
-        nc.scalar.activation(warm_out[:], warm[:], SILU)
-
-        def load_words(g):
-            nc.sync.dma_start(out=xw[g][:].bitcast(I32), in_=x_words[g].rearrange("p n t -> p (n t)").bitcast(I32))
-
-        def load_rows(raw, rows):
-            nc.sync.dma_start(out=raw, in_=rows.rearrange("(p j) c -> p j c", j=PACK))
 
         def load_angles(c, d):
             load_rows(a_raw[c, d], aT[:, V * d + HALF_V * c : V * d + HALF_V * (c + 1)])
 
-        load_words(0)
-        nc.sync.dma_start(offs_t[:], offs)
-        for q in range(P // QUADRANT):
-            nc.sync.dma_start(
-                out=xs[QUADRANT * q : QUADRANT * q + 2 * ROWS, :].bitcast(I32),
-                in_=x_scales[:, ROWS * q : ROWS * (q + 1), :].bitcast(I32),
-            )
-        load_rows(w1_raw[0][:], w1[0:K_PASS, :])
-        load_words(1)
-        load_rows(w1_raw[1][:], w1[K_PASS:K, :])
-        load_rows(w3_raw[:], w3)
+        load_rows(w1_raw[1], w1[K_PASS:K, :])
+        load_rows(w3_raw, w3)
         load_angles(0, 0)
-        nc.sync.dma_start(pos_t[0][:], pos1)
         load_angles(0, 1)
-        nc.sync.dma_start(pos_t[1][:], pos2)
         load_angles(1, 0)
         load_angles(1, 1)
-        nc.sync.dma_start(out=w2w[:].bitcast(I32), in_=w2_words[0].bitcast(I32))
         for q in range(P // QUADRANT):
             nc.sync.dma_start(
                 out=w2s[QUADRANT * q : QUADRANT * q + ROWS, :].bitcast(I32),
@@ -110,7 +122,7 @@ def tile_picked_dime_none_p_kernel(
         def cast_weight(copy, dst, raw, u, m0=0, m1=P):
             copy(
                 dst[:].rearrange("p (e m j) -> p m j e", e=2, j=PACK)[:, m0:m1],
-                raw[:].rearrange("p j (m t) -> p m j t", t=PACK)[:, m0:m1, :, 2 * u : 2 * u + 2],
+                raw.rearrange("p j (m t) -> p m j t", t=PACK)[:, m0:m1, :, 2 * u : 2 * u + 2],
             )
 
         def round_on_gpsimd(dst, src):
@@ -118,15 +130,13 @@ def tile_picked_dime_none_p_kernel(
 
         def quantize(name, src, tag=None):
             cols = src.shape[1] // PACK
-            codes = keep.tile([P, cols], U32, name=name + "_codes", tag=tag or name + "_codes", align_bytes=64)
+            codes = keep.tile([P, cols], U32, name=name + "_codes", tag=tag or name + "_codes", align_bytes=256)
             scales = sb(name + "_scales", [P, cols], U8)
             nc.vector.quantize_mx(out=codes[:].bitcast(FP8X4), scales=scales[:], in_=src)
             return codes, scales
 
         h = [sb("h%d" % t, [P, S], F32) for t in range(PACK)]
         h_ps = [[bank("h_ps%d_%d" % (t, s), 2 * t + s) for s in range(2)] for t in range(PACK)]
-        gw = [sb("gw%d" % g, [P, S], U32) for g in range(2)]
-        gs = sb("gs", [P, S], U8)
 
         def h_pass(wq, g, t0):
             for e in range(wq[0].shape[1] // P):
@@ -143,17 +153,14 @@ def tile_picked_dime_none_p_kernel(
                         stop=(g != first),
                     )
 
-        nc.vector.tensor_copy(gw[0][:], xw[0][:].indirect(offs_t[:]))
-        nc.vector.tensor_copy(gs[:], xs[:].indirect(offs_t[:]))
         w1_bf = [[sb("w1_bf%d%d" % (g, u), [P, 2 * H], BF16) for u in range(2)] for g in range(2)]
-        cast_weight(nc.scalar.copy, w1_bf[0][0], w1_raw[0], 0)
-        cast_weight(nc.scalar.copy, w1_bf[0][1], w1_raw[0], 1, 0, P // 2)
-        round_on_gpsimd(
-            w1_bf[0][1][:].rearrange("p (e m j) -> p m e j", e=2, j=PACK)[:, P // 2 : P],
-            w1_raw[0][:].rearrange("p j (m t) -> p m t j", t=PACK)[:, P // 2 : P, 2:PACK],
-        )
+        cast_weight(nc.vector.tensor_copy, w1_bf[0][0], w1_raw[0], 0)
+        cast_weight(nc.scalar.copy, w1_bf[0][1], w1_raw[0], 1, 0, 5 * P // 8)
+        cast_weight(nc.vector.tensor_copy, w1_bf[0][1], w1_raw[0], 1, 5 * P // 8, P)
         h_pass(quantize("w1q00", w1_bf[0][0][:]), 0, 0)
         h_pass(quantize("w1q02", w1_bf[0][1][:, 0:H]), 0, 2)
+        w2w = sb("w2w", [P, 2 * N], U8, "w1_raw0")
+        nc.sync.dma_start(out=w2w[:].bitcast(I32), in_=w2_words[0].bitcast(I32))
         nc.vector.tensor_copy(gw[1][:], xw[1][:].indirect(offs_t[:]))
         for u in range(2):
             cast_weight(nc.scalar.copy, w1_bf[1][u], w1_raw[1], u, 0, SCALAR_M[u])

@@ -79,13 +79,13 @@ def tile_picked_dime_none_p_kernel(
         load_words(1)
         nc.vector.tensor_copy(gs_rows[:], xs[:].indirect(offs_t[:]))
         for q in range(P // QUADRANT):
-            nc.sync.dma_start(
+            nc.scalar.dma_start(
                 out=gs[QUADRANT * q : QUADRANT * q + 2 * ROWS, :].bitcast(I32),
                 in_=gs_rows[q:QUADRANT:ROWS, :].bitcast(I32),
             )
 
         nc.vector.tensor_copy(gw[0][:], xw[0][:].indirect(offs_t[:]))
-        shared = sb("shared", [P, 56 * P], F32, "xw0")
+        shared = sb("shared", [P, 72 * P], F32, "xw0")
 
         def blocks(first, count):
             return shared[:, first * P : (first + count) * P]
@@ -96,7 +96,7 @@ def tile_picked_dime_none_p_kernel(
             for stage, first in (((0, 0), 14), ((0, 1), 6), ((1, 0), 22))
         }
         a_raw[1, 1] = blocks(32, stage_blocks).rearrange("p (j c) -> p j c", j=PACK)
-        w1_raw.append(sb("w1_raw1", [P, PACK, H], F32, "xs")[:])
+        w1_raw.append(blocks(56, 16).rearrange("p (j c) -> p j c", j=PACK))
         w3_raw = blocks(40, 16).rearrange("p (j c) -> p j c", j=PACK)
         rounded = sb("rounded", [P, PACK * (HALF_V + P)], BF16)
         a_bf = rounded[:, 0 : PACK * HALF_V]
@@ -108,7 +108,8 @@ def tile_picked_dime_none_p_kernel(
             load_rows(a_raw[c, d], aT[:, V * d + HALF_V * c : V * d + HALF_V * (c + 1)])
 
         load_rows(w1_raw[1], w1[K_PASS:K, :])
-        load_rows(w3_raw, w3)
+        for j in (0, 2):
+            nc.sync.dma_start(out=w3_raw[:, j : j + 2], in_=w3.rearrange("(p j) c -> p j c", j=PACK)[:, j : j + 2])
         load_angles(0, 0)
         load_angles(0, 1)
         load_angles(1, 0)
@@ -119,10 +120,10 @@ def tile_picked_dime_none_p_kernel(
                 in_=w2_scales[0, ROWS * q : ROWS * (q + 1), :].bitcast(I32),
             )
 
-        def cast_weight(copy, dst, raw, u, m0=0, m1=P):
+        def cast_weight(copy, dst, raw, u, m0=0, m1=P, j0=0, j1=PACK):
             copy(
-                dst[:].rearrange("p (e m j) -> p m j e", e=2, j=PACK)[:, m0:m1],
-                raw.rearrange("p j (m t) -> p m j t", t=PACK)[:, m0:m1, :, 2 * u : 2 * u + 2],
+                dst[:].rearrange("p (e m j) -> p m j e", e=2, j=PACK)[:, m0:m1, j0:j1],
+                raw.rearrange("p j (m t) -> p m j t", t=PACK)[:, m0:m1, j0:j1, 2 * u : 2 * u + 2],
             )
 
         def round_on_gpsimd(dst, src):
@@ -158,17 +159,18 @@ def tile_picked_dime_none_p_kernel(
         cast_weight(nc.scalar.copy, w1_bf[0][1], w1_raw[0], 1, 0, 5 * P // 8)
         cast_weight(nc.vector.tensor_copy, w1_bf[0][1], w1_raw[0], 1, 5 * P // 8, P)
         h_pass(quantize("w1q00", w1_bf[0][0][:]), 0, 0)
-        h_pass(quantize("w1q02", w1_bf[0][1][:, 0:H]), 0, 2)
+        w1q01 = quantize("w1q01", w1_bf[0][1][:])
+        h_pass((w1q01[0][:, 0:P], w1q01[1][:, 0:P]), 0, 2)
         w2w = sb("w2w", [P, 2 * N], U8, "w1_raw0")
         nc.sync.dma_start(out=w2w[:].bitcast(I32), in_=w2_words[0].bitcast(I32))
         nc.vector.tensor_copy(gw[1][:], xw[1][:].indirect(offs_t[:]))
         for u in range(2):
             cast_weight(nc.scalar.copy, w1_bf[1][u], w1_raw[1], u, 0, SCALAR_M[u])
             cast_weight(nc.vector.tensor_copy, w1_bf[1][u], w1_raw[1], u, SCALAR_M[u], P)
-        h_pass(quantize("w1q10", w1_bf[1][0][:]), 1, 0)
-        last = quantize("w1q03", w1_bf[0][1][:, H:], "w1_bf10")
-        h_pass(quantize("w1q11", w1_bf[1][1][:]), 1, 2)
-        h_pass(last, 0, PACK - 1)
+        for t in range(2):
+            h_pass(quantize("w1q1%d" % t, w1_bf[1][0][:, H * t : H * (t + 1)]), 1, t)
+        h_pass(quantize("w1q12", w1_bf[1][1][:]), 1, 2)
+        h_pass((w1q01[0][:, P:], w1q01[1][:, P:]), 0, PACK - 1)
         for t in range(PACK):
             for s in range(2):
                 nc.scalar.activation(h[t][:, BANK * s : BANK * (s + 1)], h_ps[t][s][:], SILU)
@@ -250,8 +252,9 @@ def tile_picked_dime_none_p_kernel(
             nc.sync.dma_start(out=out[:, v0:v1], in_=o_sb[:])
 
         w3_bf = [sb("w3_bf%d" % u, [P, 2 * H], BF16) for u in range(2)]
-        for u in range(2):
-            cast_weight(nc.vector.tensor_copy, w3_bf[u], w3_raw, u)
+        for j in (0, 2):
+            for u in range(2):
+                cast_weight(nc.vector.tensor_copy, w3_bf[u], w3_raw, u, 0, P, j, j + 2)
         w3q = [quantize("w3q0", w3_bf[0][:])]
         nc.vector.tensor_copy(
             a_bf.rearrange("p (v e j) -> p v j e", e=2, j=PACK),

@@ -79,13 +79,13 @@ def tile_picked_dime_none_p_kernel(
         load_words(1)
         nc.vector.tensor_copy(gs_rows[:], xs[:].indirect(offs_t[:]))
         for q in range(P // QUADRANT):
-            nc.scalar.dma_start(
+            nc.sync.dma_start(
                 out=gs[QUADRANT * q : QUADRANT * q + 2 * ROWS, :].bitcast(I32),
                 in_=gs_rows[q:QUADRANT:ROWS, :].bitcast(I32),
             )
 
         nc.vector.tensor_copy(gw[0][:], xw[0][:].indirect(offs_t[:]))
-        shared = sb("shared", [P, 72 * P], F32, "xw0")
+        shared = sb("shared", [P, 56 * P], F32, "xw0")
 
         def blocks(first, count):
             return shared[:, first * P : (first + count) * P]
@@ -96,7 +96,7 @@ def tile_picked_dime_none_p_kernel(
             for stage, first in (((0, 0), 14), ((0, 1), 6), ((1, 0), 22))
         }
         a_raw[1, 1] = blocks(32, stage_blocks).rearrange("p (j c) -> p j c", j=PACK)
-        w1_raw.append(blocks(56, 16).rearrange("p (j c) -> p j c", j=PACK))
+        w1_raw.append(sb("w1_raw1", [P, PACK, H], F32, "xs")[:])
         w3_raw = blocks(40, 16).rearrange("p (j c) -> p j c", j=PACK)
         rounded = sb("rounded", [P, PACK * (HALF_V + P)], BF16)
         a_bf = rounded[:, 0 : PACK * HALF_V]

@@ -108,8 +108,7 @@ def tile_picked_dime_none_p_kernel(
             load_rows(a_raw[c, d], aT[:, V * d + HALF_V * c : V * d + HALF_V * (c + 1)])
 
         load_rows(w1_raw[1], w1[K_PASS:K, :])
-        for j in (0, 2):
-            nc.sync.dma_start(out=w3_raw[:, j : j + 2], in_=w3.rearrange("(p j) c -> p j c", j=PACK)[:, j : j + 2])
+        load_rows(w3_raw, w3)
         load_angles(0, 0)
         load_angles(0, 1)
         load_angles(1, 0)
@@ -120,10 +119,10 @@ def tile_picked_dime_none_p_kernel(
                 in_=w2_scales[0, ROWS * q : ROWS * (q + 1), :].bitcast(I32),
             )
 
-        def cast_weight(copy, dst, raw, u, m0=0, m1=P, j0=0, j1=PACK):
+        def cast_weight(copy, dst, raw, u, m0=0, m1=P):
             copy(
-                dst[:].rearrange("p (e m j) -> p m j e", e=2, j=PACK)[:, m0:m1, j0:j1],
-                raw.rearrange("p j (m t) -> p m j t", t=PACK)[:, m0:m1, j0:j1, 2 * u : 2 * u + 2],
+                dst[:].rearrange("p (e m j) -> p m j e", e=2, j=PACK)[:, m0:m1],
+                raw.rearrange("p j (m t) -> p m j t", t=PACK)[:, m0:m1, :, 2 * u : 2 * u + 2],
             )
 
         def round_on_gpsimd(dst, src):
@@ -178,7 +177,7 @@ def tile_picked_dime_none_p_kernel(
         pair_blocks = 2 * HALF_V // P
         picked = {
             key: blocks(first, pair_blocks)
-            for key, first in (((0, 0, 0), 18), ((0, 1, 1), 8), ((1, 0, 0), 13), ((1, 1, 1), 20))
+            for key, first in (((0, 0, 0), 18), ((0, 1, 1), 8), ((1, 0, 0), 14), ((1, 1, 1), 20))
         }
         for key in ((0, 0, 1), (0, 1, 0), (1, 0, 1), (1, 1, 0)):
             picked[key] = sb("picked%d%d%d" % key, [P, 2 * HALF_V], F32)[:]
@@ -252,9 +251,8 @@ def tile_picked_dime_none_p_kernel(
             nc.sync.dma_start(out=out[:, v0:v1], in_=o_sb[:])
 
         w3_bf = [sb("w3_bf%d" % u, [P, 2 * H], BF16) for u in range(2)]
-        for j in (0, 2):
-            for u in range(2):
-                cast_weight(nc.vector.tensor_copy, w3_bf[u], w3_raw, u, 0, P, j, j + 2)
+        for u in range(2):
+            cast_weight(nc.vector.tensor_copy, w3_bf[u], w3_raw, u)
         w3q = [quantize("w3q0", w3_bf[0][:])]
         nc.vector.tensor_copy(
             a_bf.rearrange("p (v e j) -> p v j e", e=2, j=PACK),
@@ -266,6 +264,7 @@ def tile_picked_dime_none_p_kernel(
         round_angles(0, 1)
         for d, t in ((0, 2), (0, 3), (1, 0), (1, 1)):
             gather_scalar(0, d, t)
+        gather_scalar(1, 0, 0, 0, P)
         for t in range(1, PACK):
             gather_scalar(1, 0, t)
         for t in range(2):
@@ -278,7 +277,6 @@ def tile_picked_dime_none_p_kernel(
         for t in range(2, PACK):
             gather_vector(0, 1, t)
         product(0, 0, 1)
-        gather_vector(1, 0, 0, 0, P)
         filters(1, 0)
 
         round_angles(1, 1)

@@ -154,9 +154,12 @@ def tile_picked_dime_none_p_kernel(
                     )
 
         w1_bf = [[sb("w1_bf%d%d" % (g, u), [P, 2 * H], BF16) for u in range(2)] for g in range(2)]
-        cast_weight(nc.vector.tensor_copy, w1_bf[0][0], w1_raw[0], 0)
-        cast_weight(nc.scalar.copy, w1_bf[0][1], w1_raw[0], 1, 0, 5 * P // 8)
-        cast_weight(nc.vector.tensor_copy, w1_bf[0][1], w1_raw[0], 1, 5 * P // 8, P)
+        cast_weight(nc.scalar.copy, w1_bf[0][0], w1_raw[0], 0)
+        cast_weight(nc.scalar.copy, w1_bf[0][1], w1_raw[0], 1, 0, P // 2)
+        round_on_gpsimd(
+            w1_bf[0][1][:].rearrange("p (e m j) -> p m e j", e=2, j=PACK)[:, P // 2 : P],
+            w1_raw[0].rearrange("p j (m t) -> p m t j", t=PACK)[:, P // 2 : P, 2:PACK],
+        )
         h_pass(quantize("w1q00", w1_bf[0][0][:]), 0, 0)
         w1q01 = quantize("w1q01", w1_bf[0][1][:])
         h_pass((w1q01[0][:, 0:P], w1q01[1][:, 0:P]), 0, 2)

@@ -26,6 +26,7 @@ QUADRANT = 32
 ROWS = 4
 PER_COL = 16
 HALF_V = V // 2
+GPSIMD_V = 5 * HALF_V // 8
 SCALAR_M = (3 * P // 8, 7 * P // 8)
 
 
@@ -180,7 +181,7 @@ def tile_picked_dime_none_p_kernel(
         pair_blocks = 2 * HALF_V // P
         picked = {
             key: blocks(first, pair_blocks)
-            for key, first in (((0, 0, 0), 18), ((0, 1, 1), 8), ((1, 0, 0), 14), ((1, 1, 1), 20))
+            for key, first in (((0, 0, 0), 18), ((0, 1, 1), 8), ((1, 0, 0), 13), ((1, 1, 1), 20))
         }
         for key in ((0, 0, 1), (0, 1, 0), (1, 0, 1), (1, 1, 0)):
             picked[key] = sb("picked%d%d%d" % key, [P, 2 * HALF_V], F32)[:]
@@ -229,11 +230,11 @@ def tile_picked_dime_none_p_kernel(
                 MULT,
             )
 
-        def add(engine, z_bf, c, b):
+        def add(engine, z_bf, c, v0, v1):
             engine.tensor_tensor(
                 z_bf.rearrange("p (v u e) -> p v u e", u=2, e=2),
-                prod[c, 0].rearrange("p (u v e) -> p v u e", u=2, e=2)[:, P * b : P * (b + 1)],
-                prod[c, 1].rearrange("p (u v e) -> p v u e", u=2, e=2)[:, P * b : P * (b + 1)],
+                prod[c, 0].rearrange("p (u v e) -> p v u e", u=2, e=2)[:, v0:v1],
+                prod[c, 1].rearrange("p (u v e) -> p v u e", u=2, e=2)[:, v0:v1],
                 ADD,
             )
 
@@ -267,7 +268,6 @@ def tile_picked_dime_none_p_kernel(
         round_angles(0, 1)
         for d, t in ((0, 2), (0, 3), (1, 0), (1, 1)):
             gather_scalar(0, d, t)
-        gather_scalar(1, 0, 0, 0, P)
         for t in range(1, PACK):
             gather_scalar(1, 0, t)
         for t in range(2):
@@ -280,6 +280,7 @@ def tile_picked_dime_none_p_kernel(
         for t in range(2, PACK):
             gather_vector(0, 1, t)
         product(0, 0, 1)
+        gather_vector(1, 0, 0, 0, P)
         filters(1, 0)
 
         round_angles(1, 1)
@@ -292,8 +293,8 @@ def tile_picked_dime_none_p_kernel(
         gather_scalar(1, 1, PACK - 1, P, HALF_V)
         filters(1, 1)
 
-        add(nc.vector, z0[:, PACK * P :], 0, 1)
-        add(nc.gpsimd, z0[:, 0 : PACK * P], 0, 0)
+        add(nc.vector, z0[:, PACK * GPSIMD_V :], 0, GPSIMD_V, HALF_V)
+        add(nc.gpsimd, z0[:, 0 : PACK * GPSIMD_V], 0, 0, GPSIMD_V)
         product(1, 0, 1)
         product(1, 1, 0)
         for b in range(2):
@@ -301,6 +302,6 @@ def tile_picked_dime_none_p_kernel(
         project(0, 0, HALF_V, z0, nc.scalar.copy)
         z1 = [sb("z1_%d" % b, [P, PACK * P], BF16)[:] for b in range(2)]
         for b in range(2):
-            add(nc.vector, z1[b], 1, b)
+            add(nc.vector, z1[b], 1, P * b, P * (b + 1))
         for b, copy in enumerate((nc.scalar.copy, nc.vector.tensor_copy)):
             project(1 + b, HALF_V + P * b, HALF_V + P * (b + 1), z1[b], copy)

from contextlib import ExitStack

import concourse.mybir as mybir

K, T, S, V, H, N, J, U = 1024, 2048, 1024, 512, 512, 128, 512, 1024
FLOPS = 2 * (K * H * S + J * H * U + H * N * V)

F32 = mybir.dt.float32
BF16 = mybir.dt.bfloat16
I32 = mybir.dt.int32
U32 = mybir.dt.uint32
U16 = mybir.dt.uint16
U8 = mybir.dt.uint8
FP8X4 = mybir.dt.float8_e4m3fn_x4
FP4X4 = mybir.dt.float4_e2m1fn_x4
SILU = mybir.ActivationFunctionType.Silu
COPY = mybir.ActivationFunctionType.Copy
MULT = mybir.AluOpType.mult
ADD = mybir.AluOpType.add

P = 128
PACK = 4
K_PASS = P * PACK
BANK = 512
QUADRANT = 32
ROWS = 4
PER_COL = 16
HALF_V = V // 2
GPSIMD_V = 5 * HALF_V // 8
SCALAR_M = (3 * P // 8, 7 * P // 8)


def tile_picked_dime_none_p_kernel(
    tc, x_words, x_scales, aT, w1, w3, w2_words, w2_scales, offs, pos1, pos2, out
):
    nc = tc.nc
    with ExitStack() as ctx:
        keep = ctx.enter_context(tc.tile_pool(name="keep", bufs=1))
        psum = ctx.enter_context(tc.psum_pool(name="psum", bufs=1))

        def sb(name, shape, dtype, tag=None):
            return keep.tile(shape, dtype, name=name, tag=tag or name, align_bytes=256)

        def bank(name, n):
            return psum.tile([P, BANK], F32, name=name, tag="bank%d" % n)

        offs_t = keep.tile([P, S // PER_COL], U16, name="offs_t")
        pos_t = [keep.tile([P, V // PER_COL], U16, name="pos%d_t" % d) for d in range(2)]
        xw = [sb("xw%d" % g, [P, T], U32) for g in range(2)]
        xs = sb("xs", [P, T], U8)
        gs_rows = sb("gs_rows", [P, S], U8)
        gs = sb("gs", [P, S], U8)
        gw = [sb("gw%d" % g, [P, S], U32) for g in range(2)]
        w1_raw = [sb("w1_raw0", [P, PACK, H], F32)[:]]
        warm = sb("warm", [P, 8], F32)
        warm_out = sb("warm_out", [P, 8], F32)

        nc.vector.memset(xs[QUADRANT : 2 * QUADRANT, :].bitcast(I32), 0)
        nc.gpsimd.memset(warm[:], 0.0)
        nc.gpsimd.memset(xs[2 * QUADRANT : P, :].bitcast(I32), 0)
        nc.vector.memset(gs[:].bitcast(I32), 0)
        nc.scalar.activation(warm_out[:], warm[:], SILU)

        def load_words(g):
            nc.sync.dma_start(out=xw[g][:].bitcast(I32), in_=x_words[g].rearrange("p n t -> p (n t)").bitcast(I32))

        def load_rows(raw, rows):
            nc.sync.dma_start(out=raw, in_=rows.rearrange("(p j) c -> p j c", j=PACK))

        nc.sync.dma_start(offs_t[:], offs)
        for g in range(2):
            nc.sync.dma_start(
                out=xs[16 * g : 16 * (g + 1), :].bitcast(I32),
                in_=x_scales[g].rearrange("(q r) c -> r q c", r=ROWS).bitcast(I32),
            )
        load_words(0)
        nc.sync.dma_start(pos_t[0][:], pos1)
        nc.sync.dma_start(pos_t[1][:], pos2)
        load_rows(w1_raw[0], w1[0:K_PASS, :])
        load_words(1)
        nc.vector.tensor_copy(gs_rows[:], xs[:].indirect(offs_t[:]))
        for q in range(P // QUADRANT):
            nc.sync.dma_start(
                out=gs[QUADRANT * q : QUADRANT * q + 2 * ROWS, :].bitcast(I32),
                in_=gs_rows[q:QUADRANT:ROWS, :].bitcast(I32),
            )

        nc.vector.tensor_copy(gw[0][:], xw[0][:].indirect(offs_t[:]))
        shared = sb("shared", [P, 56 * P], F32, "xw0")

        def blocks(first, count):
            return shared[:, first * P : (first + count) * P]

        stage_blocks = PACK * HALF_V // P
        a_raw = {
            stage: blocks(first, stage_blocks).rearrange("p (j c) -> p j c", j=PACK)
            for stage, first in (((0, 0), 14), ((0, 1), 6), ((1, 0), 22))
        }
        a_raw[1, 1] = blocks(32, stage_blocks).rearrange("p (j c) -> p j c", j=PACK)
        w1_raw.append(sb("w1_raw1", [P, PACK, H], F32, "xs")[:])
        w3_raw = blocks(40, 16).rearrange("p (j c) -> p j c", j=PACK)
        rounded = sb("rounded", [P, PACK * (HALF_V + P)], BF16)
        a_bf = rounded[:, 0 : PACK * HALF_V]
        z0 = rounded[:, PACK * P :]
        w2s = sb("w2s", [P, N], U8, "gs_rows")
        nc.gpsimd.memset(w2s[:].bitcast(I32), 0)

        def load_angles(c, d):
            load_rows(a_raw[c, d], aT[:, V * d + HALF_V * c : V * d + HALF_V * (c + 1)])

        load_rows(w1_raw[1], w1[K_PASS:K, :])
        load_rows(w3_raw, w3)
        load_angles(0, 0)
        load_angles(0, 1)
        load_angles(1, 0)
        load_angles(1, 1)
        for q in range(P // QUADRANT):
            nc.sync.dma_start(
                out=w2s[QUADRANT * q : QUADRANT * q + ROWS, :].bitcast(I32),
                in_=w2_scales[0, ROWS * q : ROWS * (q + 1), :].bitcast(I32),
            )

        def cast_weight(copy, dst, raw, u, m0=0, m1=P):
            copy(
                dst[:].rearrange("p (e m j) -> p m j e", e=2, j=PACK)[:, m0:m1],
                raw.rearrange("p j (m t) -> p m j t", t=PACK)[:, m0:m1, :, 2 * u : 2 * u + 2],
            )

        def round_on_gpsimd(dst, src):
            nc.gpsimd.tensor_scalar(dst, src, 1.0, 0.0, MULT, ADD)

        def quantize(name, src, tag=None):
            cols = src.shape[1] // PACK
            codes = keep.tile([P, cols], U32, name=name + "_codes", tag=tag or name + "_codes", align_bytes=256)
            scales = sb(name + "_scales", [P, cols], U8)
            nc.vector.quantize_mx(out=codes[:].bitcast(FP8X4), scales=scales[:], in_=src)
            return codes, scales

        h = [sb("h%d" % t, [P, S], F32) for t in range(PACK)]
        h_ps = [[bank("h_ps%d_%d" % (t, s), 2 * t + s) for s in range(2)] for t in range(PACK)]

        def h_pass(wq, g, t0):
            for e in range(wq[0].shape[1] // P):
                first = int(t0 + e == PACK - 1)
                for s in range(2):
                    cols = slice(BANK * s, BANK * (s + 1))
                    nc.tensor.matmul_mx(
                        out=h_ps[t0 + e][s][:],
                        lhsT=wq[0][:, P * e : P * (e + 1)].bitcast(FP8X4),
                        lhsT_scale=wq[1][:, P * e : P * (e + 1)],
                        rhs=gw[g][:, cols].bitcast(FP8X4),
                        rhs_scale=gs[ROWS * g : P, cols],
                        start=(g == first),
                        stop=(g != first),
                    )

        w1_bf = [[sb("w1_bf%d%d" % (g, u), [P, 2 * H], BF16) for u in range(2)] for g in range(2)]
        cast_weight(nc.scalar.copy, w1_bf[0][0], w1_raw[0], 0)
        cast_weight(nc.scalar.copy, w1_bf[0][1], w1_raw[0], 1, 0, P // 2)
        round_on_gpsimd(
            w1_bf[0][1][:].rearrange("p (e m j) -> p m e j", e=2, j=PACK)[:, P // 2 : P],
            w1_raw[0].rearrange("p j (m t) -> p m t j", t=PACK)[:, P // 2 : P, 2:PACK],
        )
        h_pass(quantize("w1q00", w1_bf[0][0][:]), 0, 0)
        w1q01 = quantize("w1q01", w1_bf[0][1][:])
        h_pass((w1q01[0][:, 0:P], w1q01[1][:, 0:P]), 0, 2)
        w2w = sb("w2w", [P, 2 * N], U8, "w1_raw0")
        nc.sync.dma_start(out=w2w[:].bitcast(I32), in_=w2_words[0].bitcast(I32))
        nc.vector.tensor_copy(gw[1][:], xw[1][:].indirect(offs_t[:]))
        for u in range(2):
            cast_weight(nc.scalar.copy, w1_bf[1][u], w1_raw[1], u, 0, SCALAR_M[u])
            cast_weight(nc.vector.tensor_copy, w1_bf[1][u], w1_raw[1], u, SCALAR_M[u], P)
        for t in range(2):
            h_pass(quantize("w1q1%d" % t, w1_bf[1][0][:, H * t : H * (t + 1)]), 1, t)
        h_pass(quantize("w1q12", w1_bf[1][1][:]), 1, 2)
        h_pass((w1q01[0][:, P:], w1q01[1][:, P:]), 0, PACK - 1)
        for t in range(PACK):
            for s in range(2):
                nc.scalar.activation(h[t][:, BANK * s : BANK * (s + 1)], h_ps[t][s][:], SILU)

        pair_blocks = 2 * HALF_V // P
        picked = {
            key: blocks(first, pair_blocks)
            for key, first in (((0, 0, 0), 18), ((0, 1, 1), 8), ((1, 0, 0), 13), ((1, 1, 1), 20))
        }
        for key in ((0, 0, 1), (0, 1, 0), (1, 0, 1), (1, 1, 0)):
            picked[key] = sb("picked%d%d%d" % key, [P, 2 * HALF_V], F32)[:]
        prod = {(0, 0): blocks(0, stage_blocks), (0, 1): blocks(24, stage_blocks)}
        for d in range(2):
            prod[1, d] = sb("prod1%d" % d, [P, PACK * HALF_V], F32)[:]
        f = {}

        def round_angles(c, d):
            round_on_gpsimd(a_bf.rearrange("p (v j) -> p v j", j=PACK), a_raw[c, d].rearrange("p j v -> p v j"))

        def filters(c, d):
            aq = quantize("aq%d%d" % (c, d), a_bf)
            for u in range(2):
                f[c, d, u] = bank("f_ps%d%d%d" % (c, d, u), PACK * c + 2 * d + u)
                codes, scales = w3q[u]
                for e in range(2):
                    cols = slice(P * e, P * (e + 1))
                    nc.tensor.matmul_mx(
                        out=f[c, d, u][:, HALF_V * e : HALF_V * (e + 1)],
                        lhsT=codes[:, cols].bitcast(FP8X4),
                        lhsT_scale=scales[:, cols],
                        rhs=aq[0][:].bitcast(FP8X4),
                        rhs_scale=aq[1][:],
                        start=True,
                        stop=True,
                    )

        def gather_operands(c, d, t, v0, v1):
            return (
                picked[c, d, t // 2][:, HALF_V * (t % 2) + v0 : HALF_V * (t % 2) + v1],
                h[t][:].indirect(pos_t[d][:, (HALF_V * c + v0) // PER_COL : (HALF_V * c + v1) // PER_COL]),
            )

        def gather_vector(c, d, t, v0=0, v1=HALF_V):
            nc.vector.tensor_copy(*gather_operands(c, d, t, v0, v1))

        def gather_scalar(c, d, t, v0=0, v1=HALF_V):
            nc.scalar.activation(*gather_operands(c, d, t, v0, v1), COPY)

        def product(c, d, u, v0=0, v1=HALF_V):
            nc.vector.tensor_tensor(
                prod[c, d].rearrange("p (u v e) -> p u v e", u=2, e=2)[:, u, v0:v1],
                picked[c, d, u].rearrange("p (e v) -> p v e", e=2)[:, v0:v1],
                f[c, d, u][:].rearrange("p (e v) -> p v e", e=2)[:, v0:v1],
                MULT,
            )

        def add(engine, z_bf, c, v0, v1):
            engine.tensor_tensor(
                z_bf.rearrange("p (v u e) -> p v u e", u=2, e=2),
                prod[c, 0].rearrange("p (u v e) -> p v u e", u=2, e=2)[:, v0:v1],
                prod[c, 1].rearrange("p (u v e) -> p v u e", u=2, e=2)[:, v0:v1],
                ADD,
            )

        def project(n, v0, v1, z_bf, copy):
            codes, scales = quantize("zq%d" % n, z_bf)
            o_ps = bank("o_ps%d" % n, n)
            nc.tensor.matmul_mx(
                out=o_ps[:, 0 : v1 - v0],
                lhsT=w2w[:].bitcast(FP4X4),
                lhsT_scale=w2s[:],
                rhs=codes[:].bitcast(FP8X4),
                rhs_scale=scales[:],
                start=True,
                stop=True,
            )
            o_sb = sb("o_sb%d" % n, [P, v1 - v0], F32)
            copy(o_sb[:], o_ps[:, 0 : v1 - v0])
            nc.sync.dma_start(out=out[:, v0:v1], in_=o_sb[:])

        w3_bf = [sb("w3_bf%d" % u, [P, 2 * H], BF16) for u in range(2)]
        for u in range(2):
            cast_weight(nc.vector.tensor_copy, w3_bf[u], w3_raw, u)
        w3q = [quantize("w3q0", w3_bf[0][:])]
        nc.vector.tensor_copy(
            a_bf.rearrange("p (v e j) -> p v j e", e=2, j=PACK),
            a_raw[0, 0].rearrange("p j (v e) -> p v j e", e=2),
        )
        w3q.append(quantize("w3q1", w3_bf[1][:]))
        filters(0, 0)

        round_angles(0, 1)
        for d, t in ((0, 2), (0, 3), (1, 0), (1, 1)):
            gather_scalar(0, d, t)
        for t in range(1, PACK):
            gather_scalar(1, 0, t)
        for t in range(2):
            gather_vector(0, 0, t)
        gather_vector(1, 0, 0, P, HALF_V)
        product(0, 0, 0)
        filters(0, 1)

        round_angles(1, 0)
        for t in range(2, PACK):
            gather_vector(0, 1, t)
        product(0, 0, 1)
        gather_vector(1, 0, 0, 0, P)
        filters(1, 0)

        round_angles(1, 1)
        for u in (1, 0):
            product(0, 1, u)
        product(1, 0, 0)
        gather_vector(1, 1, PACK - 1, 0, P)
        for t in range(PACK - 1):
            gather_scalar(1, 1, t)
        gather_scalar(1, 1, PACK - 1, P, HALF_V)
        filters(1, 1)

        add(nc.vector, z0[:, PACK * GPSIMD_V :], 0, GPSIMD_V, HALF_V)
        add(nc.gpsimd, z0[:, 0 : PACK * GPSIMD_V], 0, 0, GPSIMD_V)
        product(1, 0, 1)
        product(1, 1, 0)
        for b in range(2):
            product(1, 1, 1, P * b, P * (b + 1))
        project(0, 0, HALF_V, z0, nc.scalar.copy)
        z1 = [sb("z1_%d" % b, [P, PACK * P], BF16)[:] for b in range(2)]
        for b in range(2):
            add(nc.vector, z1[b], 1, P * b, P * (b + 1))
        for b, copy in enumerate((nc.scalar.copy, nc.vector.tensor_copy)):
            project(1 + b, HALF_V + P * b, HALF_V + P * (b + 1), z1[b], copy)
